import numpy as np
import ml_dtypes


def mxq(x, axis, fmt="e4m3"):
    dtype, down = {"e4m3": (ml_dtypes.float8_e4m3fn, 7), "e5m2": (ml_dtypes.float8_e5m2, 14)}[fmt]
    v = np.moveaxis(np.asarray(x, np.float32).astype(ml_dtypes.bfloat16).astype(np.float64), axis, -1)
    blocks = v.reshape(v.shape[:-1] + (-1, 32))
    amax = np.abs(blocks).max(-1, keepdims=True)
    byte = np.maximum(np.where(amax > 0, np.frexp(amax)[1] - 1 + 127, 0) - down, 1)
    scale = np.exp2(byte - 127.0)
    codes = (blocks / scale).astype(np.float32).astype(dtype).astype(np.float64)
    return np.moveaxis((codes * scale).reshape(v.shape), -1, axis)


WIDE = False


def mx_kscale(k):
    if not WIDE:
        return np.ones(k)
    levels = np.array([10, -10, 5, -5, 0])
    if k % 512:
        return np.exp2(np.random.permutation(np.resize(levels, k // 32))).repeat(32)
    a = np.empty((k // 512, 16))
    for p in range(k // 512):
        a[p, :8] = np.random.permutation(np.resize(levels, 8))
        for g in range(8):
            far = levels[np.abs(levels - a[p, g]) >= 10]
            a[p, g + 8] = far[np.random.randint(len(far))]
    return np.exp2(a.ravel()).repeat(32)


def f64(x):
    return np.asarray(x).astype(np.float64)


def striped(idx):
    return np.tile(idx.reshape(-1, 16).T, (8, 1)).astype(np.uint16)


def unstriped(offs):
    return offs[:16].T.reshape(-1).astype(np.int64)


E2M1 = np.array([0.0, 0.5, 1.0, 1.5, 2.0, 3.0, 4.0, 6.0, -0.0, -0.5, -1.0, -1.5, -2.0, -3.0, -4.0, -6.0])


def pack_weight(w, fmt):
    k, n = w.shape
    w = f64(np.asarray(w, np.float32).astype(ml_dtypes.bfloat16)).reshape(k // 32, 32, n)
    amax = np.abs(w).max(1)
    if fmt == "e4m3":
        byte = np.frexp(amax)[1] - 1 + 127 - 7
    else:
        mant, ex = np.frexp(amax / 6.0)
        byte = np.where(mant > 0.5, ex, ex - 1) + 127
    byte = np.clip(np.where(amax > 0, byte, 1), 1, 254)
    scaled = (w * np.exp2(127.0 - byte)[:, None, :]).reshape(k, n).astype(np.float32)
    by_word = np.ascontiguousarray(scaled.reshape(k // 512, 128, 4, n).transpose(0, 1, 3, 2))
    if fmt == "e4m3":
        words = by_word.astype(ml_dtypes.float8_e4m3fn).view(np.uint8)
    else:
        c = by_word.astype(ml_dtypes.float4_e2m1fn).view(np.uint8) & 0xF
        words = (c[..., 0::2] | (c[..., 1::2] << 4)).reshape(k // 512, 128, 2 * n)
    return np.ascontiguousarray(words), np.ascontiguousarray(byte.astype(np.uint8).reshape(k // 512, 16, n))


def unpack_weight(words, scales, fmt):
    g, _, n = scales.shape
    words = np.ascontiguousarray(words).reshape(g, 128, n, -1)
    if fmt == "e4m3":
        vals = words.view(ml_dtypes.float8_e4m3fn).astype(np.float64)
    else:
        nib = np.empty((g, 128, n, 4), np.uint8)
        nib[..., 0::2] = words & 0xF
        nib[..., 1::2] = words >> 4
        vals = E2M1[nib]
    vals = vals * np.repeat(np.exp2(scales.astype(np.float64) - 127.0), 8, axis=1)[..., None]
    return vals.transpose(0, 1, 3, 2).reshape(g * 512, n)


def sigmoid(v):
    return 1.0 / (1.0 + np.exp(-np.maximum(v, -700.0)))


K, T, E, C, H, N = 1024, 768, 6, 256, 512, 128


def by_expert(wq, xq):
    return np.concatenate([wq[e].T @ xq[:, e * C:(e + 1) * C] for e in range(E)], axis=1)


def setup_inputs():
    n = np.random.standard_normal
    s = mx_kscale(K)[:, None]
    u = mx_kscale(H)
    first = np.random.permutation(np.repeat(np.arange(E), T // E))
    second = (first + 1 + np.random.permutation(np.repeat(np.arange(E - 1), -(-T // (E - 1)))[:T])) % E
    while np.bincount(second, minlength=E).max() != T // E:
        load = np.bincount(second, minlength=E); hi, lo = int(load.argmax()), int(load.argmin())
        t = np.flatnonzero((second == hi) & (first != lo))[0]; second[t] = lo
    slot_token = np.empty(E * C, np.int64); pos = np.empty((2, T), np.int64); fill = np.zeros(E, np.int64)
    place = np.stack([np.random.permutation(C) for _ in range(E)])
    for r, deal in enumerate((first, second)):
        for t in np.random.permutation(T):
            e = deal[t]; j = e * C + place[e, fill[e]]; fill[e] += 1; slot_token[j] = t; pos[r, t] = j
    g = np.random.uniform(0.2, 0.8, T)
    w1 = [pack_weight(m, "e2m1") for m in n((E + 1, K, H)) / np.sqrt(K) / s[None]]
    w3 = [pack_weight(m, "e2m1") for m in n((E + 1, K, H)) / np.sqrt(K) / s[None] * u[None, None, :]]
    w2 = [pack_weight(m, "e2m1") for m in n((E + 1, H, N)) / np.sqrt(H) / u[None, :, None]]
    x = pack_weight(n((K, T)) * s, "e4m3")
    return {
        "x_words": x[0],
        "x_scales": x[1],
        "w1_words": np.stack([m[0] for m in w1]),
        "w1_scales": np.stack([m[1] for m in w1]),
        "w3_words": np.stack([m[0] for m in w3]),
        "w3_scales": np.stack([m[1] for m in w3]),
        "w2_words": np.stack([m[0] for m in w2]),
        "w2_scales": np.stack([m[1] for m in w2]),
        "gate": np.stack([np.tile(g, (N, 1)), np.tile(1.0 - g, (N, 1))]).astype(np.float32),
        "offs": striped(slot_token),
        "pos1": striped(pos[0]),
        "pos2": striped(pos[1]),
    }


def reference(x_words, x_scales, w1_words, w1_scales, w3_words, w3_scales, w2_words, w2_scales, gate, offs, pos1, pos2):
    idx = unstriped(offs)
    w1 = np.stack([unpack_weight(w1_words[e], w1_scales[e], "e2m1") for e in range(E + 1)])
    w3 = np.stack([unpack_weight(w3_words[e], w3_scales[e], "e2m1") for e in range(E + 1)])
    w2 = np.stack([unpack_weight(w2_words[e], w2_scales[e], "e2m1") for e in range(E + 1)])
    w1q, w3q, w2q = w1, w3, w2
    xs = unpack_weight(x_words, x_scales, "e4m3")
    hs = sigmoid(w1q[E].T @ xs) * (w3q[E].T @ xs)
    ys = w2q[E].T @ mxq(hs, 0, "e4m3")
    xq = unpack_weight(x_words, x_scales, "e4m3")[:, idx]
    h = sigmoid(by_expert(w1q, xq))
    h = h * by_expert(w3q, xq)
    y = by_expert(w2q, mxq(h, 0, "e4m3"))
    return ys + f64(gate[0]) * y[:, unstriped(pos1)] + f64(gate[1]) * y[:, unstriped(pos2)]

@@ -1,0 +1,257 @@
+from contextlib import ExitStack
+
+import concourse.mybir as mybir
+from concourse.masks import make_identity
+
+K, T, E, C, H, N = 1024, 768, 6, 256, 512, 128
+S = E * C
+FLOPS = 2 * (S + T) * (2 * K * H + H * N)
+
+F32 = mybir.dt.float32
+BF16 = mybir.dt.bfloat16
+I32 = mybir.dt.int32
+U32 = mybir.dt.uint32
+U16 = mybir.dt.uint16
+U8 = mybir.dt.uint8
+FP8X4 = mybir.dt.float8_e4m3fn_x4
+FP4X4 = mybir.dt.float4_e2m1fn_x4
+MULT = mybir.AluOpType.mult
+ADD = mybir.AluOpType.add
+SIGMOID = mybir.ActivationFunctionType.Sigmoid
+
+P = 128
+PASSES = K // 512
+SHARED = E
+FIRST = E - 1
+PACKED_WINDOW = 1024
+
+
+def tile_moe_shr_glu_sigmoid_kernel(
+    tc, x_words, x_scales, w1_words, w1_scales, w3_words, w3_scales, w2_words, w2_scales, gate, offs, pos1, pos2, out
+):
+    nc = tc.nc
+    with ExitStack() as ctx:
+        keep = ctx.enter_context(tc.tile_pool(name="keep", bufs=1))
+        ring = ctx.enter_context(tc.tile_pool(name="ring", bufs=3))
+        psum = ctx.enter_context(tc.psum_pool(name="psum", bufs=1))
+
+        def held(shape, dtype, name):
+            return keep.tile(shape, dtype, name=name, align_bytes=64)
+
+        def zero(engine, tile):
+            engine.memset(tile[:].bitcast(I32), 0)
+
+        def load_scales(queue, plane, scales):
+            for q in range(4):
+                queue.dma_start(
+                    plane[32 * q : 32 * q + 4, :, :].bitcast(I32),
+                    scales[:, :, 4 * q : 4 * q + 4, :].rearrange("e s q n -> q (e s) n").bitcast(I32),
+                )
+
+        def load_words(tile, words):
+            nc.sync.dma_start(tile[:].bitcast(I32), words.rearrange("s p b -> p s b").bitcast(I32))
+
+        offs_sb = held([P, S // 16], U16, "offs_sb")
+        pos1_sb = held([P, T // 16], U16, "pos1_sb")
+        pos2_sb = held([P, T // 16], U16, "pos2_sb")
+        xw = [held([P, T], I32, f"xw{o}") for o in range(PASSES)]
+        xs = held([P, PASSES, T], U8, "xs")
+        xs_packed = held([P, PACKED_WINDOW], U8, "xs_packed")
+        w1s_early = held([P, 2 * PASSES, H], U8, "w1s_early")
+        w3s_early = held([P, 2 * PASSES, H], U8, "w3s_early")
+        w1s_late = held([P, FIRST * PASSES, H], U8, "w1s_late")
+        w3s_late = held([P, FIRST * PASSES, H], U8, "w3s_late")
+        w2s = held([P, E + 1, N], U8, "w2s")
+        w1w = [held([P, PASSES, 2 * H], U8, f"w1w{e}") for e in range(E + 1)]
+        w3w = [held([P, PASSES, 2 * H], U8, f"w3w{e}") for e in range(E + 1)]
+        w2w = held([P, E + 1, 2 * N], U8, "w2w")
+        gate_sb = held([P, 2, T], F32, "gate_sb")
+        ident = held([P, P], F32, "ident")
+        gw = [held([P, S], U32, f"gw{o}") for o in range(PASSES)]
+        gs_first = held([P, PASSES, C], U8, "gs_first")
+        gs_packed = held([P, FIRST * C], U8, "gs_packed")
+        gs_moved = held([P, FIRST * C], U8, "gs_moved")
+        y_all = held([P, S], F32, "y_all")
+        warm = held([P, 2], F32, "warm")
+
+        zero(nc.vector, w1s_early)
+        zero(nc.vector, xs)
+        zero(nc.vector, w3s_early)
+        nc.vector.memset(warm[:, 0:1], 0.0)
+        nc.scalar.activation(warm[:, 1:2], warm[:, 0:1], SIGMOID)
+        zero(nc.vector, w1s_late)
+        zero(nc.vector, w3s_late)
+        zero(nc.vector, gs_moved)
+
+        zero(nc.gpsimd, xs_packed)
+        zero(nc.gpsimd, w2s)
+        make_identity(nc, ident[:])
+
+        nc.sync.dma_start(offs_sb[:], offs)
+        load_scales(nc.sync, w1s_early, w1_scales[FIRST : E + 1])
+        load_words(w1w[SHARED], w1_words[SHARED])
+        for o in range(PASSES):
+            nc.sync.dma_start(xw[o][:], x_words[o].rearrange("p t r -> p (t r)").bitcast(I32))
+        for q in range(4):
+            nc.sync.dma_start(
+                xs[32 * q : 32 * q + 4, :, :].bitcast(I32),
+                x_scales[:, 4 * q : 4 * q + 4, :].rearrange("o q t -> q o t").bitcast(I32),
+            )
+        load_words(w3w[SHARED], w3_words[SHARED])
+        load_scales(nc.sync, w3s_early, w3_scales[FIRST : E + 1])
+        load_words(w1w[FIRST], w1_words[FIRST])
+        load_words(w3w[FIRST], w3_words[FIRST])
+        for q in range(4):
+            nc.sync.dma_start(
+                xs_packed[32 * q : 32 * q + 8, 0:T].bitcast(I32), x_scales[:, 4 * q : 4 * q + 4, :].bitcast(I32)
+            )
+        load_scales(nc.sync, w1s_late, w1_scales[0:FIRST])
+        load_scales(nc.sync, w3s_late, w3_scales[0:FIRST])
+        for e in range(2):
+            load_words(w1w[e], w1_words[e])
+            load_words(w3w[e], w3_words[e])
+
+        def slot_offsets(lo, hi):
+            return offs_sb[:, lo // 16 : hi // 16]
+
+        def gather_words(lo, hi):
+            for o in range(PASSES):
+                nc.vector.tensor_copy(gw[o][:, lo:hi], xw[o][:].bitcast(U32).indirect(slot_offsets(lo, hi)))
+
+        def gather_packed_scales(lo, hi):
+            nc.vector.tensor_copy(gs_packed[:, lo:hi], xs_packed[:].indirect(slot_offsets(lo, hi)))
+            for q in range(4):
+                nc.sync.dma_start(
+                    gs_moved[32 * q : 32 * q + 4, lo:hi].bitcast(I32),
+                    gs_packed[32 * q + 4 : 32 * q + 8, lo:hi].bitcast(I32),
+                )
+
+        def token_operands(e, lo, o):
+            cols = slice(lo, lo + P)
+            if e == SHARED:
+                return xw[o][:, cols], xs[:, o, cols]
+            if e == FIRST:
+                return gw[o][:, cols], gs_first[:, o, lo - FIRST * C : lo - FIRST * C + P]
+            return gw[o][:, cols], (gs_packed, gs_moved)[o][:, cols]
+
+        def first_layer(e, lo):
+            row = (e - FIRST) * PASSES if e >= FIRST else e * PASSES
+            sums = []
+            for name, depth, words, scales in (
+                ("a", 2, w1w[e], w1s_early if e >= FIRST else w1s_late),
+                ("b", 3, w3w[e], w3s_early if e >= FIRST else w3s_late),
+            ):
+                acc = psum.tile([P, H], F32, name=name, bufs=depth)
+                for o in range(PASSES):
+                    codes, code_scales = token_operands(e, lo, o)
+                    nc.tensor.matmul_mx(
+                        out=acc[:],
+                        lhsT=codes.bitcast(FP8X4),
+                        lhsT_scale=code_scales,
+                        rhs=words[:, o, :].bitcast(FP4X4),
+                        rhs_scale=scales[:, row + o, :],
+                        start=(o == 0),
+                        stop=(o == PASSES - 1),
+                    )
+                sums.append(acc[:].rearrange("t (p u f) -> t u p f", u=2, f=2))
+            sig = ring.tile([P, 2, P, 2], F32, name="sig", align_bytes=64)
+            nc.scalar.activation(sig[:], sums[0], SIGMOID)
+            h = ring.tile([P, 2, P, 2], BF16, name="h", bufs=4, align_bytes=64)
+            nc.vector.tensor_tensor(h[:], sums[1], sig[:], MULT)
+            return h
+
+        def turn(hs):
+            turned = psum.tile([P, 2, 2, P], F32, name="turned", bufs=2)
+            for j, h in enumerate(hs):
+                pairs = h[:].rearrange("t u p f -> t (u p f)").bitcast(F32)
+                for u in range(2):
+                    nc.tensor.transpose(turned[:, j, u, :], pairs[:, u * P : (u + 1) * P], ident[:])
+            hT = ring.tile([P, 2, P, 4], BF16, name="hT", align_bytes=64)
+            nc.scalar.copy(hT[:].bitcast(F32), turned[:].rearrange("p j u t -> p j t u"))
+            return hT
+
+        def quantise(hT, k):
+            codes = held([P, C], U32, f"h_codes{k}")
+            scales = held([P, C], U8, f"h_scales{k}")
+            nc.vector.quantize_mx(
+                out=codes[:].bitcast(FP8X4), scales=scales[:], in_=hT[:].rearrange("p j t r -> p (j t r)")
+            )
+            return codes, scales
+
+        def second_layer(e, quantised):
+            codes, scales = quantised
+            y = psum.tile([P, C], F32, name="y")
+            nc.tensor.matmul_mx(
+                out=y[:],
+                lhsT=w2w[:, e, :].bitcast(FP4X4),
+                lhsT_scale=w2s[:, e, :],
+                rhs=codes[:].bitcast(FP8X4),
+                rhs_scale=scales[:],
+                start=True,
+                stop=True,
+            )
+            return y
+
+        units = [(SHARED, 0), (FIRST, FIRST * C)] + [(e, e * C) for e in range(FIRST)] + [(SHARED, C), (SHARED, 2 * C)]
+        ys_front = held([P, 2 * C], F32, "ys_front")
+        routed = held([P, T], F32, "routed")
+        result = held([P, T], F32, "result")
+
+        def finish(k, quantised):
+            e, lo = units[k]
+            y = second_layer(e, quantised)
+            if e != SHARED:
+                nc.scalar.copy(y_all[:, lo : lo + C], y[:])
+            elif lo < 2 * C:
+                nc.scalar.copy(ys_front[:, lo : lo + C], y[:])
+            return y
+
+        gather_words(FIRST * C, S)
+        for o in range(PASSES):
+            nc.vector.tensor_copy(gs_first[:, o, :], xs[:, o, :].indirect(slot_offsets(FIRST * C, S)))
+
+        hs, quantised = {}, {}
+        done = 0
+        for k, (e, lo) in enumerate(units):
+            h0 = first_layer(e, lo)
+            if k == 0:
+                gather_packed_scales(0, 2 * C)
+                load_scales(nc.sync, w2s, w2_scales)
+                nc.sync.dma_start(w2w[:].bitcast(I32), w2_words.rearrange("e s p b -> p (e s) b").bitcast(I32))
+                for late in range(2, FIRST):
+                    load_words(w1w[late], w1_words[late])
+                    load_words(w3w[late], w3_words[late])
+            if k >= 1:
+                hT = turn(hs[k - 1])
+            h1 = first_layer(e, lo + P)
+            hs[k] = (h0, h1)
+            if k < FIRST:
+                gather_words(k * C, (k + 1) * C)
+            if k == 1:
+                gather_packed_scales(2 * C, FIRST * C)
+                nc.sync.dma_start(pos1_sb[:], pos1)
+                nc.sync.dma_start(pos2_sb[:], pos2)
+                nc.sync.dma_start(gate_sb[:], gate.rearrange("g n t -> n g t"))
+            if k >= 1:
+                quantised[k - 1] = quantise(hT, k - 1)
+            while k >= 3 and done < k - 1:
+                finish(done, quantised[done])
+                done += 1
+            if k == len(units) - 2:
+                finish(done, quantised[done])
+                done += 1
+
+        last = len(units) - 1
+        first_choice = held([P, T], F32, "first_choice")
+        second_choice = held([P, T], F32, "second_choice")
+        nc.vector.tensor_tensor(first_choice[:], y_all[:].indirect(pos1_sb[:]), gate_sb[:, 0, :], MULT)
+        hT = turn(hs[last])
+        finish(last - 1, quantised[last - 1])
+        nc.vector.tensor_tensor(second_choice[:], y_all[:].indirect(pos2_sb[:]), gate_sb[:, 1, :], MULT)
+        quantised[last] = quantise(hT, last)
+        nc.vector.tensor_tensor(routed[:], first_choice[:], second_choice[:], ADD)
+        ys_last = finish(last, quantised[last])
+        nc.vector.tensor_tensor(result[:, 0 : 2 * C], routed[:, 0 : 2 * C], ys_front[:], ADD)
+        nc.sync.dma_start(out[:, 0 : 2 * C], result[:, 0 : 2 * C])
+        nc.vector.tensor_tensor(result[:, 2 * C : T], ys_last[:], routed[:, 2 * C : T], ADD)
+        nc.sync.dma_start(out[:, 2 * C : T], result[:, 2 * C : T])

@@ -22,8 +22,11 @@ SIGMOID = mybir.ActivationFunctionType.Sigmoid
 P = 128
 PASSES = K // 512
 SHARED = E
-FIRST = E - 1
-PACKED_WINDOW = 1024
+SCALE_WINDOW = 1024
+SCALE_GROUPS = ((5, 7), (3, 5), (0, 3))
+FRONT = (2,)
+DIRECT = 4
+BACK = (2, 1, 1)
 
 
 def tile_moe_shr_glu_sigmoid_kernel(
@@ -32,11 +35,16 @@ def tile_moe_shr_glu_sigmoid_kernel(
     nc = tc.nc
     with ExitStack() as ctx:
         keep = ctx.enter_context(tc.tile_pool(name="keep", bufs=1))
-        ring = ctx.enter_context(tc.tile_pool(name="ring", bufs=3))
         psum = ctx.enter_context(tc.psum_pool(name="psum", bufs=1))
 
         def held(shape, dtype, name):
             return keep.tile(shape, dtype, name=name, align_bytes=64)
+
+        def ring(count, shape, dtype, name):
+            return [held(shape, dtype, f"{name}{r}") for r in range(count)]
+
+        def banks(count, shape, name):
+            return [psum.tile(shape, F32, name=f"{name}{r}") for r in range(count)]
 
         def zero(engine, tile):
             engine.memset(tile[:].bitcast(I32), 0)
@@ -48,102 +56,99 @@ def tile_moe_shr_glu_sigmoid_kernel(
                     scales[:, :, 4 * q : 4 * q + 4, :].rearrange("e s q n -> q (e s) n").bitcast(I32),
                 )
 
-        def load_words(tile, words):
-            nc.sync.dma_start(tile[:].bitcast(I32), words.rearrange("s p b -> p s b").bitcast(I32))
+        def load_words(queue, tile, words):
+            queue.dma_start(tile[:].bitcast(I32), words.rearrange("s p b -> p s b").bitcast(I32))
 
         offs_sb = held([P, S // 16], U16, "offs_sb")
         pos1_sb = held([P, T // 16], U16, "pos1_sb")
         pos2_sb = held([P, T // 16], U16, "pos2_sb")
-        xw = [held([P, T], I32, f"xw{o}") for o in range(PASSES)]
-        xs = held([P, PASSES, T], U8, "xs")
-        xs_packed = held([P, PACKED_WINDOW], U8, "xs_packed")
-        w1s_early = held([P, 2 * PASSES, H], U8, "w1s_early")
-        w3s_early = held([P, 2 * PASSES, H], U8, "w3s_early")
-        w1s_late = held([P, FIRST * PASSES, H], U8, "w1s_late")
-        w3s_late = held([P, FIRST * PASSES, H], U8, "w3s_late")
+        xw = ring(PASSES, [P, T], I32, "xw")
+        xs_both = held([P, SCALE_WINDOW], U8, "xs_both")
+        xs_second = held([P, T], U8, "xs_second")
+        w1s = [held([P, (hi - lo) * PASSES, H], U8, f"w1s{lo}") for lo, hi in SCALE_GROUPS]
+        w3s = [held([P, (hi - lo) * PASSES, H], U8, f"w3s{lo}") for lo, hi in SCALE_GROUPS]
         w2s = held([P, E + 1, N], U8, "w2s")
-        w1w = [held([P, PASSES, 2 * H], U8, f"w1w{e}") for e in range(E + 1)]
-        w3w = [held([P, PASSES, 2 * H], U8, f"w3w{e}") for e in range(E + 1)]
+        w1w = ring(E + 1, [P, PASSES, 2 * H], U8, "w1w")
+        w3w = ring(E + 1, [P, PASSES, 2 * H], U8, "w3w")
         w2w = held([P, E + 1, 2 * N], U8, "w2w")
         gate_sb = held([P, 2, T], F32, "gate_sb")
         ident = held([P, P], F32, "ident")
-        gw = [held([P, S], U32, f"gw{o}") for o in range(PASSES)]
-        gs_first = held([P, PASSES, C], U8, "gs_first")
-        gs_packed = held([P, FIRST * C], U8, "gs_packed")
-        gs_moved = held([P, FIRST * C], U8, "gs_moved")
+        gw = ring(2, [P, PASSES, C], U32, "gw")
+        gs_both = held([P, S], U8, "gs_both")
+        gs_direct = held([P, S - DIRECT * C], U8, "gs_direct")
+        gs_second = held([P, DIRECT * C], U8, "gs_second")
         y_all = held([P, S], F32, "y_all")
         warm = held([P, 2], F32, "warm")
+        sig = ring(3, [P, 2, P, 2], F32, "sig")
+        h = ring(4, [P, 2, P, 2], BF16, "h")
+        hT = ring(2, [P, 2, P, 4], BF16, "hT")
+        a_banks = banks(2, [P, H], "a")
+        b_banks = banks(3, [P, H], "b")
+        turned = banks(2, [P, 2, P], "turned")
+        y_bank = psum.tile([P, C], F32, name="y_bank")
 
-        zero(nc.vector, w1s_early)
-        zero(nc.vector, xs)
-        zero(nc.vector, w3s_early)
-        nc.vector.memset(warm[:, 0:1], 0.0)
-        nc.scalar.activation(warm[:, 1:2], warm[:, 0:1], SIGMOID)
-        zero(nc.vector, w1s_late)
-        zero(nc.vector, w3s_late)
-        zero(nc.vector, gs_moved)
+        def group(scales, g):
+            return scales[SCALE_GROUPS[g][0] : SCALE_GROUPS[g][1]]
 
-        zero(nc.gpsimd, xs_packed)
-        zero(nc.gpsimd, w2s)
-        make_identity(nc, ident[:])
+        def load_tokens(queue, o):
+            queue.dma_start(xw[o][:], x_words[o].rearrange("p t r -> p (t r)").bitcast(I32))
 
-        nc.sync.dma_start(offs_sb[:], offs)
-        load_scales(nc.sync, w1s_early, w1_scales[FIRST : E + 1])
-        load_words(w1w[SHARED], w1_words[SHARED])
-        for o in range(PASSES):
-            nc.sync.dma_start(xw[o][:], x_words[o].rearrange("p t r -> p (t r)").bitcast(I32))
-        for q in range(4):
-            nc.sync.dma_start(
-                xs[32 * q : 32 * q + 4, :, :].bitcast(I32),
-                x_scales[:, 4 * q : 4 * q + 4, :].rearrange("o q t -> q o t").bitcast(I32),
-            )
-        load_words(w3w[SHARED], w3_words[SHARED])
-        load_scales(nc.sync, w3s_early, w3_scales[FIRST : E + 1])
-        load_words(w1w[FIRST], w1_words[FIRST])
-        load_words(w3w[FIRST], w3_words[FIRST])
-        for q in range(4):
-            nc.sync.dma_start(
-                xs_packed[32 * q : 32 * q + 8, 0:T].bitcast(I32), x_scales[:, 4 * q : 4 * q + 4, :].bitcast(I32)
-            )
-        load_scales(nc.sync, w1s_late, w1_scales[0:FIRST])
-        load_scales(nc.sync, w3s_late, w3_scales[0:FIRST])
-        for e in range(2):
-            load_words(w1w[e], w1_words[e])
-            load_words(w3w[e], w3_words[e])
+        def load_both_token_scales(queue):
+            for q in range(4):
+                queue.dma_start(
+                    xs_both[32 * q : 32 * q + 8, 0:T].bitcast(I32), x_scales[:, 4 * q : 4 * q + 4, :].bitcast(I32)
+                )
+
+        def load_second_token_scales(queue):
+            for q in range(4):
+                queue.dma_start(
+                    xs_second[32 * q : 32 * q + 4, :].bitcast(I32), x_scales[1, 4 * q : 4 * q + 4, :].bitcast(I32)
+                )
+
+        def load_expert_words(e):
+            load_words(nc.sync, w1w[e], w1_words[e])
+            load_words(nc.sync, w3w[e], w3_words[e])
 
         def slot_offsets(lo, hi):
             return offs_sb[:, lo // 16 : hi // 16]
 
-        def gather_words(lo, hi):
+        def gather_words(e):
             for o in range(PASSES):
-                nc.vector.tensor_copy(gw[o][:, lo:hi], xw[o][:].bitcast(U32).indirect(slot_offsets(lo, hi)))
+                nc.vector.tensor_copy(
+                    gw[e % 2][:, o, :], xw[o][:].bitcast(U32).indirect(slot_offsets(e * C, (e + 1) * C))
+                )
 
-        def gather_packed_scales(lo, hi):
-            nc.vector.tensor_copy(gs_packed[:, lo:hi], xs_packed[:].indirect(slot_offsets(lo, hi)))
+        def gather_direct_scales(lo, hi):
+            nc.vector.tensor_copy(
+                gs_direct[:, lo - DIRECT * C : hi - DIRECT * C], xs_second[:].indirect(slot_offsets(lo, hi))
+            )
+
+        def gather_scales(lo, hi):
+            nc.vector.tensor_copy(gs_both[:, lo:hi], xs_both[:].indirect(slot_offsets(lo, hi)))
+
+        def move_scales(queue, lo, hi):
             for q in range(4):
-                nc.sync.dma_start(
-                    gs_moved[32 * q : 32 * q + 4, lo:hi].bitcast(I32),
-                    gs_packed[32 * q + 4 : 32 * q + 8, lo:hi].bitcast(I32),
+                queue.dma_start(
+                    gs_second[32 * q : 32 * q + 4, lo:hi].bitcast(I32),
+                    gs_both[32 * q + 4 : 32 * q + 8, lo:hi].bitcast(I32),
                 )
 
         def token_operands(e, lo, o):
             cols = slice(lo, lo + P)
             if e == SHARED:
-                return xw[o][:, cols], xs[:, o, cols]
-            if e == FIRST:
-                return gw[o][:, cols], gs_first[:, o, lo - FIRST * C : lo - FIRST * C + P]
-            return gw[o][:, cols], (gs_packed, gs_moved)[o][:, cols]
+                return xw[o][:, cols], (xs_both, xs_second)[o][:, cols]
+            codes = gw[e % 2][:, o, lo - e * C : lo - e * C + P]
+            if o == 1 and e >= DIRECT:
+                return codes, gs_direct[:, lo - DIRECT * C : lo - DIRECT * C + P]
+            return codes, (gs_both, gs_second)[o][:, cols]
 
-        def first_layer(e, lo):
-            row = (e - FIRST) * PASSES if e >= FIRST else e * PASSES
-            sums = []
-            for name, depth, words, scales in (
-                ("a", 2, w1w[e], w1s_early if e >= FIRST else w1s_late),
-                ("b", 3, w3w[e], w3s_early if e >= FIRST else w3s_late),
-            ):
-                acc = psum.tile([P, H], F32, name=name, bufs=depth)
-                for o in range(PASSES):
-                    codes, code_scales = token_operands(e, lo, o)
+        def first_layer(j, e, lo):
+            g = [lo_e <= e < hi_e for lo_e, hi_e in SCALE_GROUPS].index(True)
+            row = (e - SCALE_GROUPS[g][0]) * PASSES
+            products = ((a_banks[j % 2], w1w[e], w1s[g]), (b_banks[j % 3], w3w[e], w3s[g]))
+            for o in range(PASSES):
+                codes, code_scales = token_operands(e, lo, o)
+                for acc, words, scales in products:
                     nc.tensor.matmul_mx(
                         out=acc[:],
                         lhsT=codes.bitcast(FP8X4),
@@ -153,105 +158,133 @@ def tile_moe_shr_glu_sigmoid_kernel(
                         start=(o == 0),
                         stop=(o == PASSES - 1),
                     )
-                sums.append(acc[:].rearrange("t (p u f) -> t u p f", u=2, f=2))
-            sig = ring.tile([P, 2, P, 2], F32, name="sig", align_bytes=64)
-            nc.scalar.activation(sig[:], sums[0], SIGMOID)
-            h = ring.tile([P, 2, P, 2], BF16, name="h", bufs=4, align_bytes=64)
-            nc.vector.tensor_tensor(h[:], sums[1], sig[:], MULT)
-            return h
+            sums = [acc[:].rearrange("t (p u f) -> t u p f", u=2, f=2) for acc, words, scales in products]
+            nc.scalar.activation(sig[j % 3][:], sums[0], SIGMOID)
+            nc.vector.tensor_tensor(h[j % len(h)][:], sums[1], sig[j % 3][:], MULT)
 
-        def turn(hs):
-            turned = psum.tile([P, 2, 2, P], F32, name="turned", bufs=2)
-            for j, h in enumerate(hs):
-                pairs = h[:].rearrange("t u p f -> t (u p f)").bitcast(F32)
-                for u in range(2):
-                    nc.tensor.transpose(turned[:, j, u, :], pairs[:, u * P : (u + 1) * P], ident[:])
-            hT = ring.tile([P, 2, P, 4], BF16, name="hT", align_bytes=64)
-            nc.scalar.copy(hT[:].bitcast(F32), turned[:].rearrange("p j u t -> p j t u"))
-            return hT
-
-        def quantise(hT, k):
-            codes = held([P, C], U32, f"h_codes{k}")
-            scales = held([P, C], U8, f"h_scales{k}")
-            nc.vector.quantize_mx(
-                out=codes[:].bitcast(FP8X4), scales=scales[:], in_=hT[:].rearrange("p j t r -> p (j t r)")
-            )
-            return codes, scales
-
-        def second_layer(e, quantised):
-            codes, scales = quantised
-            y = psum.tile([P, C], F32, name="y")
-            nc.tensor.matmul_mx(
-                out=y[:],
-                lhsT=w2w[:, e, :].bitcast(FP4X4),
-                lhsT_scale=w2s[:, e, :],
-                rhs=codes[:].bitcast(FP8X4),
-                rhs_scale=scales[:],
-                start=True,
-                stop=True,
-            )
-            return y
-
-        units = [(SHARED, 0), (FIRST, FIRST * C)] + [(e, e * C) for e in range(FIRST)] + [(SHARED, C), (SHARED, 2 * C)]
-        ys_front = held([P, 2 * C], F32, "ys_front")
+        units = []
+        token = 0
+        for tiles in FRONT:
+            units.append((SHARED, token, tiles))
+            token += tiles * P
+        units.extend((e, e * C, 2) for e in reversed(range(E)))
+        for tiles in BACK:
+            units.append((SHARED, token, tiles))
+            token += tiles * P
+        first_tile = [sum(u[2] for u in units[:k]) for k in range(len(units))]
+        h_codes = ring(len(units), [P, C], U32, "h_codes")
+        h_scales = ring(len(units), [P, C], U8, "h_scales")
+        last = len(units) - 1
+        early = units[last][1]
+        ys_early = held([P, early], F32, "ys_early")
         routed = held([P, T], F32, "routed")
         result = held([P, T], F32, "result")
 
-        def finish(k, quantised):
-            e, lo = units[k]
-            y = second_layer(e, quantised)
+        def turn(k):
+            tiles = units[k][2]
+            for u in range(2):
+                for half in range(tiles):
+                    j = first_tile[k] + half
+                    pairs = h[j % len(h)][:].rearrange("t u p f -> t (u p f)").bitcast(F32)
+                    nc.tensor.transpose(turned[j % 2][:, u, :], pairs[:, u * P : (u + 1) * P], ident[:])
+            for half in range(tiles):
+                j = first_tile[k] + half
+                nc.scalar.copy(hT[k % 2][:, half].bitcast(F32), turned[j % 2][:].rearrange("p u t -> p t u"))
+
+        def quantise(k):
+            tiles = units[k][2]
+            nc.vector.quantize_mx(
+                out=h_codes[k][:, 0 : tiles * P].bitcast(FP8X4),
+                scales=h_scales[k][:, 0 : tiles * P],
+                in_=hT[k % 2][:, 0:tiles].rearrange("p j t r -> p (j t r)"),
+            )
+
+        def second_layer(k):
+            e, lo, tiles = units[k]
+            width = tiles * P
+            nc.tensor.matmul_mx(
+                out=y_bank[:, 0:width],
+                lhsT=w2w[:, e, :].bitcast(FP4X4),
+                lhsT_scale=w2s[:, e, :],
+                rhs=h_codes[k][:, 0:width].bitcast(FP8X4),
+                rhs_scale=h_scales[k][:, 0:width],
+                start=True,
+                stop=True,
+            )
             if e != SHARED:
-                nc.scalar.copy(y_all[:, lo : lo + C], y[:])
-            elif lo < 2 * C:
-                nc.scalar.copy(ys_front[:, lo : lo + C], y[:])
-            return y
+                nc.scalar.copy(y_all[:, lo : lo + width], y_bank[:, 0:width])
+            elif k < last:
+                nc.scalar.copy(ys_early[:, lo : lo + width], y_bank[:, 0:width])
 
-        gather_words(FIRST * C, S)
-        for o in range(PASSES):
-            nc.vector.tensor_copy(gs_first[:, o, :], xs[:, o, :].indirect(slot_offsets(FIRST * C, S)))
+        zero(nc.vector, xs_both)
+        zero(nc.gpsimd, xs_second)
+        nc.vector.memset(warm[:, 0:1], 0.0)
+        zero(nc.vector, w1s[0])
+        zero(nc.vector, w3s[0])
+        zero(nc.vector, w1s[1])
+        zero(nc.vector, w3s[1])
+        zero(nc.vector, gs_second)
+        zero(nc.vector, w1s[2])
+        zero(nc.vector, w2s)
+        load_second_token_scales(nc.gpsimd)
+        make_identity(nc, ident[:])
+        nc.sync.dma_start(offs_sb[:], offs)
+        load_both_token_scales(nc.scalar)
+        nc.scalar.activation(warm[:, 1:2], warm[:, 0:1], SIGMOID)
+        load_tokens(nc.sync, 0)
+        load_words(nc.sync, w1w[SHARED], w1_words[SHARED])
+        load_scales(nc.sync, w1s[0], group(w1_scales, 0))
+        load_scales(nc.scalar, w3s[0], group(w3_scales, 0))
+        load_words(nc.sync, w3w[SHARED], w3_words[SHARED])
+        load_tokens(nc.sync, 1)
+        load_expert_words(5)
+        gather_scales(4 * C, S)
+        gather_scales(2 * C, 4 * C)
+        gather_scales(0, 2 * C)
+        move_scales(nc.gpsimd, 0, 4 * C)
+        zero(nc.gpsimd, w3s[2])
+        gather_direct_scales(5 * C, S)
+        gather_words(5)
+        gather_direct_scales(4 * C, 5 * C)
+        gather_words(4)
+        load_scales(nc.scalar, w3s[1], group(w3_scales, 1))
+        load_scales(nc.sync, w1s[1], group(w1_scales, 1))
+        load_expert_words(4)
+        load_expert_words(3)
+        load_scales(nc.sync, w1s[2], group(w1_scales, 2))
+        load_expert_words(2)
+        load_expert_words(1)
+        load_scales(nc.sync, w2s, w2_scales)
+        nc.sync.dma_start(w2w[:].bitcast(I32), w2_words.rearrange("e s p b -> p (e s) b").bitcast(I32))
+        load_expert_words(0)
+        nc.sync.dma_start(pos1_sb[:], pos1)
+        nc.sync.dma_start(pos2_sb[:], pos2)
+        nc.sync.dma_start(gate_sb[:], gate.rearrange("g n t -> n g t"))
 
-        hs, quantised = {}, {}
-        done = 0
-        for k, (e, lo) in enumerate(units):
-            h0 = first_layer(e, lo)
-            if k == 0:
-                gather_packed_scales(0, 2 * C)
-                load_scales(nc.sync, w2s, w2_scales)
-                nc.sync.dma_start(w2w[:].bitcast(I32), w2_words.rearrange("e s p b -> p (e s) b").bitcast(I32))
-                for late in range(2, FIRST):
-                    load_words(w1w[late], w1_words[late])
-                    load_words(w3w[late], w3_words[late])
+        for k, (e, lo, tiles) in enumerate(units):
+            for half in range(tiles):
+                first_layer(first_tile[k] + half, e, lo + half * P)
+            if e != SHARED and e >= 2:
+                gather_words(e - 2)
+            if k >= 2:
+                second_layer(k - 2)
             if k >= 1:
-                hT = turn(hs[k - 1])
-            h1 = first_layer(e, lo + P)
-            hs[k] = (h0, h1)
-            if k < FIRST:
-                gather_words(k * C, (k + 1) * C)
-            if k == 1:
-                gather_packed_scales(2 * C, FIRST * C)
-                nc.sync.dma_start(pos1_sb[:], pos1)
-                nc.sync.dma_start(pos2_sb[:], pos2)
-                nc.sync.dma_start(gate_sb[:], gate.rearrange("g n t -> n g t"))
-            if k >= 1:
-                quantised[k - 1] = quantise(hT, k - 1)
-            while k >= 3 and done < k - 1:
-                finish(done, quantised[done])
-                done += 1
-            if k == len(units) - 2:
-                finish(done, quantised[done])
-                done += 1
+                turn(k - 1)
+                quantise(k - 1)
+            if k == 2:
+                load_scales(nc.scalar, w3s[2], group(w3_scales, 2))
 
-        last = len(units) - 1
         first_choice = held([P, T], F32, "first_choice")
         second_choice = held([P, T], F32, "second_choice")
+        second_layer(last - 1)
+        turn(last)
         nc.vector.tensor_tensor(first_choice[:], y_all[:].indirect(pos1_sb[:]), gate_sb[:, 0, :], MULT)
-        hT = turn(hs[last])
-        finish(last - 1, quantised[last - 1])
+        quantise(last)
         nc.vector.tensor_tensor(second_choice[:], y_all[:].indirect(pos2_sb[:]), gate_sb[:, 1, :], MULT)
-        quantised[last] = quantise(hT, last)
-        nc.vector.tensor_tensor(routed[:], first_choice[:], second_choice[:], ADD)
-        ys_last = finish(last, quantised[last])
-        nc.vector.tensor_tensor(result[:, 0 : 2 * C], routed[:, 0 : 2 * C], ys_front[:], ADD)
-        nc.sync.dma_start(out[:, 0 : 2 * C], result[:, 0 : 2 * C])
-        nc.vector.tensor_tensor(result[:, 2 * C : T], ys_last[:], routed[:, 2 * C : T], ADD)
-        nc.sync.dma_start(out[:, 2 * C : T], result[:, 2 * C : T])
+        second_layer(last)
+        nc.vector.tensor_tensor(routed[:, 0:early], first_choice[:, 0:early], ys_early[:], ADD)
+        nc.vector.tensor_tensor(routed[:, early:T], y_bank[:, 0 : T - early], first_choice[:, early:T], ADD)
+        for lo in range(0, T, T // 2):
+            cols = slice(lo, lo + T // 2)
+            nc.vector.tensor_tensor(result[:, cols], routed[:, cols], second_choice[:, cols], ADD)
+            nc.sync.dma_start(out[:, cols], result[:, cols])

@@ -21,12 +21,14 @@ SIGMOID = mybir.ActivationFunctionType.Sigmoid
 
 P = 128
 PASSES = K // 512
+QUADRANTS = 4
+LIST_ROWS = 16
 SHARED = E
 SCALE_WINDOW = 1024
 SCALE_GROUPS = ((5, 7), (3, 5), (0, 3))
-FRONT = (2,)
-DIRECT = 4
-BACK = (2, 1, 1)
+SHARED_FIRST = (2,)
+SHARED_LAST = (2, 1, 1)
+MOVED = E - 2
 
 
 def tile_moe_shr_glu_sigmoid_kernel(
@@ -50,7 +52,7 @@ def tile_moe_shr_glu_sigmoid_kernel(
             engine.memset(tile[:].bitcast(I32), 0)
 
         def load_scales(queue, plane, scales):
-            for q in range(4):
+            for q in range(QUADRANTS):
                 queue.dma_start(
                     plane[32 * q : 32 * q + 4, :, :].bitcast(I32),
                     scales[:, :, 4 * q : 4 * q + 4, :].rearrange("e s q n -> q (e s) n").bitcast(I32),
@@ -59,9 +61,9 @@ def tile_moe_shr_glu_sigmoid_kernel(
         def load_words(queue, tile, words):
             queue.dma_start(tile[:].bitcast(I32), words.rearrange("s p b -> p s b").bitcast(I32))
 
-        offs_sb = held([P, S // 16], U16, "offs_sb")
-        pos1_sb = held([P, T // 16], U16, "pos1_sb")
-        pos2_sb = held([P, T // 16], U16, "pos2_sb")
+        offs_sb = held([P, S // LIST_ROWS], U16, "offs_sb")
+        pos1_sb = held([P, T // LIST_ROWS], U16, "pos1_sb")
+        pos2_sb = held([P, T // LIST_ROWS], U16, "pos2_sb")
         xw = ring(PASSES, [P, T], I32, "xw")
         xs_both = held([P, SCALE_WINDOW], U8, "xs_both")
         xs_second = held([P, T], U8, "xs_second")
@@ -75,33 +77,32 @@ def tile_moe_shr_glu_sigmoid_kernel(
         ident = held([P, P], F32, "ident")
         gw = ring(2, [P, PASSES, C], U32, "gw")
         gs_both = held([P, S], U8, "gs_both")
-        gs_direct = held([P, S - DIRECT * C], U8, "gs_direct")
-        gs_second = held([P, DIRECT * C], U8, "gs_second")
+        gs_direct = held([P, S - MOVED * C], U8, "gs_direct")
+        gs_second = held([P, MOVED * C], U8, "gs_second")
         y_all = held([P, S], F32, "y_all")
-        warm = held([P, 2], F32, "warm")
         sig = ring(3, [P, 2, P, 2], F32, "sig")
         h = ring(4, [P, 2, P, 2], BF16, "h")
-        hT = ring(2, [P, 2, P, 4], BF16, "hT")
+        h_turned = ring(2, [P, 2, P, 4], BF16, "hT")
         a_banks = banks(2, [P, H], "a")
         b_banks = banks(3, [P, H], "b")
-        turned = banks(2, [P, 2, P], "turned")
+        turn_banks = banks(2, [P, 2, P], "turned")
         y_bank = psum.tile([P, C], F32, name="y_bank")
 
         def group(scales, g):
             return scales[SCALE_GROUPS[g][0] : SCALE_GROUPS[g][1]]
 
-        def load_tokens(queue, o):
-            queue.dma_start(xw[o][:], x_words[o].rearrange("p t r -> p (t r)").bitcast(I32))
+        def load_tokens(o):
+            nc.sync.dma_start(xw[o][:], x_words[o].rearrange("p t r -> p (t r)").bitcast(I32))
 
-        def load_both_token_scales(queue):
-            for q in range(4):
-                queue.dma_start(
+        def load_both_token_scales():
+            for q in range(QUADRANTS):
+                nc.scalar.dma_start(
                     xs_both[32 * q : 32 * q + 8, 0:T].bitcast(I32), x_scales[:, 4 * q : 4 * q + 4, :].bitcast(I32)
                 )
 
-        def load_second_token_scales(queue):
-            for q in range(4):
-                queue.dma_start(
+        def load_second_token_scales():
+            for q in range(QUADRANTS):
+                nc.gpsimd.dma_start(
                     xs_second[32 * q : 32 * q + 4, :].bitcast(I32), x_scales[1, 4 * q : 4 * q + 4, :].bitcast(I32)
                 )
 
@@ -110,42 +111,46 @@ def tile_moe_shr_glu_sigmoid_kernel(
             load_words(nc.sync, w3w[e], w3_words[e])
 
         def slot_offsets(lo, hi):
-            return offs_sb[:, lo // 16 : hi // 16]
+            return offs_sb[:, lo // LIST_ROWS : hi // LIST_ROWS]
 
         def gather_words(e):
             for o in range(PASSES):
                 nc.vector.tensor_copy(
-                    gw[e % 2][:, o, :], xw[o][:].bitcast(U32).indirect(slot_offsets(e * C, (e + 1) * C))
+                    gw[e % len(gw)][:, o, :], xw[o][:].bitcast(U32).indirect(slot_offsets(e * C, (e + 1) * C))
                 )
 
-        def gather_direct_scales(lo, hi):
+        def gather_second_scales(e):
             nc.vector.tensor_copy(
-                gs_direct[:, lo - DIRECT * C : hi - DIRECT * C], xs_second[:].indirect(slot_offsets(lo, hi))
+                gs_direct[:, (e - MOVED) * C : (e - MOVED + 1) * C],
+                xs_second[:].indirect(slot_offsets(e * C, (e + 1) * C)),
             )
 
-        def gather_scales(lo, hi):
+        def gather_both_scales(lo, hi):
             nc.vector.tensor_copy(gs_both[:, lo:hi], xs_both[:].indirect(slot_offsets(lo, hi)))
 
-        def move_scales(queue, lo, hi):
-            for q in range(4):
-                queue.dma_start(
-                    gs_second[32 * q : 32 * q + 4, lo:hi].bitcast(I32),
-                    gs_both[32 * q + 4 : 32 * q + 8, lo:hi].bitcast(I32),
+        def move_second_scales():
+            for q in range(QUADRANTS):
+                nc.gpsimd.dma_start(
+                    gs_second[32 * q : 32 * q + 4, :].bitcast(I32),
+                    gs_both[32 * q + 4 : 32 * q + 8, 0 : MOVED * C].bitcast(I32),
                 )
 
         def token_operands(e, lo, o):
             cols = slice(lo, lo + P)
             if e == SHARED:
                 return xw[o][:, cols], (xs_both, xs_second)[o][:, cols]
-            codes = gw[e % 2][:, o, lo - e * C : lo - e * C + P]
-            if o == 1 and e >= DIRECT:
-                return codes, gs_direct[:, lo - DIRECT * C : lo - DIRECT * C + P]
+            codes = gw[e % len(gw)][:, o, lo - e * C : lo - e * C + P]
+            if o == 1 and e >= MOVED:
+                return codes, gs_direct[:, lo - MOVED * C : lo - MOVED * C + P]
             return codes, (gs_both, gs_second)[o][:, cols]
 
         def first_layer(j, e, lo):
-            g = [lo_e <= e < hi_e for lo_e, hi_e in SCALE_GROUPS].index(True)
+            g = [first <= e < end for first, end in SCALE_GROUPS].index(True)
             row = (e - SCALE_GROUPS[g][0]) * PASSES
-            products = ((a_banks[j % 2], w1w[e], w1s[g]), (b_banks[j % 3], w3w[e], w3s[g]))
+            products = (
+                (a_banks[j % len(a_banks)], w1w[e], w1s[g]),
+                (b_banks[j % len(b_banks)], w3w[e], w3s[g]),
+            )
             for o in range(PASSES):
                 codes, code_scales = token_operands(e, lo, o)
                 for acc, words, scales in products:
@@ -158,67 +163,71 @@ def tile_moe_shr_glu_sigmoid_kernel(
                         start=(o == 0),
                         stop=(o == PASSES - 1),
                     )
-            sums = [acc[:].rearrange("t (p u f) -> t u p f", u=2, f=2) for acc, words, scales in products]
-            nc.scalar.activation(sig[j % 3][:], sums[0], SIGMOID)
-            nc.vector.tensor_tensor(h[j % len(h)][:], sums[1], sig[j % 3][:], MULT)
+            a, b = [acc[:].rearrange("t (p u f) -> t u p f", u=2, f=2) for acc, words, scales in products]
+            nc.scalar.activation(sig[j % len(sig)][:], a, SIGMOID)
+            nc.vector.tensor_tensor(h[j % len(h)][:], b, sig[j % len(sig)][:], MULT)
 
         units = []
         token = 0
-        for tiles in FRONT:
+        for tiles in SHARED_FIRST:
             units.append((SHARED, token, tiles))
             token += tiles * P
-        units.extend((e, e * C, 2) for e in reversed(range(E)))
-        for tiles in BACK:
+        units.extend((e, e * C, C // P) for e in reversed(range(E)))
+        for tiles in SHARED_LAST:
             units.append((SHARED, token, tiles))
             token += tiles * P
-        first_tile = [sum(u[2] for u in units[:k]) for k in range(len(units))]
+        first_tile = [sum(unit[2] for unit in units[:m]) for m in range(len(units))]
         h_codes = ring(len(units), [P, C], U32, "h_codes")
         h_scales = ring(len(units), [P, C], U8, "h_scales")
         last = len(units) - 1
         early = units[last][1]
         ys_early = held([P, early], F32, "ys_early")
-        routed = held([P, T], F32, "routed")
+        partial = held([P, T], F32, "routed")
         result = held([P, T], F32, "result")
 
-        def turn(k):
-            tiles = units[k][2]
+        def turn(m):
+            tiles = units[m][2]
             for u in range(2):
-                for half in range(tiles):
-                    j = first_tile[k] + half
+                for part in range(tiles):
+                    j = first_tile[m] + part
                     pairs = h[j % len(h)][:].rearrange("t u p f -> t (u p f)").bitcast(F32)
-                    nc.tensor.transpose(turned[j % 2][:, u, :], pairs[:, u * P : (u + 1) * P], ident[:])
-            for half in range(tiles):
-                j = first_tile[k] + half
-                nc.scalar.copy(hT[k % 2][:, half].bitcast(F32), turned[j % 2][:].rearrange("p u t -> p t u"))
+                    nc.tensor.transpose(
+                        turn_banks[j % len(turn_banks)][:, u, :], pairs[:, u * P : (u + 1) * P], ident[:]
+                    )
+            for part in range(tiles):
+                j = first_tile[m] + part
+                nc.scalar.copy(
+                    h_turned[m % len(h_turned)][:, part].bitcast(F32),
+                    turn_banks[j % len(turn_banks)][:].rearrange("p u t -> p t u"),
+                )
 
-        def quantise(k):
-            tiles = units[k][2]
+        def quantise(m):
+            tiles = units[m][2]
             nc.vector.quantize_mx(
-                out=h_codes[k][:, 0 : tiles * P].bitcast(FP8X4),
-                scales=h_scales[k][:, 0 : tiles * P],
-                in_=hT[k % 2][:, 0:tiles].rearrange("p j t r -> p (j t r)"),
+                out=h_codes[m][:, 0 : tiles * P].bitcast(FP8X4),
+                scales=h_scales[m][:, 0 : tiles * P],
+                in_=h_turned[m % len(h_turned)][:, 0:tiles].rearrange("p j t r -> p (j t r)"),
             )
 
-        def second_layer(k):
-            e, lo, tiles = units[k]
+        def second_layer(m):
+            e, lo, tiles = units[m]
             width = tiles * P
             nc.tensor.matmul_mx(
                 out=y_bank[:, 0:width],
                 lhsT=w2w[:, e, :].bitcast(FP4X4),
                 lhsT_scale=w2s[:, e, :],
-                rhs=h_codes[k][:, 0:width].bitcast(FP8X4),
-                rhs_scale=h_scales[k][:, 0:width],
+                rhs=h_codes[m][:, 0:width].bitcast(FP8X4),
+                rhs_scale=h_scales[m][:, 0:width],
                 start=True,
                 stop=True,
             )
             if e != SHARED:
                 nc.scalar.copy(y_all[:, lo : lo + width], y_bank[:, 0:width])
-            elif k < last:
+            elif m < last:
                 nc.scalar.copy(ys_early[:, lo : lo + width], y_bank[:, 0:width])
 
         zero(nc.vector, xs_both)
         zero(nc.gpsimd, xs_second)
-        nc.vector.memset(warm[:, 0:1], 0.0)
         zero(nc.vector, w1s[0])
         zero(nc.vector, w3s[0])
         zero(nc.vector, w1s[1])
@@ -226,34 +235,31 @@ def tile_moe_shr_glu_sigmoid_kernel(
         zero(nc.vector, gs_second)
         zero(nc.vector, w1s[2])
         zero(nc.vector, w2s)
-        load_second_token_scales(nc.gpsimd)
+        load_second_token_scales()
         make_identity(nc, ident[:])
         nc.sync.dma_start(offs_sb[:], offs)
-        load_both_token_scales(nc.scalar)
-        nc.scalar.activation(warm[:, 1:2], warm[:, 0:1], SIGMOID)
-        load_tokens(nc.sync, 0)
+        load_both_token_scales()
+        load_tokens(0)
         load_words(nc.sync, w1w[SHARED], w1_words[SHARED])
         load_scales(nc.sync, w1s[0], group(w1_scales, 0))
         load_scales(nc.scalar, w3s[0], group(w3_scales, 0))
         load_words(nc.sync, w3w[SHARED], w3_words[SHARED])
-        load_tokens(nc.sync, 1)
-        load_expert_words(5)
-        gather_scales(4 * C, S)
-        gather_scales(2 * C, 4 * C)
-        gather_scales(0, 2 * C)
-        move_scales(nc.gpsimd, 0, 4 * C)
+        load_tokens(1)
+        load_expert_words(E - 1)
+        for lo in reversed(range(0, S, 2 * C)):
+            gather_both_scales(lo, lo + 2 * C)
+        move_second_scales()
         zero(nc.gpsimd, w3s[2])
-        gather_direct_scales(5 * C, S)
-        gather_words(5)
-        gather_direct_scales(4 * C, 5 * C)
-        gather_words(4)
+        for e in reversed(range(MOVED, E)):
+            gather_second_scales(e)
+            gather_words(e)
         load_scales(nc.scalar, w3s[1], group(w3_scales, 1))
         load_scales(nc.sync, w1s[1], group(w1_scales, 1))
-        load_expert_words(4)
-        load_expert_words(3)
+        for e in reversed(range(*SCALE_GROUPS[1])):
+            load_expert_words(e)
         load_scales(nc.sync, w1s[2], group(w1_scales, 2))
-        load_expert_words(2)
-        load_expert_words(1)
+        for e in reversed(range(1, SCALE_GROUPS[2][1])):
+            load_expert_words(e)
         load_scales(nc.sync, w2s, w2_scales)
         nc.sync.dma_start(w2w[:].bitcast(I32), w2_words.rearrange("e s p b -> p (e s) b").bitcast(I32))
         load_expert_words(0)
@@ -261,17 +267,17 @@ def tile_moe_shr_glu_sigmoid_kernel(
         nc.sync.dma_start(pos2_sb[:], pos2)
         nc.sync.dma_start(gate_sb[:], gate.rearrange("g n t -> n g t"))
 
-        for k, (e, lo, tiles) in enumerate(units):
-            for half in range(tiles):
-                first_layer(first_tile[k] + half, e, lo + half * P)
-            if e != SHARED and e >= 2:
-                gather_words(e - 2)
-            if k >= 2:
-                second_layer(k - 2)
-            if k >= 1:
-                turn(k - 1)
-                quantise(k - 1)
-            if k == 2:
+        for m, (e, lo, tiles) in enumerate(units):
+            for part in range(tiles):
+                first_layer(first_tile[m] + part, e, lo + part * P)
+            if e != SHARED and e >= len(gw):
+                gather_words(e - len(gw))
+            if m >= 2:
+                second_layer(m - 2)
+            if m >= 1:
+                turn(m - 1)
+                quantise(m - 1)
+            if e == MOVED:
                 load_scales(nc.scalar, w3s[2], group(w3_scales, 2))
 
         first_choice = held([P, T], F32, "first_choice")
@@ -282,9 +288,9 @@ def tile_moe_shr_glu_sigmoid_kernel(
         quantise(last)
         nc.vector.tensor_tensor(second_choice[:], y_all[:].indirect(pos2_sb[:]), gate_sb[:, 1, :], MULT)
         second_layer(last)
-        nc.vector.tensor_tensor(routed[:, 0:early], first_choice[:, 0:early], ys_early[:], ADD)
-        nc.vector.tensor_tensor(routed[:, early:T], y_bank[:, 0 : T - early], first_choice[:, early:T], ADD)
+        nc.vector.tensor_tensor(partial[:, 0:early], first_choice[:, 0:early], ys_early[:], ADD)
+        nc.vector.tensor_tensor(partial[:, early:T], y_bank[:, 0 : T - early], first_choice[:, early:T], ADD)
         for lo in range(0, T, T // 2):
             cols = slice(lo, lo + T // 2)
-            nc.vector.tensor_tensor(result[:, cols], routed[:, cols], second_choice[:, cols], ADD)
+            nc.vector.tensor_tensor(result[:, cols], partial[:, cols], second_choice[:, cols], ADD)
             nc.sync.dma_start(out[:, cols], result[:, cols])

@@ -24,11 +24,10 @@ PASSES = K // 512
 QUADRANTS = 4
 LIST_ROWS = 16
 SHARED = E
-SCALE_WINDOW = 1024
-SCALE_GROUPS = ((5, 7), (3, 5), (0, 3))
-SHARED_FIRST = (2,)
-SHARED_LAST = (2, 1, 1)
-MOVED = E - 2
+DIRECT = 2
+SCALE_GROUPS = ((0, 3), (3, 7))
+WORD_GROUPS = ((0, 1), (1, 2), (2, 4), (4, 6), (6, 7))
+SHARED_UNITS = (2, 2, 1, 1)
 
 
 def tile_moe_shr_glu_sigmoid_kernel(
@@ -39,258 +38,285 @@ def tile_moe_shr_glu_sigmoid_kernel(
         keep = ctx.enter_context(tc.tile_pool(name="keep", bufs=1))
         psum = ctx.enter_context(tc.psum_pool(name="psum", bufs=1))
 
-        def held(shape, dtype, name):
-            return keep.tile(shape, dtype, name=name, align_bytes=64)
+        def held(shape, dtype, name, tag=None):
+            return keep.tile(shape, dtype, name=name, tag=tag or name, align_bytes=64)
 
         def ring(count, shape, dtype, name):
             return [held(shape, dtype, f"{name}{r}") for r in range(count)]
 
-        def banks(count, shape, name):
-            return [psum.tile(shape, F32, name=f"{name}{r}") for r in range(count)]
+        def banks(count, name):
+            return [psum.tile([P, H], F32, name=f"{name}{r}") for r in range(count)]
 
         def zero(engine, tile):
             engine.memset(tile[:].bitcast(I32), 0)
 
-        def load_scales(queue, plane, scales):
-            for q in range(QUADRANTS):
-                queue.dma_start(
-                    plane[32 * q : 32 * q + 4, :, :].bitcast(I32),
-                    scales[:, :, 4 * q : 4 * q + 4, :].rearrange("e s q n -> q (e s) n").bitcast(I32),
-                )
-
-        def load_words(queue, tile, words):
-            queue.dma_start(tile[:].bitcast(I32), words.rearrange("s p b -> p s b").bitcast(I32))
-
         offs_sb = held([P, S // LIST_ROWS], U16, "offs_sb")
-        pos1_sb = held([P, T // LIST_ROWS], U16, "pos1_sb")
-        pos2_sb = held([P, T // LIST_ROWS], U16, "pos2_sb")
+        pos_sb = [held([P, T // LIST_ROWS], U16, f"pos{r}_sb") for r in (1, 2)]
         xw = ring(PASSES, [P, T], I32, "xw")
-        xs_both = held([P, SCALE_WINDOW], U8, "xs_both")
-        xs_second = held([P, T], U8, "xs_second")
+        xs_planes = held([P, PASSES, T], U8, "xs_planes")
         w1s = [held([P, (hi - lo) * PASSES, H], U8, f"w1s{lo}") for lo, hi in SCALE_GROUPS]
         w3s = [held([P, (hi - lo) * PASSES, H], U8, f"w3s{lo}") for lo, hi in SCALE_GROUPS]
+        w1w = ring(3, [P, 2 * PASSES, 2 * H], U8, "w1w")
+        w3w = ring(3, [P, 2 * PASSES, 2 * H], U8, "w3w")
         w2s = held([P, E + 1, N], U8, "w2s")
-        w1w = ring(E + 1, [P, PASSES, 2 * H], U8, "w1w")
-        w3w = ring(E + 1, [P, PASSES, 2 * H], U8, "w3w")
         w2w = held([P, E + 1, 2 * N], U8, "w2w")
-        gate_sb = held([P, 2, T], F32, "gate_sb")
         ident = held([P, P], F32, "ident")
         gw = ring(2, [P, PASSES, C], U32, "gw")
-        gs_both = held([P, S], U8, "gs_both")
-        gs_direct = held([P, S - MOVED * C], U8, "gs_direct")
-        gs_second = held([P, MOVED * C], U8, "gs_second")
+        gs = ring(3, [P, PASSES, C], U8, "gs")
         y_all = held([P, S], F32, "y_all")
-        sig = ring(3, [P, 2, P, 2], F32, "sig")
-        h = ring(4, [P, 2, P, 2], BF16, "h")
-        h_turned = ring(2, [P, 2, P, 4], BF16, "hT")
-        a_banks = banks(2, [P, H], "a")
-        b_banks = banks(3, [P, H], "b")
-        turn_banks = banks(2, [P, 2, P], "turned")
-        y_bank = psum.tile([P, C], F32, name="y_bank")
+        sig = ring(3, [P, H], F32, "sig")
+        sig_shared = ring(T // P, [P, H], F32, "sig_shared")
+        h = ring(8, [P, H], BF16, "h")
+        h_turned = ring(3, [P, 2, P, 4], BF16, "hT")
+        a_banks = banks(3, "a")
+        b_banks = banks(4, "b")
+        spare_bank = psum.tile([P, H], F32, name="spare_bank")
 
-        def group(scales, g):
-            return scales[SCALE_GROUPS[g][0] : SCALE_GROUPS[g][1]]
+        def load_scales(queue, planes, scales, g):
+            lo, hi = SCALE_GROUPS[g]
+            for q in range(QUADRANTS):
+                queue.dma_start(
+                    planes[g][32 * q : 32 * q + 4, :, :].bitcast(I32),
+                    scales[lo:hi, :, 4 * q : 4 * q + 4, :].rearrange("e s q n -> q (e s) n").bitcast(I32),
+                )
+
+        def load_words(slots, words, g):
+            lo, hi = WORD_GROUPS[g]
+            nc.sync.dma_start(
+                slots[g % len(slots)][:, 0 : (hi - lo) * PASSES, :].bitcast(I32),
+                words[lo:hi].rearrange("e s p b -> p (e s) b").bitcast(I32),
+            )
 
         def load_tokens(o):
             nc.sync.dma_start(xw[o][:], x_words[o].rearrange("p t r -> p (t r)").bitcast(I32))
 
-        def load_both_token_scales():
+        def load_token_planes():
             for q in range(QUADRANTS):
-                nc.scalar.dma_start(
-                    xs_both[32 * q : 32 * q + 8, 0:T].bitcast(I32), x_scales[:, 4 * q : 4 * q + 4, :].bitcast(I32)
+                nc.sync.dma_start(
+                    xs_planes[32 * q : 32 * q + 4, :, :].bitcast(I32),
+                    x_scales[:, 4 * q : 4 * q + 4, :].rearrange("s q n -> q s n").bitcast(I32),
                 )
-
-        def load_second_token_scales():
-            for q in range(QUADRANTS):
-                nc.gpsimd.dma_start(
-                    xs_second[32 * q : 32 * q + 4, :].bitcast(I32), x_scales[1, 4 * q : 4 * q + 4, :].bitcast(I32)
-                )
-
-        def load_expert_words(e):
-            load_words(nc.sync, w1w[e], w1_words[e])
-            load_words(nc.sync, w3w[e], w3_words[e])
 
         def slot_offsets(lo, hi):
             return offs_sb[:, lo // LIST_ROWS : hi // LIST_ROWS]
 
-        def gather_words(e):
-            for o in range(PASSES):
-                nc.vector.tensor_copy(
-                    gw[e % len(gw)][:, o, :], xw[o][:].bitcast(U32).indirect(slot_offsets(e * C, (e + 1) * C))
-                )
-
-        def gather_second_scales(e):
+        def gather_words(e, o):
             nc.vector.tensor_copy(
-                gs_direct[:, (e - MOVED) * C : (e - MOVED + 1) * C],
-                xs_second[:].indirect(slot_offsets(e * C, (e + 1) * C)),
+                gw[e % len(gw)][:, o, :], xw[o][:].bitcast(U32).indirect(slot_offsets(e * C, (e + 1) * C))
             )
 
-        def gather_both_scales(lo, hi):
-            nc.vector.tensor_copy(gs_both[:, lo:hi], xs_both[:].indirect(slot_offsets(lo, hi)))
+        def gather_scales(target, window, lo, hi):
+            nc.vector.tensor_copy(target, window.indirect(slot_offsets(lo * C, hi * C)))
 
-        def move_second_scales():
-            for q in range(QUADRANTS):
-                nc.gpsimd.dma_start(
-                    gs_second[32 * q : 32 * q + 4, :].bitcast(I32),
-                    gs_both[32 * q + 4 : 32 * q + 8, 0 : MOVED * C].bitcast(I32),
-                )
+        def expert_plane(e, o):
+            return gs[e % len(gs)][:, o, :]
 
         def token_operands(e, lo, o):
-            cols = slice(lo, lo + P)
             if e == SHARED:
-                return xw[o][:, cols], (xs_both, xs_second)[o][:, cols]
-            codes = gw[e % len(gw)][:, o, lo - e * C : lo - e * C + P]
-            if o == 1 and e >= MOVED:
-                return codes, gs_direct[:, lo - MOVED * C : lo - MOVED * C + P]
-            return codes, (gs_both, gs_second)[o][:, cols]
+                return xw[o][:, lo : lo + P], xs_planes[:, o, lo : lo + P]
+            c = lo - e * C
+            return gw[e % len(gw)][:, o, c : c + P], expert_plane(e, o)[:, c : c + P]
 
-        def first_layer(j, e, lo):
-            g = [first <= e < end for first, end in SCALE_GROUPS].index(True)
-            row = (e - SCALE_GROUPS[g][0]) * PASSES
-            products = (
-                (a_banks[j % len(a_banks)], w1w[e], w1s[g]),
-                (b_banks[j % len(b_banks)], w3w[e], w3s[g]),
-            )
-            for o in range(PASSES):
+        def place(groups, e, o):
+            g = [first <= e < end for first, end in groups].index(True)
+            return g, (e - groups[g][0]) * PASSES + o
+
+        def a_bank(j):
+            if j >= S // P:
+                return a_banks[2 * (j % 2)]
+            return a_banks[1] if j % 2 else a_banks[j % 4]
+
+        def product(bank, slots, planes, e, lo, passes):
+            for o in passes:
+                g, row = place(SCALE_GROUPS, e, o)
+                gword, wrow = place(WORD_GROUPS, e, o)
                 codes, code_scales = token_operands(e, lo, o)
-                for acc, words, scales in products:
-                    nc.tensor.matmul_mx(
-                        out=acc[:],
-                        lhsT=codes.bitcast(FP8X4),
-                        lhsT_scale=code_scales,
-                        rhs=words[:, o, :].bitcast(FP4X4),
-                        rhs_scale=scales[:, row + o, :],
-                        start=(o == 0),
-                        stop=(o == PASSES - 1),
-                    )
-            a, b = [acc[:].rearrange("t (p u f) -> t u p f", u=2, f=2) for acc, words, scales in products]
-            nc.scalar.activation(sig[j % len(sig)][:], a, SIGMOID)
-            nc.vector.tensor_tensor(h[j % len(h)][:], b, sig[j % len(sig)][:], MULT)
+                nc.tensor.matmul_mx(
+                    out=bank[:],
+                    lhsT=codes.bitcast(FP8X4),
+                    lhsT_scale=code_scales,
+                    rhs=slots[gword % len(slots)][:, wrow, :].bitcast(FP4X4),
+                    rhs_scale=planes[g][:, row, :],
+                    start=(o == 0),
+                    stop=(o == PASSES - 1),
+                )
 
-        units = []
+        def sig_tile(j):
+            return sig[j % len(sig)] if j < S // P else sig_shared[j - S // P]
+
+        def paired(ap):
+            return ap.rearrange("t (u p f) -> t u p f", u=2, f=2)
+
+        def permuted(ap):
+            return ap.rearrange("t (p u f) -> t u p f", u=2, f=2)
+
+        def product_a(j, e, lo, passes=(0, 1)):
+            product(a_bank(j), w1w, w1s, e, lo, passes)
+            if passes[-1] != PASSES - 1:
+                return
+            nc.scalar.activation(paired(sig_tile(j)[:]), permuted(a_bank(j)[:]), SIGMOID)
+
+        def product_b(j, e, lo, passes=(0, 1)):
+            product(b_banks[j % len(b_banks)], w3w, w3s, e, lo, passes)
+            if passes[-1] != PASSES - 1:
+                return
+            nc.vector.tensor_tensor(
+                paired(h[j % len(h)][:]), permuted(b_banks[j % len(b_banks)][:]), paired(sig_tile(j)[:]), MULT
+            )
+
+        units = [(e, e * C, C // P) for e in range(E)]
         token = 0
-        for tiles in SHARED_FIRST:
-            units.append((SHARED, token, tiles))
-            token += tiles * P
-        units.extend((e, e * C, C // P) for e in reversed(range(E)))
-        for tiles in SHARED_LAST:
+        for tiles in SHARED_UNITS:
             units.append((SHARED, token, tiles))
             token += tiles * P
         first_tile = [sum(unit[2] for unit in units[:m]) for m in range(len(units))]
         h_codes = ring(len(units), [P, C], U32, "h_codes")
         h_scales = ring(len(units), [P, C], U8, "h_scales")
-        last = len(units) - 1
-        early = units[last][1]
-        ys_early = held([P, early], F32, "ys_early")
-        partial = held([P, T], F32, "routed")
+        products0 = held([P, 2 * C], F32, "products0")
+        partial = held([P, T], F32, "partial")
         result = held([P, T], F32, "result")
 
-        def turn(m):
-            tiles = units[m][2]
-            for u in range(2):
-                for part in range(tiles):
-                    j = first_tile[m] + part
-                    pairs = h[j % len(h)][:].rearrange("t u p f -> t (u p f)").bitcast(F32)
-                    nc.tensor.transpose(
-                        turn_banks[j % len(turn_banks)][:, u, :], pairs[:, u * P : (u + 1) * P], ident[:]
-                    )
-            for part in range(tiles):
-                j = first_tile[m] + part
-                nc.scalar.copy(
-                    h_turned[m % len(h_turned)][:, part].bitcast(F32),
-                    turn_banks[j % len(turn_banks)][:].rearrange("p u t -> p t u"),
-                )
+        def tile_products(m, part):
+            e, lo, tiles = units[m]
+            product_a(first_tile[m] + part, e, lo + part * P)
+            product_b(first_tile[m] + part, e, lo + part * P)
 
-        def quantise(m):
+        def turn(m, bank):
             tiles = units[m][2]
+            for part in range(tiles):
+                pairs = h[(first_tile[m] + part) % len(h)][:].bitcast(F32)
+                for u in range(2):
+                    nc.tensor.transpose(
+                        bank[:, (2 * part + u) * P : (2 * part + u + 1) * P], pairs[:, u * P : (u + 1) * P], ident[:]
+                    )
+            turned = h_turned[m % len(h_turned)]
+            nc.scalar.copy(
+                turned[:, 0:tiles].bitcast(F32),
+                bank[:, 0 : 2 * tiles * P].rearrange("p (j u t) -> p j t u", u=2, t=P),
+            )
             nc.vector.quantize_mx(
                 out=h_codes[m][:, 0 : tiles * P].bitcast(FP8X4),
                 scales=h_scales[m][:, 0 : tiles * P],
-                in_=h_turned[m % len(h_turned)][:, 0:tiles].rearrange("p j t r -> p (j t r)"),
+                in_=turned[:, 0:tiles].rearrange("p j t r -> p (j t r)"),
             )
 
-        def second_layer(m):
+        def second_layer(m, target):
             e, lo, tiles = units[m]
-            width = tiles * P
             nc.tensor.matmul_mx(
-                out=y_bank[:, 0:width],
+                out=target,
                 lhsT=w2w[:, e, :].bitcast(FP4X4),
                 lhsT_scale=w2s[:, e, :],
-                rhs=h_codes[m][:, 0:width].bitcast(FP8X4),
-                rhs_scale=h_scales[m][:, 0:width],
+                rhs=h_codes[m][:, 0 : tiles * P].bitcast(FP8X4),
+                rhs_scale=h_scales[m][:, 0 : tiles * P],
                 start=True,
                 stop=True,
             )
-            if e != SHARED:
-                nc.scalar.copy(y_all[:, lo : lo + width], y_bank[:, 0:width])
-            elif m < last:
-                nc.scalar.copy(ys_early[:, lo : lo + width], y_bank[:, 0:width])
 
-        zero(nc.vector, xs_both)
-        zero(nc.gpsimd, xs_second)
+        def routed_results(lo, hi):
+            for e in range(lo, hi):
+                second_layer(e, a_banks[1][:, (e - lo) * C : (e - lo + 1) * C])
+            nc.scalar.copy(y_all[:, lo * C : hi * C], a_banks[1][:, 0 : (hi - lo) * C])
+
+        zero(nc.gpsimd, xs_planes)
         zero(nc.vector, w1s[0])
         zero(nc.vector, w3s[0])
-        zero(nc.vector, w1s[1])
-        zero(nc.vector, w3s[1])
-        zero(nc.vector, gs_second)
-        zero(nc.vector, w1s[2])
-        zero(nc.vector, w2s)
-        load_second_token_scales()
         make_identity(nc, ident[:])
+        zero(nc.gpsimd, w3s[1])
+        zero(nc.gpsimd, w1s[1])
+        zero(nc.gpsimd, w2s)
         nc.sync.dma_start(offs_sb[:], offs)
-        load_both_token_scales()
         load_tokens(0)
-        load_words(nc.sync, w1w[SHARED], w1_words[SHARED])
-        load_scales(nc.sync, w1s[0], group(w1_scales, 0))
-        load_scales(nc.scalar, w3s[0], group(w3_scales, 0))
-        load_words(nc.sync, w3w[SHARED], w3_words[SHARED])
         load_tokens(1)
-        load_expert_words(E - 1)
-        for lo in reversed(range(0, S, 2 * C)):
-            gather_both_scales(lo, lo + 2 * C)
-        move_second_scales()
-        zero(nc.gpsimd, w3s[2])
-        for e in reversed(range(MOVED, E)):
-            gather_second_scales(e)
-            gather_words(e)
-        load_scales(nc.scalar, w3s[1], group(w3_scales, 1))
-        load_scales(nc.sync, w1s[1], group(w1_scales, 1))
-        for e in reversed(range(*SCALE_GROUPS[1])):
-            load_expert_words(e)
-        load_scales(nc.sync, w1s[2], group(w1_scales, 2))
-        for e in reversed(range(1, SCALE_GROUPS[2][1])):
-            load_expert_words(e)
-        load_scales(nc.sync, w2s, w2_scales)
+        load_token_planes()
+        load_words(w1w, w1_words, 0)
+        load_scales(nc.sync, w1s, w1_scales, 0)
+        load_words(w3w, w3_words, 0)
+        load_scales(nc.sync, w3s, w3_scales, 0)
+        load_words(w3w, w3_words, 1)
+        load_words(w1w, w1_words, 1)
+        load_words(w3w, w3_words, 2)
+        load_words(w1w, w1_words, 2)
         nc.sync.dma_start(w2w[:].bitcast(I32), w2_words.rearrange("e s p b -> p (e s) b").bitcast(I32))
-        load_expert_words(0)
-        nc.sync.dma_start(pos1_sb[:], pos1)
-        nc.sync.dma_start(pos2_sb[:], pos2)
-        nc.sync.dma_start(gate_sb[:], gate.rearrange("g n t -> n g t"))
+        for q in range(QUADRANTS):
+            nc.sync.dma_start(
+                w2s[32 * q : 32 * q + 4, :, :].bitcast(I32),
+                w2_scales[:, :, 4 * q : 4 * q + 4, :].rearrange("e s q n -> q (e s) n").bitcast(I32),
+            )
+        load_scales(nc.sync, w3s, w3_scales, 1)
+        load_scales(nc.sync, w1s, w1_scales, 1)
 
-        for m, (e, lo, tiles) in enumerate(units):
-            for part in range(tiles):
-                first_layer(first_tile[m] + part, e, lo + part * P)
-            if e != SHARED and e >= len(gw):
-                gather_words(e - len(gw))
-            if m >= 2:
-                second_layer(m - 2)
-            if m >= 1:
-                turn(m - 1)
-                quantise(m - 1)
-            if e == MOVED:
-                load_scales(nc.scalar, w3s[2], group(w3_scales, 2))
+        for e in range(DIRECT):
+            for o in range(PASSES):
+                gather_scales(expert_plane(e, o), xs_planes[:, o, :], e, e + 1)
+                gather_words(e, o)
+        for o in range(PASSES):
+            gather_scales(expert_plane(2, o), xs_planes[:, o, :], 2, 3)
 
-        first_choice = held([P, T], F32, "first_choice")
-        second_choice = held([P, T], F32, "second_choice")
-        second_layer(last - 1)
-        turn(last)
-        nc.vector.tensor_tensor(first_choice[:], y_all[:].indirect(pos1_sb[:]), gate_sb[:, 0, :], MULT)
-        quantise(last)
-        nc.vector.tensor_tensor(second_choice[:], y_all[:].indirect(pos2_sb[:]), gate_sb[:, 1, :], MULT)
-        second_layer(last)
-        nc.vector.tensor_tensor(partial[:, 0:early], first_choice[:, 0:early], ys_early[:], ADD)
-        nc.vector.tensor_tensor(partial[:, early:T], y_bank[:, 0 : T - early], first_choice[:, early:T], ADD)
-        for lo in range(0, T, T // 2):
-            cols = slice(lo, lo + T // 2)
-            nc.vector.tensor_tensor(result[:, cols], partial[:, cols], second_choice[:, cols], ADD)
+        gate_sb = []
+        for e in range(E):
+            if e == 0:
+                for o in range(PASSES):
+                    for part in range(2):
+                        product_a(part, 0, part * P, (o,))
+                for o in range(PASSES):
+                    for part in range(2):
+                        product_b(part, 0, part * P, (o,))
+            else:
+                for part in range(2):
+                    tile_products(e, part)
+            if e + 2 < E:
+                for o in range(PASSES):
+                    gather_words(e + 2, o)
+            if e + 3 < E:
+                for o in range(PASSES):
+                    gather_scales(expert_plane(e + 3, o), xs_planes[:, o, :], e + 3, e + 4)
+            if e < 2:
+                load_words(w3w, w3_words, 3 + e)
+                load_words(w1w, w1_words, 3 + e)
+            if e == 3:
+                gate_sb.append(held([P, 2, T], F32, "gate_sb", "w3s0"))
+                nc.sync.dma_start(gate_sb[0][:], gate.rearrange("g n t -> n g t"))
+                nc.sync.dma_start(pos_sb[0][:], pos1)
+                nc.sync.dma_start(pos_sb[1][:], pos2)
+            if e >= 1:
+                turn(e - 1, a_bank(2 * e))
+            if e == E - 1:
+                turn(e, spare_bank)
+            if e >= 2:
+                routed_results(e - 2, e - 1)
+
+        def choice(r, block, target):
+            cols = slice(block * C, (block + 1) * C)
+            offsets = pos_sb[r][:, block * C // LIST_ROWS : (block + 1) * C // LIST_ROWS]
+            nc.vector.tensor_tensor(target, y_all[:].indirect(offsets), gate_sb[0][:, r, cols], MULT)
+
+        def combine(block, first, second):
+            choice(0, block, first)
+            choice(1, block, second)
+            nc.vector.tensor_tensor(partial[:, block * C : (block + 1) * C], first, second, ADD)
+
+        def finish(m, bank):
+            e, lo, tiles = units[m]
+            cols = slice(lo, lo + tiles * P)
+            second_layer(m, bank[:, 0 : tiles * P])
+            nc.vector.tensor_tensor(result[:, cols], bank[:, 0 : tiles * P], partial[:, cols], ADD)
             nc.sync.dma_start(out[:, cols], result[:, cols])
+
+        tile_products(E, 0)
+        routed_results(E - 2, E)
+        tile_products(E, 1)
+        tile_products(E + 1, 0)
+        combine(0, products0[:, 0:C], products0[:, C : 2 * C])
+        turn(E, spare_bank)
+        tile_products(E + 1, 1)
+        tile_products(E + 2, 0)
+        combine(1, sig_shared[2][:, 0:C], sig_shared[2][:, C : 2 * C])
+        finish(E, a_banks[1])
+        turn(E + 1, spare_bank)
+        tile_products(E + 3, 0)
+        finish(E + 1, b_banks[2])
+        turn(E + 2, a_banks[0])
+        turn(E + 3, spare_bank)
+        combine(2, sig_shared[4][:, 0:C], sig_shared[5][:, 0:C])
+        finish(E + 2, b_banks[3])
+        finish(E + 3, b_banks[0])

@@ -24,9 +24,8 @@ PASSES = K // 512
 QUADRANTS = 4
 LIST_ROWS = 16
 SHARED = E
-DIRECT = 2
-SCALE_GROUPS = ((0, 3), (3, 7))
-WORD_GROUPS = ((0, 1), (1, 2), (2, 4), (4, 6), (6, 7))
+SCALE_GROUPS = ((0, 2), (2, 7))
+WORD_GROUPS = ((0, 1), (1, 3), (3, 5), (5, 7))
 SHARED_UNITS = (2, 2, 1, 1)
 
 
@@ -56,13 +55,16 @@ def tile_moe_shr_glu_sigmoid_kernel(
         xs_planes = held([P, PASSES, T], U8, "xs_planes")
         w1s = [held([P, (hi - lo) * PASSES, H], U8, f"w1s{lo}") for lo, hi in SCALE_GROUPS]
         w3s = [held([P, (hi - lo) * PASSES, H], U8, f"w3s{lo}") for lo, hi in SCALE_GROUPS]
-        w1w = ring(3, [P, 2 * PASSES, 2 * H], U8, "w1w")
-        w3w = ring(3, [P, 2 * PASSES, 2 * H], U8, "w3w")
+        w1w = [held([P, (hi - lo) * PASSES, 2 * H], U8, f"w1w{lo}") for lo, hi in WORD_GROUPS]
+        w3w = [held([P, (hi - lo) * PASSES, 2 * H], U8, f"w3w{lo}") for lo, hi in WORD_GROUPS]
         w2s = held([P, E + 1, N], U8, "w2s")
         w2w = held([P, E + 1, 2 * N], U8, "w2w")
         ident = held([P, P], F32, "ident")
         gw = ring(2, [P, PASSES, C], U32, "gw")
-        gs = ring(3, [P, PASSES, C], U8, "gs")
+        gs_direct = ring(3, [P, C], U8, "gs_direct")
+        gs_one = held([P, C], U8, "gs_one")
+        gs_packed = held([P, 4 * C], U8, "gs_packed")
+        gs_moved = held([P, 4 * C], U8, "gs_moved")
         y_all = held([P, S], F32, "y_all")
         sig = ring(3, [P, H], F32, "sig")
         sig_shared = ring(T // P, [P, H], F32, "sig_shared")
@@ -72,30 +74,17 @@ def tile_moe_shr_glu_sigmoid_kernel(
         b_banks = banks(4, "b")
         spare_bank = psum.tile([P, H], F32, name="spare_bank")
 
-        def load_scales(queue, planes, scales, g):
+        def load_rows(queue, plane, rows, r):
+            queue.dma_start(plane[r:P:32].bitcast(I32), rows[r:16:4].bitcast(I32))
+
+        def load_scales(queue, planes, scales, g, which=range(4)):
             lo, hi = SCALE_GROUPS[g]
-            for q in range(QUADRANTS):
-                queue.dma_start(
-                    planes[g][32 * q : 32 * q + 4, :, :].bitcast(I32),
-                    scales[lo:hi, :, 4 * q : 4 * q + 4, :].rearrange("e s q n -> q (e s) n").bitcast(I32),
-                )
+            for r in which:
+                load_rows(queue, planes[g], scales[lo:hi].rearrange("e s f n -> f (e s) n"), r)
 
         def load_words(slots, words, g):
             lo, hi = WORD_GROUPS[g]
-            nc.sync.dma_start(
-                slots[g % len(slots)][:, 0 : (hi - lo) * PASSES, :].bitcast(I32),
-                words[lo:hi].rearrange("e s p b -> p (e s) b").bitcast(I32),
-            )
-
-        def load_tokens(o):
-            nc.sync.dma_start(xw[o][:], x_words[o].rearrange("p t r -> p (t r)").bitcast(I32))
-
-        def load_token_planes():
-            for q in range(QUADRANTS):
-                nc.sync.dma_start(
-                    xs_planes[32 * q : 32 * q + 4, :, :].bitcast(I32),
-                    x_scales[:, 4 * q : 4 * q + 4, :].rearrange("s q n -> q s n").bitcast(I32),
-                )
+            nc.sync.dma_start(slots[g][:].bitcast(I32), words[lo:hi].rearrange("e s p b -> p (e s) b").bitcast(I32))
 
         def slot_offsets(lo, hi):
             return offs_sb[:, lo // LIST_ROWS : hi // LIST_ROWS]
@@ -105,11 +94,19 @@ def tile_moe_shr_glu_sigmoid_kernel(
                 gw[e % len(gw)][:, o, :], xw[o][:].bitcast(U32).indirect(slot_offsets(e * C, (e + 1) * C))
             )
 
-        def gather_scales(target, window, lo, hi):
-            nc.vector.tensor_copy(target, window.indirect(slot_offsets(lo * C, hi * C)))
+        def gather_scales(target, o, lo, hi):
+            nc.vector.tensor_copy(target, xs_planes[:, o, :].indirect(slot_offsets(lo, hi)))
+
+        def move_second_planes(target, gathered):
+            for r in range(4):
+                nc.sync.dma_start(target[r:P:32].bitcast(I32), gathered[16 + r : 32 : 4].bitcast(I32))
 
         def expert_plane(e, o):
-            return gs[e % len(gs)][:, o, :]
+            if e == 0:
+                return gs_direct[o][:]
+            if e == 1:
+                return (gs_one, gs_direct[2])[o][:]
+            return (gs_packed, gs_moved)[o][:, (e - 2) * C : (e - 1) * C]
 
         def token_operands(e, lo, o):
             if e == SHARED:
@@ -135,7 +132,7 @@ def tile_moe_shr_glu_sigmoid_kernel(
                     out=bank[:],
                     lhsT=codes.bitcast(FP8X4),
                     lhsT_scale=code_scales,
-                    rhs=slots[gword % len(slots)][:, wrow, :].bitcast(FP4X4),
+                    rhs=slots[gword][:, wrow, :].bitcast(FP4X4),
                     rhs_scale=planes[g][:, row, :],
                     start=(o == 0),
                     stop=(o == PASSES - 1),
@@ -219,38 +216,48 @@ def tile_moe_shr_glu_sigmoid_kernel(
 
         zero(nc.gpsimd, xs_planes)
         zero(nc.vector, w1s[0])
-        zero(nc.vector, w3s[0])
+        zero(nc.gpsimd, w3s[0])
+        zero(nc.vector, w3s[1])
         make_identity(nc, ident[:])
-        zero(nc.gpsimd, w3s[1])
-        zero(nc.gpsimd, w1s[1])
-        zero(nc.gpsimd, w2s)
+        for plane in (w1s[1], gs_moved, w2s):
+            zero(nc.gpsimd, plane)
+        token_rows = x_scales.rearrange("s f t -> f s t")
+
+        def load_tokens(o):
+            nc.sync.dma_start(xw[o][:], x_words[o].rearrange("p t r -> p (t r)").bitcast(I32))
+
         nc.sync.dma_start(offs_sb[:], offs)
         load_tokens(0)
-        load_tokens(1)
-        load_token_planes()
+        for r in range(4):
+            load_rows(nc.sync, xs_planes, token_rows, r)
         load_words(w1w, w1_words, 0)
         load_scales(nc.sync, w1s, w1_scales, 0)
+        load_tokens(1)
         load_words(w3w, w3_words, 0)
         load_scales(nc.sync, w3s, w3_scales, 0)
+        gather_words(0, 0)
+        for o in range(PASSES):
+            gather_scales(expert_plane(0, o), o, 0, C)
+        nc.sync.dma_start(xs_planes[16:32, 0, :].bitcast(I32), x_scales[1].bitcast(I32))
+        gather_words(0, 1)
         load_words(w3w, w3_words, 1)
         load_words(w1w, w1_words, 1)
-        load_words(w3w, w3_words, 2)
-        load_words(w1w, w1_words, 2)
-        nc.sync.dma_start(w2w[:].bitcast(I32), w2_words.rearrange("e s p b -> p (e s) b").bitcast(I32))
-        for q in range(QUADRANTS):
-            nc.sync.dma_start(
-                w2s[32 * q : 32 * q + 4, :, :].bitcast(I32),
-                w2_scales[:, :, 4 * q : 4 * q + 4, :].rearrange("e s q n -> q (e s) n").bitcast(I32),
-            )
+        gather_words(1, 0)
+        gather_words(1, 1)
+        for o in range(PASSES):
+            gather_scales(expert_plane(1, o), o, C, 2 * C)
+        for pair in range(2):
+            gather_scales(gs_packed[:, 2 * pair * C : 2 * (pair + 1) * C], 0, 2 * (pair + 1) * C, 2 * (pair + 2) * C)
         load_scales(nc.sync, w3s, w3_scales, 1)
         load_scales(nc.sync, w1s, w1_scales, 1)
-
-        for e in range(DIRECT):
-            for o in range(PASSES):
-                gather_scales(expert_plane(e, o), xs_planes[:, o, :], e, e + 1)
-                gather_words(e, o)
-        for o in range(PASSES):
-            gather_scales(expert_plane(2, o), xs_planes[:, o, :], 2, 3)
+        move_second_planes(gs_moved, gs_packed)
+        nc.sync.dma_start(w2w[:].bitcast(I32), w2_words.rearrange("e s p b -> p (e s) b").bitcast(I32))
+        for r in range(4):
+            load_rows(nc.sync, w2s, w2_scales.rearrange("e s f n -> f (e s) n"), r)
+        load_words(w3w, w3_words, 2)
+        load_words(w1w, w1_words, 2)
+        load_words(w3w, w3_words, 3)
+        load_words(w1w, w1_words, 3)
 
         gate_sb = []
         for e in range(E):
@@ -261,20 +268,19 @@ def tile_moe_shr_glu_sigmoid_kernel(
                 for o in range(PASSES):
                     for part in range(2):
                         product_b(part, 0, part * P, (o,))
+            elif e == 2:
+                for o in range(PASSES):
+                    for part in range(2):
+                        product_a(4 + part, 2, 2 * C + part * P, (o,))
+                        product_b(4 + part, 2, 2 * C + part * P, (o,))
             else:
                 for part in range(2):
                     tile_products(e, part)
             if e + 2 < E:
                 for o in range(PASSES):
                     gather_words(e + 2, o)
-            if e + 3 < E:
-                for o in range(PASSES):
-                    gather_scales(expert_plane(e + 3, o), xs_planes[:, o, :], e + 3, e + 4)
-            if e < 2:
-                load_words(w3w, w3_words, 3 + e)
-                load_words(w1w, w1_words, 3 + e)
             if e == 3:
-                gate_sb.append(held([P, 2, T], F32, "gate_sb", "w3s0"))
+                gate_sb.append(held([P, 2, T], F32, "gate_sb"))
                 nc.sync.dma_start(gate_sb[0][:], gate.rearrange("g n t -> n g t"))
                 nc.sync.dma_start(pos_sb[0][:], pos1)
                 nc.sync.dma_start(pos_sb[1][:], pos2)

@@ -24,8 +24,8 @@ PASSES = K // 512
 QUADRANTS = 4
 LIST_ROWS = 16
 SHARED = E
-SCALE_GROUPS = ((0, 2), (2, 7))
-WORD_GROUPS = ((0, 1), (1, 3), (3, 5), (5, 7))
+SCALE_GROUPS = ((0, 2), (2, 4), (4, 7))
+WORD_GROUPS = tuple((e, e + 1) for e in range(E + 1))
 SHARED_UNITS = (2, 2, 1, 1)
 
 
@@ -217,9 +217,10 @@ def tile_moe_shr_glu_sigmoid_kernel(
         zero(nc.gpsimd, xs_planes)
         zero(nc.vector, w1s[0])
         zero(nc.gpsimd, w3s[0])
-        zero(nc.vector, w3s[1])
+        zero(nc.vector, w3s[2])
+        zero(nc.vector, w1s[2])
         make_identity(nc, ident[:])
-        for plane in (w1s[1], gs_moved, w2s):
+        for plane in (w3s[1], w1s[1], gs_moved, w2s):
             zero(nc.gpsimd, plane)
         token_rows = x_scales.rearrange("s f t -> f s t")
 
@@ -248,16 +249,17 @@ def tile_moe_shr_glu_sigmoid_kernel(
             gather_scales(expert_plane(1, o), o, C, 2 * C)
         for pair in range(2):
             gather_scales(gs_packed[:, 2 * pair * C : 2 * (pair + 1) * C], 0, 2 * (pair + 1) * C, 2 * (pair + 2) * C)
-        load_scales(nc.sync, w3s, w3_scales, 1)
-        load_scales(nc.sync, w1s, w1_scales, 1)
-        move_second_planes(gs_moved, gs_packed)
-        nc.sync.dma_start(w2w[:].bitcast(I32), w2_words.rearrange("e s p b -> p (e s) b").bitcast(I32))
-        for r in range(4):
-            load_rows(nc.sync, w2s, w2_scales.rearrange("e s f n -> f (e s) n"), r)
-        load_words(w3w, w3_words, 2)
-        load_words(w1w, w1_words, 2)
-        load_words(w3w, w3_words, 3)
-        load_words(w1w, w1_words, 3)
+        for e in range(2, E + 1):
+            if e == 3:
+                move_second_planes(gs_moved, gs_packed)
+            if e == 5:
+                nc.sync.dma_start(w2w[:].bitcast(I32), w2_words.rearrange("e s p b -> p (e s) b").bitcast(I32))
+                for r in range(4):
+                    load_rows(nc.sync, w2s, w2_scales.rearrange("e s f n -> f (e s) n"), r)
+            for slots, words, planes, scales in ((w3w, w3_words, w3s, w3_scales), (w1w, w1_words, w1s, w1_scales)):
+                if e in (2, 4):
+                    load_scales(nc.sync, planes, scales, e // 2)
+                load_words(slots, words, e)
 
         gate_sb = []
         for e in range(E):
@@ -288,8 +290,8 @@ def tile_moe_shr_glu_sigmoid_kernel(
                 turn(e - 1, a_bank(2 * e))
             if e == E - 1:
                 turn(e, spare_bank)
-            if e >= 2:
-                routed_results(e - 2, e - 1)
+            if e >= 4:
+                routed_results(2 * (e - 4), 2 * (e - 3))
 
         def choice(r, block, target):
             cols = slice(block * C, (block + 1) * C)

@@ -53,8 +53,8 @@ def tile_moe_shr_glu_sigmoid_kernel(
         pos_sb = [held([P, T // LIST_ROWS], U16, f"pos{r}_sb") for r in (1, 2)]
         xw = ring(PASSES, [P, T], I32, "xw")
         xs_planes = held([P, PASSES, T], U8, "xs_planes")
-        w1s = [held([P, (hi - lo) * PASSES, H], U8, f"w1s{lo}") for lo, hi in SCALE_GROUPS]
-        w3s = [held([P, (hi - lo) * PASSES, H], U8, f"w3s{lo}") for lo, hi in SCALE_GROUPS]
+        w1s = 2 * [held([P, rows * PASSES, H], U8, f"w1s{rows}") for rows in (3, 2)]
+        w3s = 2 * [held([P, rows * PASSES, H], U8, f"w3s{rows}") for rows in (3, 2)]
         w1w = [held([P, (hi - lo) * PASSES, 2 * H], U8, f"w1w{lo}") for lo, hi in WORD_GROUPS]
         w3w = [held([P, (hi - lo) * PASSES, 2 * H], U8, f"w3w{lo}") for lo, hi in WORD_GROUPS]
         w2s = held([P, E + 1, N], U8, "w2s")
@@ -80,7 +80,7 @@ def tile_moe_shr_glu_sigmoid_kernel(
         def load_scales(queue, planes, scales, g, which=range(4)):
             lo, hi = SCALE_GROUPS[g]
             for r in which:
-                load_rows(queue, planes[g], scales[lo:hi].rearrange("e s f n -> f (e s) n"), r)
+                load_rows(queue, planes[g][:, 0 : (hi - lo) * PASSES, :], scales[lo:hi].rearrange("e s f n -> f (e s) n"), r)
 
         def load_words(slots, words, g):
             lo, hi = WORD_GROUPS[g]
@@ -215,13 +215,10 @@ def tile_moe_shr_glu_sigmoid_kernel(
             nc.scalar.copy(y_all[:, lo * C : hi * C], a_banks[1][:, 0 : (hi - lo) * C])
 
         zero(nc.gpsimd, xs_planes)
-        zero(nc.vector, w1s[0])
-        zero(nc.gpsimd, w3s[0])
-        zero(nc.vector, w3s[2])
-        zero(nc.vector, w1s[2])
+        for plane in (w1s[0], w3s[0], w3s[1], w1s[1], gs_moved):
+            zero(nc.vector, plane)
+        zero(nc.gpsimd, w2s)
         make_identity(nc, ident[:])
-        for plane in (w3s[1], w1s[1], gs_moved, w2s):
-            zero(nc.gpsimd, plane)
         token_rows = x_scales.rearrange("s f t -> f s t")
 
         def load_tokens(o):
@@ -249,17 +246,16 @@ def tile_moe_shr_glu_sigmoid_kernel(
             gather_scales(expert_plane(1, o), o, C, 2 * C)
         for pair in range(2):
             gather_scales(gs_packed[:, 2 * pair * C : 2 * (pair + 1) * C], 0, 2 * (pair + 1) * C, 2 * (pair + 2) * C)
-        for e in range(2, E + 1):
-            if e == 3:
-                move_second_planes(gs_moved, gs_packed)
-            if e == 5:
-                nc.sync.dma_start(w2w[:].bitcast(I32), w2_words.rearrange("e s p b -> p (e s) b").bitcast(I32))
-                for r in range(4):
-                    load_rows(nc.sync, w2s, w2_scales.rearrange("e s f n -> f (e s) n"), r)
+
+        def load_expert(e):
             for slots, words, planes, scales in ((w3w, w3_words, w3s, w3_scales), (w1w, w1_words, w1s, w1_scales)):
                 if e in (2, 4):
                     load_scales(nc.sync, planes, scales, e // 2)
                 load_words(slots, words, e)
+
+        load_expert(2)
+        move_second_planes(gs_moved, gs_packed)
+        load_expert(3)
 
         gate_sb = []
         for e in range(E):
@@ -281,6 +277,13 @@ def tile_moe_shr_glu_sigmoid_kernel(
             if e + 2 < E:
                 for o in range(PASSES):
                     gather_words(e + 2, o)
+            if e == 1:
+                load_expert(4)
+                nc.sync.dma_start(w2w[:].bitcast(I32), w2_words.rearrange("e s p b -> p (e s) b").bitcast(I32))
+                for r in range(4):
+                    load_rows(nc.sync, w2s, w2_scales.rearrange("e s f n -> f (e s) n"), r)
+                load_expert(5)
+                load_expert(SHARED)
             if e == 3:
                 gate_sb.append(held([P, 2, T], F32, "gate_sb"))
                 nc.sync.dma_start(gate_sb[0][:], gate.rearrange("g n t -> n g t"))

@@ -26,7 +26,7 @@ LIST_ROWS = 16
 SHARED = E
 SCALE_GROUPS = ((0, 2), (2, 4), (4, 7))
 WORD_GROUPS = tuple((e, e + 1) for e in range(E + 1))
-SHARED_UNITS = (2, 2, 1, 1)
+SHARED_UNITS = (2, 2, 2)
 
 
 def tile_moe_shr_glu_sigmoid_kernel(
@@ -161,7 +161,8 @@ def tile_moe_shr_glu_sigmoid_kernel(
                 paired(h[j % len(h)][:]), permuted(b_banks[j % len(b_banks)][:]), paired(sig_tile(j)[:]), MULT
             )
 
-        units = [(e, e * C, C // P) for e in range(E)]
+        units = [(e, e * C, C // P) for e in range(E - 1)]
+        units += [(E - 1, (E - 1) * C + part * P, 1) for part in range(C // P)]
         token = 0
         for tiles in SHARED_UNITS:
             units.append((SHARED, token, tiles))
@@ -209,10 +210,13 @@ def tile_moe_shr_glu_sigmoid_kernel(
                 stop=True,
             )
 
-        def routed_results(lo, hi):
-            for e in range(lo, hi):
-                second_layer(e, a_banks[1][:, (e - lo) * C : (e - lo + 1) * C])
-            nc.scalar.copy(y_all[:, lo * C : hi * C], a_banks[1][:, 0 : (hi - lo) * C])
+        def routed_results(first, end, bank):
+            start = units[first][1]
+            for m in range(first, end):
+                e, lo, tiles = units[m]
+                second_layer(m, bank[:, lo - start : lo - start + tiles * P])
+            width = units[end][1] - start if end <= E else S - start
+            nc.scalar.copy(y_all[:, start : start + width], bank[:, 0:width])
 
         zero(nc.gpsimd, xs_planes)
         for plane in (w1s[0], w3s[0], w3s[1], w1s[1], gs_moved):
@@ -238,8 +242,8 @@ def tile_moe_shr_glu_sigmoid_kernel(
             gather_scales(expert_plane(0, o), o, 0, C)
         nc.sync.dma_start(xs_planes[16:32, 0, :].bitcast(I32), x_scales[1].bitcast(I32))
         gather_words(0, 1)
-        load_words(w3w, w3_words, 1)
         load_words(w1w, w1_words, 1)
+        load_words(w3w, w3_words, 1)
         gather_words(1, 0)
         gather_words(1, 1)
         for o in range(PASSES):
@@ -248,17 +252,18 @@ def tile_moe_shr_glu_sigmoid_kernel(
             gather_scales(gs_packed[:, 2 * pair * C : 2 * (pair + 1) * C], 0, 2 * (pair + 1) * C, 2 * (pair + 2) * C)
 
         def load_expert(e):
-            for slots, words, planes, scales in ((w3w, w3_words, w3s, w3_scales), (w1w, w1_words, w1s, w1_scales)):
-                if e in (2, 4):
-                    load_scales(nc.sync, planes, scales, e // 2)
-                load_words(slots, words, e)
+            if e in (2, 4):
+                load_scales(nc.sync, w1s, w1_scales, e // 2)
+                load_scales(nc.sync, w3s, w3_scales, e // 2)
+            load_words(w1w, w1_words, e)
+            load_words(w3w, w3_words, e)
 
         load_expert(2)
         move_second_planes(gs_moved, gs_packed)
         load_expert(3)
 
         gate_sb = []
-        for e in range(E):
+        for e in range(E - 1):
             if e == 0:
                 for o in range(PASSES):
                     for part in range(2):
@@ -291,10 +296,8 @@ def tile_moe_shr_glu_sigmoid_kernel(
                 nc.sync.dma_start(pos_sb[1][:], pos2)
             if e >= 1:
                 turn(e - 1, a_bank(2 * e))
-            if e == E - 1:
-                turn(e, spare_bank)
-            if e >= 4:
-                routed_results(2 * (e - 4), 2 * (e - 3))
+            if e == 4:
+                routed_results(0, 2, a_banks[1])
 
         def choice(r, block, target):
             cols = slice(block * C, (block + 1) * C)
@@ -313,21 +316,27 @@ def tile_moe_shr_glu_sigmoid_kernel(
             nc.vector.tensor_tensor(result[:, cols], bank[:, 0 : tiles * P], partial[:, cols], ADD)
             nc.sync.dma_start(out[:, cols], result[:, cols])
 
+        shared = E + 1
+        tile_products(E - 1, 0)
+        routed_results(2, 4, a_banks[2])
         tile_products(E, 0)
-        routed_results(E - 2, E)
-        tile_products(E, 1)
-        tile_products(E + 1, 0)
+        turn(E - 1, spare_bank)
+        turn(E - 2, b_banks[2])
+        turn(E, b_banks[3])
+        routed_results(4, E, a_banks[1])
+        routed_results(E, E + 1, spare_bank)
+        tile_products(shared, 0)
+        tile_products(shared, 1)
+        tile_products(shared + 1, 0)
         combine(0, products0[:, 0:C], products0[:, C : 2 * C])
-        turn(E, spare_bank)
-        tile_products(E + 1, 1)
-        tile_products(E + 2, 0)
-        combine(1, sig_shared[2][:, 0:C], sig_shared[2][:, C : 2 * C])
-        finish(E, a_banks[1])
-        turn(E + 1, spare_bank)
-        tile_products(E + 3, 0)
-        finish(E + 1, b_banks[2])
-        turn(E + 2, a_banks[0])
-        turn(E + 3, spare_bank)
-        combine(2, sig_shared[4][:, 0:C], sig_shared[5][:, 0:C])
-        finish(E + 2, b_banks[3])
-        finish(E + 3, b_banks[0])
+        tile_products(shared + 1, 1)
+        turn(shared, spare_bank)
+        tile_products(shared + 2, 0)
+        tile_products(shared + 2, 1)
+        turn(shared + 1, a_banks[0])
+        turn(shared + 2, a_banks[2])
+        combine(1, sig_shared[3][:, 0:C], sig_shared[5][:, 0:C])
+        finish(shared, a_banks[1])
+        finish(shared + 1, b_banks[2])
+        combine(2, sig_shared[5][:, C : 2 * C], sig_shared[3][:, 0:C])
+        finish(shared + 2, b_banks[3])

@@ -172,6 +172,7 @@ def tile_moe_shr_glu_sigmoid_kernel(
         h_scales = ring(len(units), [P, C], U8, "h_scales")
         products0 = held([P, 2 * C], F32, "products0")
         partial = held([P, T], F32, "partial")
+        by_token = ring(1, [P, 2 * C], F32, "by_token")
         result = held([P, T], F32, "result")
 
         def tile_products(m, part):
@@ -316,6 +317,36 @@ def tile_moe_shr_glu_sigmoid_kernel(
             nc.vector.tensor_tensor(result[:, cols], bank[:, 0 : tiles * P], partial[:, cols], ADD)
             nc.sync.dma_start(out[:, cols], result[:, cols])
 
+        def added_transposes(target, terms):
+            for r, term in enumerate(terms):
+                nc.tensor.matmul(
+                    target, term, ident[:], start=(r == 0), stop=(r == len(terms) - 1), is_transpose=True
+                )
+
+        def summed_on_tensor(block, first, second, by_token_bank, result_bank):
+            m = shared + block
+            cols = slice(block * C, (block + 1) * C)
+            parts = [slice(part * P, (part + 1) * P) for part in range(C // P)]
+            for part in parts:
+                added_transposes(by_token_bank[:, part], (first[:, part], second[:, part]))
+            for part in parts:
+                nc.tensor.matmul_mx(
+                    out=by_token_bank[:, C : 2 * C][:, part],
+                    lhsT=h_codes[m][:, part].bitcast(FP8X4),
+                    lhsT_scale=h_scales[m][:, part],
+                    rhs=w2w[:, SHARED, :].bitcast(FP4X4),
+                    rhs_scale=w2s[:, SHARED, :],
+                    start=True,
+                    stop=True,
+                )
+            nc.scalar.copy(by_token[block][:], by_token_bank[:])
+            for part in parts:
+                added_transposes(
+                    result_bank[:, part], (by_token[block][:, part], by_token[block][:, C : 2 * C][:, part])
+                )
+            nc.scalar.copy(result[:, cols], result_bank[:, 0:C])
+            nc.sync.dma_start(out[:, cols], result[:, cols])
+
         shared = E + 1
         tile_products(E - 1, 0)
         routed_results(2, 4, a_banks[2])
@@ -328,15 +359,26 @@ def tile_moe_shr_glu_sigmoid_kernel(
         tile_products(shared, 0)
         tile_products(shared, 1)
         tile_products(shared + 1, 0)
-        combine(0, products0[:, 0:C], products0[:, C : 2 * C])
+
+        def freed(j):
+            return h[j % len(h)][:].bitcast(F32)
+
+        choice(0, 0, products0[:, 0:C])
+        choice(1, 0, products0[:, C : 2 * C])
         tile_products(shared + 1, 1)
         turn(shared, spare_bank)
         tile_products(shared + 2, 0)
         tile_products(shared + 2, 1)
         turn(shared + 1, a_banks[0])
+        summed_on_tensor(0, products0[:, 0:C], products0[:, C : 2 * C], spare_bank, a_banks[1])
         turn(shared + 2, a_banks[2])
-        combine(1, sig_shared[3][:, 0:C], sig_shared[5][:, 0:C])
-        finish(shared, a_banks[1])
+        combine(1, freed(12), freed(13))
         finish(shared + 1, b_banks[2])
-        combine(2, sig_shared[5][:, C : 2 * C], sig_shared[3][:, 0:C])
-        finish(shared + 2, b_banks[3])
+        cols = slice(2 * C, 3 * C)
+        both = h_turned[(shared + 2) % len(h_turned)][:, 0].rearrange("p t r -> p (t r)").bitcast(F32)
+        choice(0, 2, freed(15))
+        choice(1, 2, freed(17))
+        nc.vector.tensor_tensor(both, freed(15), freed(17), ADD)
+        second_layer(shared + 2, b_banks[3][:, 0:C])
+        nc.vector.tensor_tensor(result[:, cols], b_banks[3][:, 0:C], both, ADD)
+        nc.sync.dma_start(out[:, cols], result[:, cols])

@@ -66,8 +66,9 @@ def tile_moe_shr_glu_sigmoid_kernel(
         gs_packed = held([P, 4 * C], U8, "gs_packed")
         gs_moved = held([P, 4 * C], U8, "gs_moved")
         y_all = held([P, S], F32, "y_all")
-        sig = ring(3, [P, H], F32, "sig")
+        sig = ring(4, [P, H], F32, "sig")
         sig_shared = ring(T // P, [P, H], F32, "sig_shared")
+        b_sb = ring(2, [P, H], F32, "b_sb")
         h = ring(8, [P, H], BF16, "h")
         h_turned = ring(3, [P, 2, P, 4], BF16, "hT")
         a_banks = banks(3, "a")
@@ -156,6 +157,11 @@ def tile_moe_shr_glu_sigmoid_kernel(
         def product_b(j, e, lo, passes=(0, 1)):
             product(b_banks[j % len(b_banks)], w3w, w3s, e, lo, passes)
             if passes[-1] != PASSES - 1:
+                return
+            if j in (0, 2, 4, 6):
+                b_copy = b_sb[j // 2 % len(b_sb)]
+                nc.scalar.copy(paired(b_copy[:]), permuted(b_banks[j % len(b_banks)][:]))
+                nc.gpsimd.tensor_tensor(h[j % len(h)][:], b_copy[:], sig_tile(j)[:], MULT)
                 return
             nc.vector.tensor_tensor(
                 paired(h[j % len(h)][:]), permuted(b_banks[j % len(b_banks)][:]), paired(sig_tile(j)[:]), MULT

@@ -18,6 +18,7 @@ FP4X4 = mybir.dt.float4_e2m1fn_x4
 MULT = mybir.AluOpType.mult
 ADD = mybir.AluOpType.add
 SIGMOID = mybir.ActivationFunctionType.Sigmoid
+COPY = mybir.ActivationFunctionType.Copy
 
 P = 128
 PASSES = K // 512
@@ -26,7 +27,7 @@ LIST_ROWS = 16
 SHARED = E
 SCALE_GROUPS = ((0, 2), (2, 4), (4, 7))
 WORD_GROUPS = tuple((e, e + 1) for e in range(E + 1))
-SHARED_UNITS = (2, 2, 2)
+SHARED_UNITS = (2, 2, 1, 1)
 
 
 def tile_moe_shr_glu_sigmoid_kernel(
@@ -70,10 +71,8 @@ def tile_moe_shr_glu_sigmoid_kernel(
         sig_shared = ring(T // P, [P, H], F32, "sig_shared")
         b_sb = ring(2, [P, H], F32, "b_sb")
         h = ring(8, [P, H], BF16, "h")
-        h_turned = ring(3, [P, 2, P, 4], BF16, "hT")
-        a_banks = banks(3, "a")
-        b_banks = banks(4, "b")
-        spare_bank = psum.tile([P, H], F32, name="spare_bank")
+        h_turned = ring(4, [P, 2, P, 4], BF16, "hT")
+        bank = banks(8, "bank")
 
         def load_rows(queue, plane, rows, r):
             queue.dma_start(plane[r:P:32].bitcast(I32), rows[r:16:4].bitcast(I32))
@@ -119,18 +118,13 @@ def tile_moe_shr_glu_sigmoid_kernel(
             g = [first <= e < end for first, end in groups].index(True)
             return g, (e - groups[g][0]) * PASSES + o
 
-        def a_bank(j):
-            if j >= S // P:
-                return a_banks[2 * (j % 2)]
-            return a_banks[1] if j % 2 else a_banks[j % 4]
-
-        def product(bank, slots, planes, e, lo, passes):
+        def product(target, slots, planes, e, lo, passes):
             for o in passes:
                 g, row = place(SCALE_GROUPS, e, o)
                 gword, wrow = place(WORD_GROUPS, e, o)
                 codes, code_scales = token_operands(e, lo, o)
                 nc.tensor.matmul_mx(
-                    out=bank[:],
+                    out=target[:],
                     lhsT=codes.bitcast(FP8X4),
                     lhsT_scale=code_scales,
                     rhs=slots[gword][:, wrow, :].bitcast(FP4X4),
@@ -148,27 +142,28 @@ def tile_moe_shr_glu_sigmoid_kernel(
         def permuted(ap):
             return ap.rearrange("t (p u f) -> t u p f", u=2, f=2)
 
-        def product_a(j, e, lo, passes=(0, 1)):
-            product(a_bank(j), w1w, w1s, e, lo, passes)
-            if passes[-1] != PASSES - 1:
-                return
-            nc.scalar.activation(paired(sig_tile(j)[:]), permuted(a_bank(j)[:]), SIGMOID)
+        def tile_place(j):
+            if j < S // P:
+                return j * P // C, j * P
+            return SHARED, j * P - S
 
-        def product_b(j, e, lo, passes=(0, 1)):
-            product(b_banks[j % len(b_banks)], w3w, w3s, e, lo, passes)
+        def product_a(j, target, passes=(0, 1)):
+            product(target, w1w, w1s, *tile_place(j), passes)
+            if passes[-1] == PASSES - 1:
+                nc.scalar.activation(paired(sig_tile(j)[:]), permuted(target[:]), SIGMOID)
+
+        def product_b(j, target, passes=(0, 1)):
+            product(target, w3w, w3s, *tile_place(j), passes)
             if passes[-1] != PASSES - 1:
                 return
             if j in (0, 2, 4, 6):
                 b_copy = b_sb[j // 2 % len(b_sb)]
-                nc.scalar.copy(paired(b_copy[:]), permuted(b_banks[j % len(b_banks)][:]))
+                nc.scalar.copy(paired(b_copy[:]), permuted(target[:]))
                 nc.gpsimd.tensor_tensor(h[j % len(h)][:], b_copy[:], sig_tile(j)[:], MULT)
                 return
-            nc.vector.tensor_tensor(
-                paired(h[j % len(h)][:]), permuted(b_banks[j % len(b_banks)][:]), paired(sig_tile(j)[:]), MULT
-            )
+            nc.vector.tensor_tensor(paired(h[j % len(h)][:]), permuted(target[:]), paired(sig_tile(j)[:]), MULT)
 
-        units = [(e, e * C, C // P) for e in range(E - 1)]
-        units += [(E - 1, (E - 1) * C + part * P, 1) for part in range(C // P)]
+        units = [(e, e * C, C // P) for e in range(E)]
         token = 0
         for tiles in SHARED_UNITS:
             units.append((SHARED, token, tiles))
@@ -176,33 +171,29 @@ def tile_moe_shr_glu_sigmoid_kernel(
         first_tile = [sum(unit[2] for unit in units[:m]) for m in range(len(units))]
         h_codes = ring(len(units), [P, C], U32, "h_codes")
         h_scales = ring(len(units), [P, C], U8, "h_scales")
-        products0 = held([P, 2 * C], F32, "products0")
+        second_choice = ring(2, [P, C], F32, "second_choice")
         partial = held([P, T], F32, "partial")
-        by_token = ring(1, [P, 2 * C], F32, "by_token")
         result = held([P, T], F32, "result")
 
-        def tile_products(m, part):
-            e, lo, tiles = units[m]
-            product_a(first_tile[m] + part, e, lo + part * P)
-            product_b(first_tile[m] + part, e, lo + part * P)
-
-        def turn(m, bank):
+        def turn(m, target):
             tiles = units[m][2]
             for part in range(tiles):
                 pairs = h[(first_tile[m] + part) % len(h)][:].bitcast(F32)
                 for u in range(2):
                     nc.tensor.transpose(
-                        bank[:, (2 * part + u) * P : (2 * part + u + 1) * P], pairs[:, u * P : (u + 1) * P], ident[:]
+                        target[:, (2 * part + u) * P : (2 * part + u + 1) * P], pairs[:, u * P : (u + 1) * P], ident[:]
                     )
-            turned = h_turned[m % len(h_turned)]
             nc.scalar.copy(
-                turned[:, 0:tiles].bitcast(F32),
-                bank[:, 0 : 2 * tiles * P].rearrange("p (j u t) -> p j t u", u=2, t=P),
+                h_turned[m % len(h_turned)][:, 0:tiles].bitcast(F32),
+                target[:, 0 : 2 * tiles * P].rearrange("p (j u t) -> p j t u", u=2, t=P),
             )
+
+        def quantise(m):
+            tiles = units[m][2]
             nc.vector.quantize_mx(
                 out=h_codes[m][:, 0 : tiles * P].bitcast(FP8X4),
                 scales=h_scales[m][:, 0 : tiles * P],
-                in_=turned[:, 0:tiles].rearrange("p j t r -> p (j t r)"),
+                in_=h_turned[m % len(h_turned)][:, 0:tiles].rearrange("p j t r -> p (j t r)"),
             )
 
         def second_layer(m, target):
@@ -217,13 +208,10 @@ def tile_moe_shr_glu_sigmoid_kernel(
                 stop=True,
             )
 
-        def routed_results(first, end, bank):
-            start = units[first][1]
+        def routed_results(first, end, target, copy):
             for m in range(first, end):
-                e, lo, tiles = units[m]
-                second_layer(m, bank[:, lo - start : lo - start + tiles * P])
-            width = units[end][1] - start if end <= E else S - start
-            nc.scalar.copy(y_all[:, start : start + width], bank[:, 0:width])
+                second_layer(m, target[:, (m - first) * C : (m - first + 1) * C])
+            copy(y_all[:, first * C : end * C], target[:, 0 : (end - first) * C])
 
         zero(nc.gpsimd, xs_planes)
         for plane in (w1s[0], w3s[0], w3s[1], w1s[1], gs_moved):
@@ -269,122 +257,110 @@ def tile_moe_shr_glu_sigmoid_kernel(
         move_second_planes(gs_moved, gs_packed)
         load_expert(3)
 
-        gate_sb = []
+        gate_sb = held([P, 2, T], F32, "gate_sb")
         for e in range(E - 1):
+            a_banks = bank[2 * (e % 2) : 2 * (e % 2) + 2]
+            b_banks = bank[4 + 2 * (e % 2) : 6 + 2 * (e % 2)]
             if e == 0:
                 for o in range(PASSES):
                     for part in range(2):
-                        product_a(part, 0, part * P, (o,))
+                        product_a(part, a_banks[part], (o,))
                 for o in range(PASSES):
                     for part in range(2):
-                        product_b(part, 0, part * P, (o,))
+                        product_b(part, b_banks[part], (o,))
             elif e == 2:
                 for o in range(PASSES):
                     for part in range(2):
-                        product_a(4 + part, 2, 2 * C + part * P, (o,))
-                        product_b(4 + part, 2, 2 * C + part * P, (o,))
+                        product_a(4 + part, a_banks[part], (o,))
+                        product_b(4 + part, b_banks[part], (o,))
             else:
                 for part in range(2):
-                    tile_products(e, part)
+                    product_a(2 * e + part, a_banks[part])
+                for part in range(2):
+                    product_b(2 * e + part, b_banks[part])
             if e + 2 < E:
                 for o in range(PASSES):
                     gather_words(e + 2, o)
             if e == 1:
                 load_expert(4)
+                load_expert(5)
                 nc.sync.dma_start(w2w[:].bitcast(I32), w2_words.rearrange("e s p b -> p (e s) b").bitcast(I32))
                 for r in range(4):
                     load_rows(nc.sync, w2s, w2_scales.rearrange("e s f n -> f (e s) n"), r)
-                load_expert(5)
                 load_expert(SHARED)
-            if e == 3:
-                gate_sb.append(held([P, 2, T], F32, "gate_sb"))
-                nc.sync.dma_start(gate_sb[0][:], gate.rearrange("g n t -> n g t"))
-                nc.sync.dma_start(pos_sb[0][:], pos1)
+                nc.sync.dma_start(gate_sb[:], gate.rearrange("g n t -> n g t"))
                 nc.sync.dma_start(pos_sb[1][:], pos2)
-            if e >= 1:
-                turn(e - 1, a_bank(2 * e))
-            if e == 4:
-                routed_results(0, 2, a_banks[1])
+                nc.sync.dma_start(pos_sb[0][:], pos1)
+            if e in (2, 4):
+                for part in range(2):
+                    turn(e - 2 + part, a_banks[part])
+                for part in range(2):
+                    quantise(e - 2 + part)
 
-        def choice(r, block, target):
-            cols = slice(block * C, (block + 1) * C)
-            offsets = pos_sb[r][:, block * C // LIST_ROWS : (block + 1) * C // LIST_ROWS]
-            nc.vector.tensor_tensor(target, y_all[:].indirect(offsets), gate_sb[0][:, r, cols], MULT)
+        def block_cols(block):
+            return slice(block * C, (block + 1) * C)
 
-        def combine(block, first, second):
-            choice(0, block, first)
-            choice(1, block, second)
-            nc.vector.tensor_tensor(partial[:, block * C : (block + 1) * C], first, second, ADD)
+        def choice(r, block):
+            return y_all[:].indirect(pos_sb[r][:, block * C // LIST_ROWS : (block + 1) * C // LIST_ROWS])
 
-        def finish(m, bank):
+        def fetch_second(block, target):
+            nc.scalar.activation(target, choice(1, block), COPY)
+
+        def gated_first(block, target):
+            nc.vector.tensor_tensor(target, choice(0, block), gate_sb[:, 0, block_cols(block)], MULT)
+
+        def add_second(block, first, fetched, target):
+            nc.vector.tensor_tensor(target, fetched, gate_sb[:, 1, block_cols(block)], MULT)
+            nc.vector.tensor_tensor(partial[:, block_cols(block)], first, target, ADD)
+
+        def finish(m, source):
             e, lo, tiles = units[m]
             cols = slice(lo, lo + tiles * P)
-            second_layer(m, bank[:, 0 : tiles * P])
-            nc.vector.tensor_tensor(result[:, cols], bank[:, 0 : tiles * P], partial[:, cols], ADD)
+            nc.vector.tensor_tensor(result[:, cols], source, partial[:, cols], ADD)
             nc.sync.dma_start(out[:, cols], result[:, cols])
 
-        def added_transposes(target, terms):
-            for r, term in enumerate(terms):
-                nc.tensor.matmul(
-                    target, term, ident[:], start=(r == 0), stop=(r == len(terms) - 1), is_transpose=True
-                )
-
-        def summed_on_tensor(block, first, second, by_token_bank, result_bank):
-            m = shared + block
-            cols = slice(block * C, (block + 1) * C)
-            parts = [slice(part * P, (part + 1) * P) for part in range(C // P)]
-            for part in parts:
-                added_transposes(by_token_bank[:, part], (first[:, part], second[:, part]))
-            for part in parts:
-                nc.tensor.matmul_mx(
-                    out=by_token_bank[:, C : 2 * C][:, part],
-                    lhsT=h_codes[m][:, part].bitcast(FP8X4),
-                    lhsT_scale=h_scales[m][:, part],
-                    rhs=w2w[:, SHARED, :].bitcast(FP4X4),
-                    rhs_scale=w2s[:, SHARED, :],
-                    start=True,
-                    stop=True,
-                )
-            nc.scalar.copy(by_token[block][:], by_token_bank[:])
-            for part in parts:
-                added_transposes(
-                    result_bank[:, part], (by_token[block][:, part], by_token[block][:, C : 2 * C][:, part])
-                )
-            nc.scalar.copy(result[:, cols], result_bank[:, 0:C])
-            nc.sync.dma_start(out[:, cols], result[:, cols])
-
-        shared = E + 1
-        tile_products(E - 1, 0)
-        routed_results(2, 4, a_banks[2])
-        tile_products(E, 0)
-        turn(E - 1, spare_bank)
-        turn(E - 2, b_banks[2])
-        turn(E, b_banks[3])
-        routed_results(4, E, a_banks[1])
-        routed_results(E, E + 1, spare_bank)
-        tile_products(shared, 0)
-        tile_products(shared, 1)
-        tile_products(shared + 1, 0)
-
-        def freed(j):
-            return h[j % len(h)][:].bitcast(F32)
-
-        choice(0, 0, products0[:, 0:C])
-        choice(1, 0, products0[:, C : 2 * C])
-        tile_products(shared + 1, 1)
-        turn(shared, spare_bank)
-        tile_products(shared + 2, 0)
-        tile_products(shared + 2, 1)
-        turn(shared + 1, a_banks[0])
-        summed_on_tensor(0, products0[:, 0:C], products0[:, C : 2 * C], spare_bank, a_banks[1])
-        turn(shared + 2, a_banks[2])
-        combine(1, freed(12), freed(13))
-        finish(shared + 1, b_banks[2])
-        cols = slice(2 * C, 3 * C)
-        both = h_turned[(shared + 2) % len(h_turned)][:, 0].rearrange("p t r -> p (t r)").bitcast(F32)
-        choice(0, 2, freed(15))
-        choice(1, 2, freed(17))
-        nc.vector.tensor_tensor(both, freed(15), freed(17), ADD)
-        second_layer(shared + 2, b_banks[3][:, 0:C])
-        nc.vector.tensor_tensor(result[:, cols], b_banks[3][:, 0:C], both, ADD)
-        nc.sync.dma_start(out[:, cols], result[:, cols])
+        product_a(10, bank[2])
+        product_a(11, bank[3])
+        turn(4, bank[6])
+        product_b(10, bank[7])
+        quantise(4)
+        routed_results(0, 2, bank[4], nc.scalar.copy)
+        product_b(11, bank[5])
+        routed_results(2, 4, bank[2], nc.vector.tensor_copy)
+        product_a(12, bank[0])
+        routed_results(4, 5, bank[1], nc.vector.tensor_copy)
+        turn(5, bank[3])
+        quantise(5)
+        product_a(13, bank[7])
+        product_b(12, bank[6])
+        routed_results(5, 6, bank[1], nc.vector.tensor_copy)
+        product_b(13, bank[4])
+        for block in range(2):
+            fetch_second(block, second_choice[block][:])
+        gated_first(0, sig_tile(13)[:, 0:C])
+        add_second(0, sig_tile(13)[:, 0:C], second_choice[0][:], sig_tile(13)[:, C : 2 * C])
+        product_a(14, bank[2])
+        product_a(15, bank[0])
+        product_b(14, bank[5])
+        product_b(15, bank[3])
+        fetch_second(2, sig_tile(14)[:, 0:C])
+        gated_first(1, sig_tile(15)[:, 0:C])
+        add_second(1, sig_tile(15)[:, 0:C], second_choice[1][:], sig_tile(15)[:, C : 2 * C])
+        product_a(16, bank[7])
+        product_a(17, bank[1])
+        turn(6, bank[2])
+        turn(7, bank[0])
+        last_first = h[12 % len(h)][:].bitcast(F32)
+        gated_first(2, last_first)
+        product_b(16, bank[6])
+        product_b(17, bank[4])
+        quantise(6)
+        quantise(7)
+        turn(8, bank[7])
+        turn(9, bank[1])
+        quantise(8)
+        quantise(9)
+        add_second(2, last_first, sig_tile(14)[:, 0:C], sig_tile(17)[:, 0:C])
+        for m, target in ((6, bank[5][:, 0:C]), (7, bank[3][:, 0:C]), (8, bank[2][:, 0:P]), (9, bank[0][:, 0:P])):
+            second_layer(m, target)
+            finish(m, target)

@@ -25,9 +25,15 @@ PASSES = K // 512
 QUADRANTS = 4
 LIST_ROWS = 16
 SHARED = E
-SCALE_GROUPS = ((0, 2), (2, 4), (4, 7))
+SCALE_GROUPS = ((4, 7), (2, 4), (0, 2))
 WORD_GROUPS = tuple((e, e + 1) for e in range(E + 1))
-SHARED_UNITS = (2, 2, 1, 1)
+UNITS = (
+    ((SHARED, 0, 2),)
+    + tuple((e, e * C, 2) for e in reversed(range(E)))
+    + ((SHARED, C, 2), (SHARED, 2 * C, 1), (SHARED, 2 * C + P, 1))
+)
+POOL_TILES = (0, 1, 2, 4, 6, 8)
+TILES = tuple((e, lo + part * P) for e, lo, tiles in UNITS for part in range(tiles))
 
 
 def tile_moe_shr_glu_sigmoid_kernel(
@@ -62,13 +68,12 @@ def tile_moe_shr_glu_sigmoid_kernel(
         w2w = held([P, E + 1, 2 * N], U8, "w2w")
         ident = held([P, P], F32, "ident")
         gw = ring(2, [P, PASSES, C], U32, "gw")
-        gs_direct = ring(3, [P, C], U8, "gs_direct")
-        gs_one = held([P, C], U8, "gs_one")
+        gs_last = ring(PASSES, [P, 2 * C], U8, "gs_last")
         gs_packed = held([P, 4 * C], U8, "gs_packed")
         gs_moved = held([P, 4 * C], U8, "gs_moved")
         y_all = held([P, S], F32, "y_all")
         sig = ring(4, [P, H], F32, "sig")
-        sig_shared = ring(T // P, [P, H], F32, "sig_shared")
+        sig_end = ring(4, [P, H], F32, "sig_end")
         b_sb = ring(2, [P, H], F32, "b_sb")
         h = ring(8, [P, H], BF16, "h")
         h_turned = ring(4, [P, 2, P, 4], BF16, "hT")
@@ -102,11 +107,9 @@ def tile_moe_shr_glu_sigmoid_kernel(
                 nc.sync.dma_start(target[r:P:32].bitcast(I32), gathered[16 + r : 32 : 4].bitcast(I32))
 
         def expert_plane(e, o):
-            if e == 0:
-                return gs_direct[o][:]
-            if e == 1:
-                return (gs_one, gs_direct[2])[o][:]
-            return (gs_packed, gs_moved)[o][:, (e - 2) * C : (e - 1) * C]
+            if e >= 4:
+                return gs_last[o][:, (e - 4) * C : (e - 3) * C]
+            return (gs_moved, gs_packed)[o][:, e * C : (e + 1) * C]
 
         def token_operands(e, lo, o):
             if e == SHARED:
@@ -134,7 +137,7 @@ def tile_moe_shr_glu_sigmoid_kernel(
                 )
 
         def sig_tile(j):
-            return sig[j % len(sig)] if j < S // P else sig_shared[j - S // P]
+            return sig[j % len(sig)] if j < 14 else sig_end[j - 14]
 
         def paired(ap):
             return ap.rearrange("t (u p f) -> t u p f", u=2, f=2)
@@ -142,40 +145,31 @@ def tile_moe_shr_glu_sigmoid_kernel(
         def permuted(ap):
             return ap.rearrange("t (p u f) -> t u p f", u=2, f=2)
 
-        def tile_place(j):
-            if j < S // P:
-                return j * P // C, j * P
-            return SHARED, j * P - S
-
         def product_a(j, target, passes=(0, 1)):
-            product(target, w1w, w1s, *tile_place(j), passes)
+            product(target, w1w, w1s, *TILES[j], passes)
             if passes[-1] == PASSES - 1:
                 nc.scalar.activation(paired(sig_tile(j)[:]), permuted(target[:]), SIGMOID)
 
         def product_b(j, target, passes=(0, 1)):
-            product(target, w3w, w3s, *tile_place(j), passes)
+            product(target, w3w, w3s, *TILES[j], passes)
             if passes[-1] != PASSES - 1:
                 return
-            if j in (0, 2, 4, 6):
-                b_copy = b_sb[j // 2 % len(b_sb)]
+            if j in POOL_TILES:
+                b_copy = b_sb[POOL_TILES.index(j) % len(b_sb)]
                 nc.scalar.copy(paired(b_copy[:]), permuted(target[:]))
                 nc.gpsimd.tensor_tensor(h[j % len(h)][:], b_copy[:], sig_tile(j)[:], MULT)
                 return
             nc.vector.tensor_tensor(paired(h[j % len(h)][:]), permuted(target[:]), paired(sig_tile(j)[:]), MULT)
 
-        units = [(e, e * C, C // P) for e in range(E)]
-        token = 0
-        for tiles in SHARED_UNITS:
-            units.append((SHARED, token, tiles))
-            token += tiles * P
+        units = UNITS
         first_tile = [sum(unit[2] for unit in units[:m]) for m in range(len(units))]
         h_codes = ring(len(units), [P, C], U32, "h_codes")
         h_scales = ring(len(units), [P, C], U8, "h_scales")
-        second_choice = ring(2, [P, C], F32, "second_choice")
+        fetched = ring(2, [P, 2, C], F32, "fetched")
         partial = held([P, T], F32, "partial")
         result = held([P, T], F32, "result")
 
-        def turn(m, target):
+        def turn(m, target, copy=nc.scalar.copy):
             tiles = units[m][2]
             for part in range(tiles):
                 pairs = h[(first_tile[m] + part) % len(h)][:].bitcast(F32)
@@ -183,7 +177,7 @@ def tile_moe_shr_glu_sigmoid_kernel(
                     nc.tensor.transpose(
                         target[:, (2 * part + u) * P : (2 * part + u + 1) * P], pairs[:, u * P : (u + 1) * P], ident[:]
                     )
-            nc.scalar.copy(
+            copy(
                 h_turned[m % len(h_turned)][:, 0:tiles].bitcast(F32),
                 target[:, 0 : 2 * tiles * P].rearrange("p (j u t) -> p j t u", u=2, t=P),
             )
@@ -208,94 +202,94 @@ def tile_moe_shr_glu_sigmoid_kernel(
                 stop=True,
             )
 
-        def routed_results(first, end, target, copy):
-            for m in range(first, end):
-                second_layer(m, target[:, (m - first) * C : (m - first + 1) * C])
-            copy(y_all[:, first * C : end * C], target[:, 0 : (end - first) * C])
+        def routed_results(members, target, copy):
+            start = min(units[m][1] for m in members)
+            for m in members:
+                e, lo, tiles = units[m]
+                second_layer(m, target[:, lo - start : lo - start + tiles * P])
+            width = sum(units[m][2] for m in members) * P
+            copy(y_all[:, start : start + width], target[:, 0:width])
 
         zero(nc.gpsimd, xs_planes)
         for plane in (w1s[0], w3s[0], w3s[1], w1s[1], gs_moved):
             zero(nc.vector, plane)
-        zero(nc.gpsimd, w2s)
-        make_identity(nc, ident[:])
+        zero(nc.vector, w2s)
+        nc.vector.memset(ident[:], 0.0)
+        make_identity(nc, ident[:], nomemset=True)
         token_rows = x_scales.rearrange("s f t -> f s t")
 
         def load_tokens(o):
             nc.sync.dma_start(xw[o][:], x_words[o].rearrange("p t r -> p (t r)").bitcast(I32))
 
+        def load_expert(e):
+            load_words(w1w, w1_words, e)
+            load_words(w3w, w3_words, e)
+
+        def load_group(g):
+            load_scales(nc.sync, w1s, w1_scales, g)
+            load_scales(nc.sync, w3s, w3_scales, g)
+
         nc.sync.dma_start(offs_sb[:], offs)
         load_tokens(0)
         for r in range(4):
             load_rows(nc.sync, xs_planes, token_rows, r)
-        load_words(w1w, w1_words, 0)
+        load_words(w1w, w1_words, SHARED)
         load_scales(nc.sync, w1s, w1_scales, 0)
         load_tokens(1)
-        load_words(w3w, w3_words, 0)
+        nc.sync.dma_start(xs_planes[16:32, 1, :].bitcast(I32), x_scales[0].bitcast(I32))
+        load_words(w3w, w3_words, SHARED)
         load_scales(nc.sync, w3s, w3_scales, 0)
-        gather_words(0, 0)
-        for o in range(PASSES):
-            gather_scales(expert_plane(0, o), o, 0, C)
-        nc.sync.dma_start(xs_planes[16:32, 0, :].bitcast(I32), x_scales[1].bitcast(I32))
-        gather_words(0, 1)
-        load_words(w1w, w1_words, 1)
-        load_words(w3w, w3_words, 1)
-        gather_words(1, 0)
-        gather_words(1, 1)
-        for o in range(PASSES):
-            gather_scales(expert_plane(1, o), o, C, 2 * C)
-        for pair in range(2):
-            gather_scales(gs_packed[:, 2 * pair * C : 2 * (pair + 1) * C], 0, 2 * (pair + 1) * C, 2 * (pair + 2) * C)
-
-        def load_expert(e):
-            if e in (2, 4):
-                load_scales(nc.sync, w1s, w1_scales, e // 2)
-                load_scales(nc.sync, w3s, w3_scales, e // 2)
-            load_words(w1w, w1_words, e)
-            load_words(w3w, w3_words, e)
-
-        load_expert(2)
-        move_second_planes(gs_moved, gs_packed)
+        load_expert(5)
+        load_expert(4)
+        gather_words(5, 0)
+        gather_scales(gs_last[0][:], 0, 4 * C, 6 * C)
+        gather_words(4, 0)
+        gather_words(5, 1)
+        gather_scales(gs_last[1][:], 1, 4 * C, 6 * C)
+        gather_words(4, 1)
+        for lo in (2 * C, 0):
+            gather_scales(gs_packed[:, lo : lo + 2 * C], 1, lo, lo + 2 * C)
+        load_group(1)
         load_expert(3)
+        move_second_planes(gs_moved, gs_packed)
+        load_expert(2)
+        nc.sync.dma_start(w2w[:].bitcast(I32), w2_words.rearrange("e s p b -> p (e s) b").bitcast(I32))
+        for r in range(4):
+            load_rows(nc.sync, w2s, w2_scales.rearrange("e s f n -> f (e s) n"), r)
 
         gate_sb = held([P, 2, T], F32, "gate_sb")
-        for e in range(E - 1):
-            a_banks = bank[2 * (e % 2) : 2 * (e % 2) + 2]
-            b_banks = bank[4 + 2 * (e % 2) : 6 + 2 * (e % 2)]
-            if e == 0:
+        for m in range(E):
+            a_banks = bank[2 * (m % 2) : 2 * (m % 2) + 2]
+            b_banks = bank[4 + 2 * (m % 2) : 6 + 2 * (m % 2)]
+            if m == 0:
                 for o in range(PASSES):
                     for part in range(2):
                         product_a(part, a_banks[part], (o,))
                 for o in range(PASSES):
                     for part in range(2):
                         product_b(part, b_banks[part], (o,))
-            elif e == 2:
-                for o in range(PASSES):
-                    for part in range(2):
-                        product_a(4 + part, a_banks[part], (o,))
-                        product_b(4 + part, b_banks[part], (o,))
             else:
                 for part in range(2):
-                    product_a(2 * e + part, a_banks[part])
+                    product_a(2 * m + part, a_banks[part])
                 for part in range(2):
-                    product_b(2 * e + part, b_banks[part])
-            if e + 2 < E:
+                    product_b(2 * m + part, b_banks[part])
+            if 1 <= m <= E - 2:
                 for o in range(PASSES):
-                    gather_words(e + 2, o)
-            if e == 1:
-                load_expert(4)
-                load_expert(5)
-                nc.sync.dma_start(w2w[:].bitcast(I32), w2_words.rearrange("e s p b -> p (e s) b").bitcast(I32))
-                for r in range(4):
-                    load_rows(nc.sync, w2s, w2_scales.rearrange("e s f n -> f (e s) n"), r)
-                load_expert(SHARED)
-                nc.sync.dma_start(gate_sb[:], gate.rearrange("g n t -> n g t"))
+                    gather_words(units[m + 2][0], o)
+            if m == 2:
+                load_group(2)
+                load_expert(1)
+                load_expert(0)
                 nc.sync.dma_start(pos_sb[1][:], pos2)
                 nc.sync.dma_start(pos_sb[0][:], pos1)
-            if e in (2, 4):
+                nc.sync.dma_start(gate_sb[:], gate.rearrange("g n t -> n g t"))
+            if m in (2, 4):
                 for part in range(2):
-                    turn(e - 2 + part, a_banks[part])
+                    turn(m - 2 + part, a_banks[part])
                 for part in range(2):
-                    quantise(e - 2 + part)
+                    quantise(m - 2 + part)
+            if m == 4:
+                routed_results((1,), bank[4], nc.vector.tensor_copy)
 
         def block_cols(block):
             return slice(block * C, (block + 1) * C)
@@ -303,15 +297,17 @@ def tile_moe_shr_glu_sigmoid_kernel(
         def choice(r, block):
             return y_all[:].indirect(pos_sb[r][:, block * C // LIST_ROWS : (block + 1) * C // LIST_ROWS])
 
-        def fetch_second(block, target):
-            nc.scalar.activation(target, choice(1, block), COPY)
+        def fetch(r, block, target):
+            nc.scalar.activation(target, choice(r, block), COPY)
 
-        def gated_first(block, target):
-            nc.vector.tensor_tensor(target, choice(0, block), gate_sb[:, 0, block_cols(block)], MULT)
+        def combine_fetched(engine, block, pair, weighted):
+            engine.tensor_tensor(weighted, pair, gate_sb[:, :, block_cols(block)], MULT)
+            engine.tensor_tensor(partial[:, block_cols(block)], weighted[:, 0, :], weighted[:, 1, :], ADD)
 
-        def add_second(block, first, fetched, target):
-            nc.vector.tensor_tensor(target, fetched, gate_sb[:, 1, block_cols(block)], MULT)
-            nc.vector.tensor_tensor(partial[:, block_cols(block)], first, target, ADD)
+        def combine(block, first, second):
+            for r, target in enumerate((first, second)):
+                nc.vector.tensor_tensor(target, choice(r, block), gate_sb[:, r, block_cols(block)], MULT)
+            nc.vector.tensor_tensor(partial[:, block_cols(block)], first, second, ADD)
 
         def finish(m, source):
             e, lo, tiles = units[m]
@@ -319,48 +315,51 @@ def tile_moe_shr_glu_sigmoid_kernel(
             nc.vector.tensor_tensor(result[:, cols], source, partial[:, cols], ADD)
             nc.sync.dma_start(out[:, cols], result[:, cols])
 
-        product_a(10, bank[2])
-        product_a(11, bank[3])
-        turn(4, bank[6])
-        product_b(10, bank[7])
-        quantise(4)
-        routed_results(0, 2, bank[4], nc.scalar.copy)
-        product_b(11, bank[5])
-        routed_results(2, 4, bank[2], nc.vector.tensor_copy)
+        def freed(j):
+            return h[j % len(h)][:].bitcast(F32)
+
+        def halves(j):
+            return sig_tile(j)[:, 0:C], sig_tile(j)[:, C : 2 * C]
+
+        def both(j):
+            return sig_tile(j)[:].rearrange("p (r c) -> p r c", r=2)
+
+        routed_results((2, 3), bank[2], nc.vector.tensor_copy)
         product_a(12, bank[0])
-        routed_results(4, 5, bank[1], nc.vector.tensor_copy)
-        turn(5, bank[3])
-        quantise(5)
-        product_a(13, bank[7])
-        product_b(12, bank[6])
-        routed_results(5, 6, bank[1], nc.vector.tensor_copy)
-        product_b(13, bank[4])
-        for block in range(2):
-            fetch_second(block, second_choice[block][:])
-        gated_first(0, sig_tile(13)[:, 0:C])
-        add_second(0, sig_tile(13)[:, 0:C], second_choice[0][:], sig_tile(13)[:, C : 2 * C])
-        product_a(14, bank[2])
-        product_a(15, bank[0])
-        product_b(14, bank[5])
-        product_b(15, bank[3])
-        fetch_second(2, sig_tile(14)[:, 0:C])
-        gated_first(1, sig_tile(15)[:, 0:C])
-        add_second(1, sig_tile(15)[:, 0:C], second_choice[1][:], sig_tile(15)[:, C : 2 * C])
-        product_a(16, bank[7])
-        product_a(17, bank[1])
-        turn(6, bank[2])
-        turn(7, bank[0])
-        last_first = h[12 % len(h)][:].bitcast(F32)
-        gated_first(2, last_first)
-        product_b(16, bank[6])
-        product_b(17, bank[4])
-        quantise(6)
-        quantise(7)
+        product_b(12, bank[4])
+        product_a(13, bank[1])
+        product_b(13, bank[5])
+        turn(4, bank[6])
+        turn(5, bank[3], nc.vector.tensor_copy)
+        turn(6, bank[0])
+        for m in (4, 5, 6):
+            quantise(m)
+        routed_results((4, 5), bank[2], nc.scalar.copy)
+        routed_results((6,), bank[4], nc.vector.tensor_copy)
+        product_a(14, bank[5])
+        product_b(14, bank[6])
+        product_a(15, bank[3])
+        product_b(15, bank[0])
+        for r in range(2):
+            fetch(r, 0, fetched[0][:, r, :])
+        fetch(1, 1, fetched[1][:, 0, :])
+        combine(2, *halves(13))
+        first, second = halves(15)
+        nc.vector.tensor_tensor(first, choice(0, 1), gate_sb[:, 0, block_cols(1)], MULT)
+        product_a(16, bank[5])
+        product_b(16, bank[2])
+        product_a(17, bank[4])
+        product_b(17, bank[6])
+        combine_fetched(nc.vector, 0, fetched[0][:], both(17))
+        turn(7, bank[1])
         turn(8, bank[7])
-        turn(9, bank[1])
-        quantise(8)
-        quantise(9)
-        add_second(2, last_first, sig_tile(14)[:, 0:C], sig_tile(17)[:, 0:C])
-        for m, target in ((6, bank[5][:, 0:C]), (7, bank[3][:, 0:C]), (8, bank[2][:, 0:P]), (9, bank[0][:, 0:P])):
+        turn(9, bank[3])
+        second_layer(0, bank[5][:, 0:C])
+        for m in (7, 8, 9):
+            quantise(m)
+        nc.vector.tensor_tensor(second, fetched[1][:, 0, :], gate_sb[:, 1, block_cols(1)], MULT)
+        nc.vector.tensor_tensor(partial[:, block_cols(1)], first, second, ADD)
+        finish(0, bank[5][:, 0:C])
+        for m, target in ((8, bank[0][:, 0:P]), (9, bank[2][:, 0:P]), (7, bank[4][:, 0:C])):
             second_layer(m, target)
             finish(m, target)

@@ -32,7 +32,7 @@ UNITS = (
     + tuple((e, e * C, 2) for e in reversed(range(E)))
     + ((SHARED, C, 2), (SHARED, 2 * C, 1), (SHARED, 2 * C + P, 1))
 )
-POOL_TILES = (0, 1, 2, 4, 6, 8)
+POOL_TILES = (0, 2, 4, 6)
 TILES = tuple((e, lo + part * P) for e, lo, tiles in UNITS for part in range(tiles))
 
 

@@ -166,6 +166,8 @@ def tile_moe_shr_glu_sigmoid_kernel(
         h_codes = ring(len(units), [P, C], U32, "h_codes")
         h_scales = ring(len(units), [P, C], U8, "h_scales")
         fetched = ring(2, [P, 2, C], F32, "fetched")
+        first_ys = held([P, C], F32, "first_ys")
+        by_token = ring(2, [P, 2 * C], F32, "by_token")
         partial = held([P, T], F32, "partial")
         result = held([P, T], F32, "result")
 
@@ -290,6 +292,8 @@ def tile_moe_shr_glu_sigmoid_kernel(
                     quantise(m - 2 + part)
             if m == 4:
                 routed_results((1,), bank[4], nc.vector.tensor_copy)
+                second_layer(0, bank[7][:, 0:C])
+                nc.scalar.copy(first_ys[:], bank[7][:, 0:C])
 
         def block_cols(block):
             return slice(block * C, (block + 1) * C)
@@ -313,7 +317,8 @@ def tile_moe_shr_glu_sigmoid_kernel(
             e, lo, tiles = units[m]
             cols = slice(lo, lo + tiles * P)
             nc.vector.tensor_tensor(result[:, cols], source, partial[:, cols], ADD)
-            nc.sync.dma_start(out[:, cols], result[:, cols])
+            if cols.stop % C == 0:
+                nc.sync.dma_start(out[:, cols.stop - C : cols.stop], result[:, cols.stop - C : cols.stop])
 
         def freed(j):
             return h[j % len(h)][:].bitcast(F32)
@@ -321,45 +326,63 @@ def tile_moe_shr_glu_sigmoid_kernel(
         def halves(j):
             return sig_tile(j)[:, 0:C], sig_tile(j)[:, C : 2 * C]
 
-        def both(j):
-            return sig_tile(j)[:].rearrange("p (r c) -> p r c", r=2)
+        def added_transposes(target, terms):
+            for part in range(C // P):
+                cols = slice(part * P, (part + 1) * P)
+                for r, term in enumerate(terms):
+                    nc.tensor.matmul(
+                        target[:, cols], term[:, cols], ident[:], start=(r == 0), stop=(r == len(terms) - 1), is_transpose=True
+                    )
+
+        def weigh(block, targets):
+            for r in range(2):
+                nc.vector.tensor_tensor(targets[r], choice(r, block), gate_sb[:, r, block_cols(block)], MULT)
+
+        def store_summed(block, terms, target):
+            added_transposes(target, terms)
+            nc.scalar.copy(result[:, block_cols(block)], target[:, 0:C])
+            nc.sync.dma_start(out[:, block_cols(block)], result[:, block_cols(block)])
 
         routed_results((2, 3), bank[2], nc.vector.tensor_copy)
         product_a(12, bank[0])
         product_b(12, bank[4])
         product_a(13, bank[1])
         product_b(13, bank[5])
+        product_a(14, bank[0])
         turn(4, bank[6])
         turn(5, bank[3], nc.vector.tensor_copy)
-        turn(6, bank[0])
+        turn(6, bank[1])
         for m in (4, 5, 6):
             quantise(m)
         routed_results((4, 5), bank[2], nc.scalar.copy)
         routed_results((6,), bank[4], nc.vector.tensor_copy)
-        product_a(14, bank[5])
+        product_a(15, bank[5])
+        product_a(16, bank[0])
         product_b(14, bank[6])
-        product_a(15, bank[3])
-        product_b(15, bank[0])
+        product_b(15, bank[3])
         for r in range(2):
-            fetch(r, 0, fetched[0][:, r, :])
-        fetch(1, 1, fetched[1][:, 0, :])
-        combine(2, *halves(13))
-        first, second = halves(15)
-        nc.vector.tensor_tensor(first, choice(0, 1), gate_sb[:, 0, block_cols(1)], MULT)
-        product_a(16, bank[5])
-        product_b(16, bank[2])
-        product_a(17, bank[4])
-        product_b(17, bank[6])
-        combine_fetched(nc.vector, 0, fetched[0][:], both(17))
-        turn(7, bank[1])
-        turn(8, bank[7])
-        turn(9, bank[3])
-        second_layer(0, bank[5][:, 0:C])
-        for m in (7, 8, 9):
+            fetch(r, 1, fetched[0][:, r, :])
+        weigh(0, halves(13))
+        first = halves(15)[0]
+        nc.vector.tensor_tensor(first, choice(0, 2), gate_sb[:, 0, block_cols(2)], MULT)
+        product_a(17, bank[5])
+        product_b(16, bank[1])
+        product_b(17, bank[0])
+        turn(7, bank[7])
+        added_transposes(bank[2], (first_ys[:], *halves(13)))
+        nc.scalar.copy(by_token[0][:, 0:C], bank[2][:, 0:C])
+        turn(8, bank[6])
+        turn(9, bank[5])
+        store_summed(0, (by_token[0][:, 0:C],), bank[4])
+        weighted = sig_tile(17)[:].rearrange("p (r c) -> p r c", r=2)
+        nc.vector.tensor_tensor(weighted, fetched[0][:], gate_sb[:, :, block_cols(1)], MULT)
+        quantise(7)
+        second = fetched[0][:, 0, :]
+        nc.vector.tensor_tensor(second, choice(1, 2), gate_sb[:, 1, block_cols(2)], MULT)
+        for m in (8, 9):
             quantise(m)
-        nc.vector.tensor_tensor(second, fetched[1][:, 0, :], gate_sb[:, 1, block_cols(1)], MULT)
-        nc.vector.tensor_tensor(partial[:, block_cols(1)], first, second, ADD)
-        finish(0, bank[5][:, 0:C])
-        for m, target in ((8, bank[0][:, 0:P]), (9, bank[2][:, 0:P]), (7, bank[4][:, 0:C])):
+        nc.vector.tensor_tensor(partial[:, block_cols(1)], *halves(17), ADD)
+        nc.vector.tensor_tensor(partial[:, block_cols(2)], first, second, ADD)
+        for m, target in ((7, bank[5][:, 0:C]), (8, bank[6][:, 0:P]), (9, bank[1][:, 0:P])):
             second_layer(m, target)
             finish(m, target)

@@ -45,7 +45,7 @@ def tile_moe_shr_glu_sigmoid_kernel(
         psum = ctx.enter_context(tc.psum_pool(name="psum", bufs=1))
 
         def held(shape, dtype, name, tag=None):
-            return keep.tile(shape, dtype, name=name, tag=tag or name, align_bytes=64)
+            return keep.tile(shape, dtype, name=name, tag=tag or name, align_bytes=256)
 
         def ring(count, shape, dtype, name):
             return [held(shape, dtype, f"{name}{r}") for r in range(count)]
@@ -326,6 +326,9 @@ def tile_moe_shr_glu_sigmoid_kernel(
         def halves(j):
             return sig_tile(j)[:, 0:C], sig_tile(j)[:, C : 2 * C]
 
+        def both(j):
+            return sig_tile(j)[:].rearrange("p (r c) -> p r c", r=2)
+
         def added_transposes(target, terms):
             for part in range(C // P):
                 cols = slice(part * P, (part + 1) * P)
@@ -348,41 +351,39 @@ def tile_moe_shr_glu_sigmoid_kernel(
         product_b(12, bank[4])
         product_a(13, bank[1])
         product_b(13, bank[5])
-        product_a(14, bank[0])
         turn(4, bank[6])
         turn(5, bank[3], nc.vector.tensor_copy)
-        turn(6, bank[1])
+        turn(6, bank[0])
         for m in (4, 5, 6):
             quantise(m)
         routed_results((4, 5), bank[2], nc.scalar.copy)
         routed_results((6,), bank[4], nc.vector.tensor_copy)
-        product_a(15, bank[5])
-        product_a(16, bank[0])
+        product_a(14, bank[5])
         product_b(14, bank[6])
-        product_b(15, bank[3])
+        product_a(15, bank[3])
+        product_a(16, bank[0])
+        product_b(15, bank[5])
         for r in range(2):
             fetch(r, 1, fetched[0][:, r, :])
         weigh(0, halves(13))
-        first = halves(15)[0]
-        nc.vector.tensor_tensor(first, choice(0, 2), gate_sb[:, 0, block_cols(2)], MULT)
-        product_a(17, bank[5])
-        product_b(16, bank[1])
+        nc.vector.tensor_tensor(halves(15)[0], choice(0, 2), gate_sb[:, 0, block_cols(2)], MULT)
+        product_a(17, bank[6])
+        product_b(16, bank[3])
         product_b(17, bank[0])
+        fetch(1, 2, halves(15)[1])
         turn(7, bank[7])
         added_transposes(bank[2], (first_ys[:], *halves(13)))
         nc.scalar.copy(by_token[0][:, 0:C], bank[2][:, 0:C])
-        turn(8, bank[6])
+        turn(8, bank[1])
         turn(9, bank[5])
         store_summed(0, (by_token[0][:, 0:C],), bank[4])
-        weighted = sig_tile(17)[:].rearrange("p (r c) -> p r c", r=2)
-        nc.vector.tensor_tensor(weighted, fetched[0][:], gate_sb[:, :, block_cols(1)], MULT)
+        nc.vector.tensor_tensor(both(16), fetched[0][:], gate_sb[:, :, block_cols(1)], MULT)
         quantise(7)
-        second = fetched[0][:, 0, :]
-        nc.vector.tensor_tensor(second, choice(1, 2), gate_sb[:, 1, block_cols(2)], MULT)
+        nc.vector.tensor_tensor(halves(17)[1], halves(15)[1], gate_sb[:, 1, block_cols(2)], MULT)
         for m in (8, 9):
             quantise(m)
-        nc.vector.tensor_tensor(partial[:, block_cols(1)], *halves(17), ADD)
-        nc.vector.tensor_tensor(partial[:, block_cols(2)], first, second, ADD)
-        for m, target in ((7, bank[5][:, 0:C]), (8, bank[6][:, 0:P]), (9, bank[1][:, 0:P])):
+        nc.vector.tensor_tensor(partial[:, block_cols(1)], *halves(16), ADD)
+        nc.vector.tensor_tensor(partial[:, block_cols(2)], halves(15)[0], halves(17)[1], ADD)
+        for m, target in ((7, bank[5][:, 0:C]), (8, bank[6][:, 0:P]), (9, bank[3][:, 0:P])):
             second_layer(m, target)
             finish(m, target)

@@ -25,15 +25,11 @@ PASSES = K // 512
 QUADRANTS = 4
 LIST_ROWS = 16
 SHARED = E
-SCALE_GROUPS = ((4, 7), (2, 4), (0, 2))
-WORD_GROUPS = tuple((e, e + 1) for e in range(E + 1))
-UNITS = (
-    ((SHARED, 0, 2),)
-    + tuple((e, e * C, 2) for e in reversed(range(E)))
-    + ((SHARED, C, 2), (SHARED, 2 * C, 1), (SHARED, 2 * C + P, 1))
-)
+SCALE_GROUPS = ((0, 2), (2, 4), (4, 7))
+PACKED_SETS = ((1, 3), (3, 6))
+ROUTED_TILES = S // P
+BLOCKS = T // C
 POOL_TILES = (0, 2, 4, 6)
-TILES = tuple((e, lo + part * P) for e, lo, tiles in UNITS for part in range(tiles))
 
 
 def tile_moe_shr_glu_sigmoid_kernel(
@@ -44,14 +40,11 @@ def tile_moe_shr_glu_sigmoid_kernel(
         keep = ctx.enter_context(tc.tile_pool(name="keep", bufs=1))
         psum = ctx.enter_context(tc.psum_pool(name="psum", bufs=1))
 
-        def held(shape, dtype, name, tag=None):
-            return keep.tile(shape, dtype, name=name, tag=tag or name, align_bytes=256)
+        def held(shape, dtype, name):
+            return keep.tile(shape, dtype, name=name, align_bytes=256)
 
         def ring(count, shape, dtype, name):
             return [held(shape, dtype, f"{name}{r}") for r in range(count)]
-
-        def banks(count, name):
-            return [psum.tile([P, H], F32, name=f"{name}{r}") for r in range(count)]
 
         def zero(engine, tile):
             engine.memset(tile[:].bitcast(I32), 0)
@@ -59,85 +52,93 @@ def tile_moe_shr_glu_sigmoid_kernel(
         offs_sb = held([P, S // LIST_ROWS], U16, "offs_sb")
         pos_sb = [held([P, T // LIST_ROWS], U16, f"pos{r}_sb") for r in (1, 2)]
         xw = ring(PASSES, [P, T], I32, "xw")
-        xs_planes = held([P, PASSES, T], U8, "xs_planes")
+        xs_planes = held([P, PASSES * T], U8, "xs_planes")
         w1s = 2 * [held([P, rows * PASSES, H], U8, f"w1s{rows}") for rows in (3, 2)]
         w3s = 2 * [held([P, rows * PASSES, H], U8, f"w3s{rows}") for rows in (3, 2)]
-        w1w = [held([P, (hi - lo) * PASSES, 2 * H], U8, f"w1w{lo}") for lo, hi in WORD_GROUPS]
-        w3w = [held([P, (hi - lo) * PASSES, 2 * H], U8, f"w3w{lo}") for lo, hi in WORD_GROUPS]
+        w1w = ring(E + 1, [P, PASSES, 2 * H], U8, "w1w")
+        w3w = ring(E + 1, [P, PASSES, 2 * H], U8, "w3w")
         w2s = held([P, E + 1, N], U8, "w2s")
         w2w = held([P, E + 1, 2 * N], U8, "w2w")
         ident = held([P, P], F32, "ident")
-        gw = ring(2, [P, PASSES, C], U32, "gw")
-        gs_last = ring(PASSES, [P, 2 * C], U8, "gs_last")
-        gs_packed = held([P, 4 * C], U8, "gs_packed")
-        gs_moved = held([P, 4 * C], U8, "gs_moved")
+        gw = [ring(2, [P, C], U32, f"gw{o}_") for o in range(PASSES)]
+        gs_first = ring(PASSES, [P, C], U8, "gs_first")
+        gs_packed = [held([P, (hi - lo) * C], U8, f"gs_packed{lo}") for lo, hi in PACKED_SETS]
+        gs_moved = [held([P, (hi - lo) * C], U8, f"gs_moved{lo}") for lo, hi in PACKED_SETS]
         y_all = held([P, S], F32, "y_all")
-        sig = ring(4, [P, H], F32, "sig")
-        sig_end = ring(4, [P, H], F32, "sig_end")
+        gate_sb = held([P, 2, T], F32, "gate_sb")
+        sig_all = held([P, 8, H], F32, "sig_all")
+        sig = [sig_all[:, r, :] for r in range(8)]
         b_sb = ring(2, [P, H], F32, "b_sb")
         h = ring(8, [P, H], BF16, "h")
-        h_turned = ring(4, [P, 2, P, 4], BF16, "hT")
-        bank = banks(8, "bank")
+        h_turned = ring(3, [P, 4, P, 4], BF16, "hT")
+        h_codes = held([P, S + T], U32, "h_codes")
+        h_scales = held([P, S + T], U8, "h_scales")
+        fetched = held([P, 4, C], F32, "fetched")
+        weighted = ring(BLOCKS, [P, 2, C], F32, "weighted")
+        partial = held([P, T], F32, "partial")
+        result = held([P, T], F32, "result")
+        short = [psum.tile([P, H], F32, name=f"short{r}") for r in range(4)]
+        long = [psum.tile([P, H], F32, name=f"long{r}") for r in range(4)]
 
-        def load_rows(queue, plane, rows, r):
-            queue.dma_start(plane[r:P:32].bitcast(I32), rows[r:16:4].bitcast(I32))
+        def load(tile, source):
+            nc.sync.dma_start(tile.bitcast(I32), source.bitcast(I32))
 
-        def load_scales(queue, planes, scales, g, which=range(4)):
+        def load_rows(plane, rows):
+            for r in range(4):
+                load(plane[r:P:32], rows[r:16:4])
+
+        def load_scales(planes, scales, g):
             lo, hi = SCALE_GROUPS[g]
-            for r in which:
-                load_rows(queue, planes[g][:, 0 : (hi - lo) * PASSES, :], scales[lo:hi].rearrange("e s f n -> f (e s) n"), r)
+            load_rows(planes[g][:, 0 : (hi - lo) * PASSES, :], scales[lo:hi].rearrange("e s f n -> f (e s) n"))
 
-        def load_words(slots, words, g):
-            lo, hi = WORD_GROUPS[g]
-            nc.sync.dma_start(slots[g][:].bitcast(I32), words[lo:hi].rearrange("e s p b -> p (e s) b").bitcast(I32))
+        def load_words(slots, words, e):
+            load(slots[e][:], words[e].rearrange("s p b -> p s b"))
 
         def slot_offsets(lo, hi):
             return offs_sb[:, lo // LIST_ROWS : hi // LIST_ROWS]
 
         def gather_words(e, o):
-            nc.vector.tensor_copy(
-                gw[e % len(gw)][:, o, :], xw[o][:].bitcast(U32).indirect(slot_offsets(e * C, (e + 1) * C))
-            )
+            nc.vector.tensor_copy(gw[o][e % 2][:], xw[o][:].bitcast(U32).indirect(slot_offsets(e * C, (e + 1) * C)))
 
-        def gather_scales(target, o, lo, hi):
-            nc.vector.tensor_copy(target, xs_planes[:, o, :].indirect(slot_offsets(lo, hi)))
+        def gather_first_scales(o):
+            nc.vector.tensor_copy(gs_first[o][:], xs_planes[:, o * T : (o + 1) * T].indirect(slot_offsets(0, C)))
 
-        def move_second_planes(target, gathered):
+        def gather_packed(g):
+            lo, hi = PACKED_SETS[g]
+            nc.vector.tensor_copy(gs_packed[g][:], xs_planes[:].indirect(slot_offsets(lo * C, hi * C)))
+
+        def move_second_planes(g):
             for r in range(4):
-                nc.sync.dma_start(target[r:P:32].bitcast(I32), gathered[16 + r : 32 : 4].bitcast(I32))
+                load(gs_moved[g][r:P:32], gs_packed[g][16 + r : 32 : 4])
 
-        def expert_plane(e, o):
-            if e >= 4:
-                return gs_last[o][:, (e - 4) * C : (e - 3) * C]
-            return (gs_moved, gs_packed)[o][:, e * C : (e + 1) * C]
-
-        def token_operands(e, lo, o):
-            if e == SHARED:
-                return xw[o][:, lo : lo + P], xs_planes[:, o, lo : lo + P]
-            c = lo - e * C
-            return gw[e % len(gw)][:, o, c : c + P], expert_plane(e, o)[:, c : c + P]
-
-        def place(groups, e, o):
+        def member(groups, e):
             g = [first <= e < end for first, end in groups].index(True)
-            return g, (e - groups[g][0]) * PASSES + o
+            return g, e - groups[g][0]
 
-        def product(target, slots, planes, e, lo, passes):
-            for o in passes:
-                g, row = place(SCALE_GROUPS, e, o)
-                gword, wrow = place(WORD_GROUPS, e, o)
-                codes, code_scales = token_operands(e, lo, o)
-                nc.tensor.matmul_mx(
-                    out=target[:],
-                    lhsT=codes.bitcast(FP8X4),
-                    lhsT_scale=code_scales,
-                    rhs=slots[gword][:, wrow, :].bitcast(FP4X4),
-                    rhs_scale=planes[g][:, row, :],
-                    start=(o == 0),
-                    stop=(o == PASSES - 1),
-                )
+        def token_operands(j, o):
+            if j >= ROUTED_TILES:
+                lo = (j - ROUTED_TILES) * P
+                return xw[o][:, lo : lo + P], xs_planes[:, o * T + lo : o * T + lo + P]
+            e, c = j // 2, j % 2 * P
+            if e == 0:
+                return gw[o][0][:, c : c + P], gs_first[o][:, c : c + P]
+            g, place = member(PACKED_SETS, e)
+            plane = (gs_packed, gs_moved)[o][g]
+            return gw[o][e % 2][:, c : c + P], plane[:, place * C + c : place * C + c + P]
 
-        def sig_tile(j):
-            return sig[j % len(sig)] if j < 14 else sig_end[j - 14]
+        def one_pass(target, slots, planes, j, o, first, last):
+            e = min(j // 2, SHARED)
+            g, place = member(SCALE_GROUPS, e)
+            codes, code_scales = token_operands(j, o)
+            nc.tensor.matmul_mx(
+                out=target[:],
+                lhsT=codes.bitcast(FP8X4),
+                lhsT_scale=code_scales,
+                rhs=slots[e][:, o, :].bitcast(FP4X4),
+                rhs_scale=planes[g][:, place * PASSES + o, :],
+                start=first,
+                stop=last,
+            )
 
         def paired(ap):
             return ap.rearrange("t (u p f) -> t u p f", u=2, f=2)
@@ -145,155 +146,96 @@ def tile_moe_shr_glu_sigmoid_kernel(
         def permuted(ap):
             return ap.rearrange("t (p u f) -> t u p f", u=2, f=2)
 
-        def product_a(j, target, passes=(0, 1)):
-            product(target, w1w, w1s, *TILES[j], passes)
-            if passes[-1] == PASSES - 1:
-                nc.scalar.activation(paired(sig_tile(j)[:]), permuted(target[:]), SIGMOID)
+        def sigmoid(j, source):
+            nc.scalar.activation(paired(sig[j % len(sig)]), permuted(source[:]), SIGMOID)
 
-        def product_b(j, target, passes=(0, 1)):
-            product(target, w3w, w3s, *TILES[j], passes)
-            if passes[-1] != PASSES - 1:
-                return
+        def b_bank(j):
+            return long[j % 4]
+
+        def product(j):
+            if j % 2 and j // 2 + 2 < E:
+                for o in range(PASSES):
+                    gather_words(j // 2 + 2, o)
             if j in POOL_TILES:
                 b_copy = b_sb[POOL_TILES.index(j) % len(b_sb)]
-                nc.scalar.copy(paired(b_copy[:]), permuted(target[:]))
-                nc.gpsimd.tensor_tensor(h[j % len(h)][:], b_copy[:], sig_tile(j)[:], MULT)
+                nc.scalar.copy(paired(b_copy[:]), permuted(b_bank(j)[:]))
+                nc.gpsimd.tensor_tensor(h[j % len(h)][:], b_copy[:], sig[j % len(sig)], MULT)
                 return
-            nc.vector.tensor_tensor(paired(h[j % len(h)][:]), permuted(target[:]), paired(sig_tile(j)[:]), MULT)
+            nc.vector.tensor_tensor(
+                paired(h[j % len(h)][:]), permuted(b_bank(j)[:]), paired(sig[j % len(sig)]), MULT
+            )
 
-        units = UNITS
-        first_tile = [sum(unit[2] for unit in units[:m]) for m in range(len(units))]
-        h_codes = ring(len(units), [P, C], U32, "h_codes")
-        h_scales = ring(len(units), [P, C], U8, "h_scales")
-        fetched = ring(2, [P, 2, C], F32, "fetched")
-        first_ys = held([P, C], F32, "first_ys")
-        by_token = ring(2, [P, 2 * C], F32, "by_token")
-        partial = held([P, T], F32, "partial")
-        result = held([P, T], F32, "result")
+        def a_pass(j, a_bank, o):
+            one_pass(a_bank, w1w, w1s, j, o, o == 0, o == 1)
+            if o == 1:
+                sigmoid(j, a_bank)
 
-        def turn(m, target, copy=nc.scalar.copy):
-            tiles = units[m][2]
+        def b_passes(j):
+            for o in range(PASSES):
+                one_pass(b_bank(j), w3w, w3s, j, o, o == 0, o == 1)
+            product(j)
+
+        def first_layer(j, a_bank):
+            for o in range(PASSES):
+                a_pass(j, a_bank, o)
+            b_passes(j)
+
+        def first_layer_first_passes(tiles, a_banks):
+            for slots, planes, targets in ((w1w, w1s, a_banks), (w3w, w3s, [b_bank(j) for j in tiles])):
+                for j, target in zip(tiles, targets):
+                    one_pass(target, slots, planes, j, 0, True, False)
+            for j, a_bank in zip(tiles, a_banks):
+                one_pass(a_bank, w1w, w1s, j, 1, False, True)
+                sigmoid(j, a_bank)
+            for j in tiles:
+                one_pass(b_bank(j), w3w, w3s, j, 1, False, True)
+                product(j)
+
+        def first_layer_by_pass(tiles, a_banks, passes):
+            for o in passes:
+                for j, a_bank in zip(tiles, a_banks):
+                    one_pass(a_bank, w1w, w1s, j, o, o == passes[0], o == passes[1])
+            for j, a_bank in zip(tiles, a_banks):
+                sigmoid(j, a_bank)
+            for j in tiles:
+                for o in passes:
+                    one_pass(b_bank(j), w3w, w3s, j, o, o == passes[0], o == passes[1])
+                product(j)
+
+        def turn(j, tiles, target, turned, copy=nc.scalar.copy):
             for part in range(tiles):
-                pairs = h[(first_tile[m] + part) % len(h)][:].bitcast(F32)
+                pairs = h[(j + part) % len(h)][:].bitcast(F32)
                 for u in range(2):
                     nc.tensor.transpose(
                         target[:, (2 * part + u) * P : (2 * part + u + 1) * P], pairs[:, u * P : (u + 1) * P], ident[:]
                     )
-            copy(
-                h_turned[m % len(h_turned)][:, 0:tiles].bitcast(F32),
-                target[:, 0 : 2 * tiles * P].rearrange("p (j u t) -> p j t u", u=2, t=P),
-            )
+            copy(turned.bitcast(F32), target[:, 0 : 2 * tiles * P].rearrange("p (j u t) -> p j t u", u=2, t=P))
 
-        def quantise(m):
-            tiles = units[m][2]
+        def quantise(j, tiles, turned):
+            cols = slice(j * P, (j + tiles) * P)
             nc.vector.quantize_mx(
-                out=h_codes[m][:, 0 : tiles * P].bitcast(FP8X4),
-                scales=h_scales[m][:, 0 : tiles * P],
-                in_=h_turned[m % len(h_turned)][:, 0:tiles].rearrange("p j t r -> p (j t r)"),
+                out=h_codes[:, cols].bitcast(FP8X4),
+                scales=h_scales[:, cols],
+                in_=turned.rearrange("p j t r -> p (j t r)"),
             )
 
-        def second_layer(m, target):
-            e, lo, tiles = units[m]
+        def second_layer(j, tiles, target):
+            e = min(j // 2, SHARED)
+            cols = slice(j * P, (j + tiles) * P)
             nc.tensor.matmul_mx(
                 out=target,
                 lhsT=w2w[:, e, :].bitcast(FP4X4),
                 lhsT_scale=w2s[:, e, :],
-                rhs=h_codes[m][:, 0 : tiles * P].bitcast(FP8X4),
-                rhs_scale=h_scales[m][:, 0 : tiles * P],
+                rhs=h_codes[:, cols].bitcast(FP8X4),
+                rhs_scale=h_scales[:, cols],
                 start=True,
                 stop=True,
             )
 
-        def routed_results(members, target, copy):
-            start = min(units[m][1] for m in members)
-            for m in members:
-                e, lo, tiles = units[m]
-                second_layer(m, target[:, lo - start : lo - start + tiles * P])
-            width = sum(units[m][2] for m in members) * P
-            copy(y_all[:, start : start + width], target[:, 0:width])
-
-        zero(nc.gpsimd, xs_planes)
-        for plane in (w1s[0], w3s[0], w3s[1], w1s[1], gs_moved):
-            zero(nc.vector, plane)
-        zero(nc.vector, w2s)
-        nc.vector.memset(ident[:], 0.0)
-        make_identity(nc, ident[:], nomemset=True)
-        token_rows = x_scales.rearrange("s f t -> f s t")
-
-        def load_tokens(o):
-            nc.sync.dma_start(xw[o][:], x_words[o].rearrange("p t r -> p (t r)").bitcast(I32))
-
-        def load_expert(e):
-            load_words(w1w, w1_words, e)
-            load_words(w3w, w3_words, e)
-
-        def load_group(g):
-            load_scales(nc.sync, w1s, w1_scales, g)
-            load_scales(nc.sync, w3s, w3_scales, g)
-
-        nc.sync.dma_start(offs_sb[:], offs)
-        load_tokens(0)
-        for r in range(4):
-            load_rows(nc.sync, xs_planes, token_rows, r)
-        load_words(w1w, w1_words, SHARED)
-        load_scales(nc.sync, w1s, w1_scales, 0)
-        load_tokens(1)
-        nc.sync.dma_start(xs_planes[16:32, 1, :].bitcast(I32), x_scales[0].bitcast(I32))
-        load_words(w3w, w3_words, SHARED)
-        load_scales(nc.sync, w3s, w3_scales, 0)
-        load_expert(5)
-        load_expert(4)
-        gather_words(5, 0)
-        gather_scales(gs_last[0][:], 0, 4 * C, 6 * C)
-        gather_words(4, 0)
-        gather_words(5, 1)
-        gather_scales(gs_last[1][:], 1, 4 * C, 6 * C)
-        gather_words(4, 1)
-        for lo in (2 * C, 0):
-            gather_scales(gs_packed[:, lo : lo + 2 * C], 1, lo, lo + 2 * C)
-        load_group(1)
-        load_expert(3)
-        move_second_planes(gs_moved, gs_packed)
-        load_expert(2)
-        nc.sync.dma_start(w2w[:].bitcast(I32), w2_words.rearrange("e s p b -> p (e s) b").bitcast(I32))
-        for r in range(4):
-            load_rows(nc.sync, w2s, w2_scales.rearrange("e s f n -> f (e s) n"), r)
-
-        gate_sb = held([P, 2, T], F32, "gate_sb")
-        for m in range(E):
-            a_banks = bank[2 * (m % 2) : 2 * (m % 2) + 2]
-            b_banks = bank[4 + 2 * (m % 2) : 6 + 2 * (m % 2)]
-            if m == 0:
-                for o in range(PASSES):
-                    for part in range(2):
-                        product_a(part, a_banks[part], (o,))
-                for o in range(PASSES):
-                    for part in range(2):
-                        product_b(part, b_banks[part], (o,))
-            else:
-                for part in range(2):
-                    product_a(2 * m + part, a_banks[part])
-                for part in range(2):
-                    product_b(2 * m + part, b_banks[part])
-            if 1 <= m <= E - 2:
-                for o in range(PASSES):
-                    gather_words(units[m + 2][0], o)
-            if m == 2:
-                load_group(2)
-                load_expert(1)
-                load_expert(0)
-                nc.sync.dma_start(pos_sb[1][:], pos2)
-                nc.sync.dma_start(pos_sb[0][:], pos1)
-                nc.sync.dma_start(gate_sb[:], gate.rearrange("g n t -> n g t"))
-            if m in (2, 4):
-                for part in range(2):
-                    turn(m - 2 + part, a_banks[part])
-                for part in range(2):
-                    quantise(m - 2 + part)
-            if m == 4:
-                routed_results((1,), bank[4], nc.vector.tensor_copy)
-                second_layer(0, bank[7][:, 0:C])
-                nc.scalar.copy(first_ys[:], bank[7][:, 0:C])
+        def routed_results(e, experts, target, copy):
+            for part in range(experts):
+                second_layer(2 * (e + part), 2, target[:, part * C : (part + 1) * C])
+            copy(y_all[:, e * C : (e + experts) * C], target[:, 0 : experts * C])
 
         def block_cols(block):
             return slice(block * C, (block + 1) * C)
@@ -304,86 +246,121 @@ def tile_moe_shr_glu_sigmoid_kernel(
         def fetch(r, block, target):
             nc.scalar.activation(target, choice(r, block), COPY)
 
-        def combine_fetched(engine, block, pair, weighted):
-            engine.tensor_tensor(weighted, pair, gate_sb[:, :, block_cols(block)], MULT)
-            engine.tensor_tensor(partial[:, block_cols(block)], weighted[:, 0, :], weighted[:, 1, :], ADD)
+        def weigh(r, block, target):
+            nc.vector.tensor_tensor(target, choice(r, block), gate_sb[:, r, block_cols(block)], MULT)
 
-        def combine(block, first, second):
-            for r, target in enumerate((first, second)):
-                nc.vector.tensor_tensor(target, choice(r, block), gate_sb[:, r, block_cols(block)], MULT)
-            nc.vector.tensor_tensor(partial[:, block_cols(block)], first, second, ADD)
+        def add_choices(block):
+            nc.gpsimd.tensor_tensor(partial[:, block_cols(block)], weighted[block][:, 0, :], weighted[block][:, 1, :], ADD)
 
-        def finish(m, source):
-            e, lo, tiles = units[m]
-            cols = slice(lo, lo + tiles * P)
+        def finish(j, tiles, source):
+            cols = slice((j - ROUTED_TILES) * P, (j - ROUTED_TILES + tiles) * P)
+            second_layer(j, tiles, source)
             nc.vector.tensor_tensor(result[:, cols], source, partial[:, cols], ADD)
             if cols.stop % C == 0:
                 nc.sync.dma_start(out[:, cols.stop - C : cols.stop], result[:, cols.stop - C : cols.stop])
 
-        def freed(j):
-            return h[j % len(h)][:].bitcast(F32)
+        zero(nc.gpsimd, xs_planes)
+        for plane in (w1s[0], w3s[0], w1s[1], w3s[1], gs_moved[0], gs_moved[1], w2s):
+            zero(nc.vector, plane)
+        nc.vector.memset(ident[:], 0.0)
+        make_identity(nc, ident[:], nomemset=True)
 
-        def halves(j):
-            return sig_tile(j)[:, 0:C], sig_tile(j)[:, C : 2 * C]
+        def load_tokens(o):
+            load(xw[o][:], x_words[o].rearrange("p t r -> p (t r)"))
 
-        def both(j):
-            return sig_tile(j)[:].rearrange("p (r c) -> p r c", r=2)
+        nc.sync.dma_start(offs_sb[:], offs)
+        load_words(w1w, w1_words, 0)
+        load_rows(xs_planes[:].rearrange("p (s t) -> p s t", s=PASSES), x_scales.rearrange("s f t -> f s t"))
+        load_tokens(0)
+        load_scales(w1s, w1_scales, 0)
+        load_tokens(1)
+        load_words(w3w, w3_words, 0)
+        for o in range(PASSES):
+            gather_first_scales(o)
+            gather_words(0, o)
+        load(xs_planes[16:32, 0:T], x_scales[1])
+        load_scales(w3s, w3_scales, 0)
+        load_words(w1w, w1_words, 1)
+        load_words(w3w, w3_words, 1)
+        for o in range(PASSES):
+            gather_words(1, o)
+        gather_packed(0)
+        gather_packed(1)
+        load_scales(w1s, w1_scales, 1)
+        move_second_planes(0)
+        load_words(w1w, w1_words, 2)
+        load_scales(w3s, w3_scales, 1)
+        load_words(w3w, w3_words, 2)
+        move_second_planes(1)
+        load_words(w1w, w1_words, 3)
+        load_words(w3w, w3_words, 3)
 
-        def added_transposes(target, terms):
-            for part in range(C // P):
-                cols = slice(part * P, (part + 1) * P)
-                for r, term in enumerate(terms):
-                    nc.tensor.matmul(
-                        target[:, cols], term[:, cols], ident[:], start=(r == 0), stop=(r == len(terms) - 1), is_transpose=True
-                    )
-
-        def weigh(block, targets):
-            for r in range(2):
-                nc.vector.tensor_tensor(targets[r], choice(r, block), gate_sb[:, r, block_cols(block)], MULT)
-
-        def store_summed(block, terms, target):
-            added_transposes(target, terms)
-            nc.scalar.copy(result[:, block_cols(block)], target[:, 0:C])
-            nc.sync.dma_start(out[:, block_cols(block)], result[:, block_cols(block)])
-
-        routed_results((2, 3), bank[2], nc.vector.tensor_copy)
-        product_a(12, bank[0])
-        product_b(12, bank[4])
-        product_a(13, bank[1])
-        product_b(13, bank[5])
-        turn(4, bank[6])
-        turn(5, bank[3], nc.vector.tensor_copy)
-        turn(6, bank[0])
-        for m in (4, 5, 6):
-            quantise(m)
-        routed_results((4, 5), bank[2], nc.scalar.copy)
-        routed_results((6,), bank[4], nc.vector.tensor_copy)
-        product_a(14, bank[5])
-        product_b(14, bank[6])
-        product_a(15, bank[3])
-        product_a(16, bank[0])
-        product_b(15, bank[5])
+        for e in range(E):
+            a_banks = short[2 * (e % 2) : 2 * (e % 2) + 2]
+            if e == 0:
+                first_layer_by_pass((0, 1), a_banks, (0, 1))
+            elif e == 1:
+                first_layer_first_passes((2, 3), a_banks)
+            else:
+                for part in range(2):
+                    for o in range(PASSES):
+                        a_pass(2 * e + part, a_banks[part], o)
+                for part in range(2):
+                    b_passes(2 * e + part)
+            if e == 1:
+                load_scales(w1s, w1_scales, 2)
+                load_scales(w3s, w3_scales, 2)
+                for e in (4, 5, 6):
+                    load_words(w1w, w1_words, e)
+                    load_words(w3w, w3_words, e)
+                    if e == 5:
+                        load(w2w[:], w2_words.rearrange("e s p b -> p (e s) b"))
+                        load_rows(w2s[:], w2_scales.rearrange("e s f n -> f (e s) n"))
+                for r, pos in enumerate((pos1, pos2)):
+                    nc.sync.dma_start(pos_sb[r][:], pos)
+                nc.sync.dma_start(gate_sb[:], gate.rearrange("g n t -> n g t"))
+            if e in (3, 4):
+                pair = e - 3
+                for part in range(2):
+                    turn(4 * pair + 2 * part, 2, a_banks[part], h_turned[pair][:, 2 * part : 2 * part + 2])
+                quantise(4 * pair, 4, h_turned[pair][:])
+        routed_results(0, 2, short[0], nc.scalar.copy)
+        routed_results(2, 2, short[1], nc.vector.tensor_copy)
+        turn(8, 2, short[2], h_turned[2][:, 0:2])
+        turn(10, 1, short[3], h_turned[0][:, 0:1])
+        turn(11, 1, long[1], h_turned[0][:, 1:2], nc.vector.tensor_copy)
+        quantise(8, 2, h_turned[2][:, 0:2])
+        quantise(10, 2, h_turned[0][:, 0:2])
+        first_layer(12, short[0])
+        a_pass(13, short[1], 0)
+        routed_results(4, 1, short[2], nc.scalar.copy)
+        routed_results(5, 1, short[3], nc.scalar.copy)
+        a_pass(13, short[1], 1)
+        fetch(0, 0, fetched[:, 0, :])
+        fetch(1, 0, fetched[:, 1, :])
+        weigh(0, 1, weighted[1][:, 0, :])
         for r in range(2):
-            fetch(r, 1, fetched[0][:, r, :])
-        weigh(0, halves(13))
-        nc.vector.tensor_tensor(halves(15)[0], choice(0, 2), gate_sb[:, 0, block_cols(2)], MULT)
-        product_a(17, bank[6])
-        product_b(16, bank[3])
-        product_b(17, bank[0])
-        fetch(1, 2, halves(15)[1])
-        turn(7, bank[7])
-        added_transposes(bank[2], (first_ys[:], *halves(13)))
-        nc.scalar.copy(by_token[0][:, 0:C], bank[2][:, 0:C])
-        turn(8, bank[1])
-        turn(9, bank[5])
-        store_summed(0, (by_token[0][:, 0:C],), bank[4])
-        nc.vector.tensor_tensor(both(16), fetched[0][:], gate_sb[:, :, block_cols(1)], MULT)
-        quantise(7)
-        nc.vector.tensor_tensor(halves(17)[1], halves(15)[1], gate_sb[:, 1, block_cols(2)], MULT)
-        for m in (8, 9):
-            quantise(m)
-        nc.vector.tensor_tensor(partial[:, block_cols(1)], *halves(16), ADD)
-        nc.vector.tensor_tensor(partial[:, block_cols(2)], halves(15)[0], halves(17)[1], ADD)
-        for m, target in ((7, bank[5][:, 0:C]), (8, bank[6][:, 0:P]), (9, bank[3][:, 0:P])):
-            second_layer(m, target)
-            finish(m, target)
+            weigh(r, 2, weighted[2][:, r, :])
+        b_passes(13)
+        first_layer(14, short[0])
+        fetch(1, 1, fetched[:, 2, :])
+        add_choices(2)
+        nc.gpsimd.tensor_tensor(weighted[0][:], fetched[:, 0:2, :], gate_sb[:, :, block_cols(0)], MULT)
+        add_choices(0)
+        nc.gpsimd.tensor_tensor(weighted[1][:, 1, :], fetched[:, 2, :], gate_sb[:, 1, block_cols(1)], MULT)
+        add_choices(1)
+        first_layer(15, short[2])
+        first_layer(16, short[3])
+        first_layer(17, short[1])
+        turn(12, 2, short[0], h_turned[1][:, 0:2])
+        turn(14, 2, short[2], h_turned[1][:, 2:4], nc.vector.tensor_copy)
+        turn(16, 1, short[3], h_turned[0][:, 0:1])
+        turn(17, 1, short[1], h_turned[2][:, 0:1])
+        quantise(12, 2, h_turned[1][:, 0:2])
+        quantise(14, 2, h_turned[1][:, 2:4])
+        quantise(16, 1, h_turned[0][:, 0:1])
+        quantise(17, 1, h_turned[2][:, 0:1])
+        finish(12, 2, long[2][:, 0:C])
+        finish(14, 2, long[3][:, 0:C])
+        finish(16, 1, long[0][:, 0:P])
+        finish(17, 1, long[1][:, 0:P])

@@ -26,7 +26,7 @@ QUADRANTS = 4
 LIST_ROWS = 16
 SHARED = E
 SCALE_GROUPS = ((0, 2), (2, 4), (4, 7))
-PACKED_SETS = ((1, 3), (3, 6))
+PACKED_SETS = ((1, 3), (3, 5))
 ROUTED_TILES = S // P
 BLOCKS = T // C
 POOL_TILES = (0, 2, 4, 6)
@@ -60,7 +60,7 @@ def tile_moe_shr_glu_sigmoid_kernel(
         w2s = held([P, E + 1, N], U8, "w2s")
         w2w = held([P, E + 1, 2 * N], U8, "w2w")
         ident = held([P, P], F32, "ident")
-        gw = [ring(2, [P, C], U32, f"gw{o}_") for o in range(PASSES)]
+        gw = ring(4, [P, C], U32, "gw")
         gs_first = ring(PASSES, [P, C], U8, "gs_first")
         gs_packed = [held([P, (hi - lo) * C], U8, f"gs_packed{lo}") for lo, hi in PACKED_SETS]
         gs_moved = [held([P, (hi - lo) * C], U8, f"gs_moved{lo}") for lo, hi in PACKED_SETS]
@@ -97,15 +97,28 @@ def tile_moe_shr_glu_sigmoid_kernel(
         def slot_offsets(lo, hi):
             return offs_sb[:, lo // LIST_ROWS : hi // LIST_ROWS]
 
-        def gather_words(e, o):
-            nc.vector.tensor_copy(gw[o][e % 2][:], xw[o][:].bitcast(U32).indirect(slot_offsets(e * C, (e + 1) * C)))
+        def gathered_words(e, o):
+            if o == 1:
+                return gw[2 * (1 - e % 2)]
+            return gw[0] if e == 0 else gw[1 + 2 * (1 - e % 2)]
 
-        def gather_first_scales(o):
-            nc.vector.tensor_copy(gs_first[o][:], xs_planes[:, o * T : (o + 1) * T].indirect(slot_offsets(0, C)))
+        def gather_words(e, o, step=C):
+            for lo in range(0, C, step):
+                nc.vector.tensor_copy(
+                    gathered_words(e, o)[:, lo : lo + step],
+                    xw[o][:].bitcast(U32).indirect(slot_offsets(e * C + lo, e * C + lo + step)),
+                )
+
+        def single_plane(e, o):
+            return gs_packed[0][:, 0:C] if (e, o) == (5, 0) else gs_first[o][:]
+
+        def gather_single(e, o):
+            window = xs_planes[:, o * T : (o + 1) * T]
+            nc.vector.tensor_copy(single_plane(e, o), window.indirect(slot_offsets(e * C, (e + 1) * C)))
 
         def gather_packed(g):
             lo, hi = PACKED_SETS[g]
-            nc.vector.tensor_copy(gs_packed[g][:], xs_planes[:].indirect(slot_offsets(lo * C, hi * C)))
+            nc.vector.tensor_copy(gs_packed[g][:], xs_planes[:, 0:T].indirect(slot_offsets(lo * C, hi * C)))
 
         def move_second_planes(g):
             for r in range(4):
@@ -120,11 +133,11 @@ def tile_moe_shr_glu_sigmoid_kernel(
                 lo = (j - ROUTED_TILES) * P
                 return xw[o][:, lo : lo + P], xs_planes[:, o * T + lo : o * T + lo + P]
             e, c = j // 2, j % 2 * P
-            if e == 0:
-                return gw[o][0][:, c : c + P], gs_first[o][:, c : c + P]
+            if e in (0, 5):
+                return gathered_words(e, o)[:, c : c + P], single_plane(e, o)[:, c : c + P]
             g, place = member(PACKED_SETS, e)
             plane = (gs_packed, gs_moved)[o][g]
-            return gw[o][e % 2][:, c : c + P], plane[:, place * C + c : place * C + c + P]
+            return gathered_words(e, o)[:, c : c + P], plane[:, place * C + c : place * C + c + P]
 
         def one_pass(target, slots, planes, j, o, first, last):
             e = min(j // 2, SHARED)
@@ -153,8 +166,10 @@ def tile_moe_shr_glu_sigmoid_kernel(
             return long[j % 4]
 
         def product(j):
-            if j % 2 and j // 2 + 2 < E:
-                for o in range(PASSES):
+            if j == 0:
+                gather_words(1, 1)
+            if j in (1, 3, 5):
+                for o in range(j == 1, PASSES):
                     gather_words(j // 2 + 2, o)
             if j in POOL_TILES:
                 b_copy = b_sb[POOL_TILES.index(j) % len(b_sb)]
@@ -174,6 +189,29 @@ def tile_moe_shr_glu_sigmoid_kernel(
             for o in range(PASSES):
                 one_pass(b_bank(j), w3w, w3s, j, o, o == 0, o == 1)
             product(j)
+
+        def last_b_in_halves(j, targets):
+            g, place = member(SCALE_GROUPS, SHARED)
+            for half, target in enumerate(targets):
+                cols = slice(half * C, (half + 1) * C)
+                for o in range(PASSES):
+                    codes, code_scales = token_operands(j, o)
+                    nc.tensor.matmul_mx(
+                        out=target[:, 0:C],
+                        lhsT=codes.bitcast(FP8X4),
+                        lhsT_scale=code_scales,
+                        rhs=w3w[SHARED][:, o, half * H : (half + 1) * H].bitcast(FP4X4),
+                        rhs_scale=w3s[g][:, place * PASSES + o, cols],
+                        start=(o == 0),
+                        stop=(o == 1),
+                    )
+                words = slice(half * P // 2, (half + 1) * P // 2)
+                nc.vector.tensor_tensor(
+                    paired(h[j % len(h)][:])[:, :, words, :],
+                    permuted(target[:, 0:C]),
+                    paired(sig[j % len(sig)])[:, :, words, :],
+                    MULT,
+                )
 
         def first_layer(j, a_bank):
             for o in range(PASSES):
@@ -198,8 +236,9 @@ def tile_moe_shr_glu_sigmoid_kernel(
             for j, a_bank in zip(tiles, a_banks):
                 sigmoid(j, a_bank)
             for j in tiles:
-                for o in passes:
-                    one_pass(b_bank(j), w3w, w3s, j, o, o == passes[0], o == passes[1])
+                one_pass(b_bank(j), w3w, w3s, j, passes[0], True, False)
+            for j in tiles:
+                one_pass(b_bank(j), w3w, w3s, j, passes[1], False, True)
                 product(j)
 
         def turn(j, tiles, target, turned, copy=nc.scalar.copy):
@@ -260,9 +299,8 @@ def tile_moe_shr_glu_sigmoid_kernel(
                 nc.sync.dma_start(out[:, cols.stop - C : cols.stop], result[:, cols.stop - C : cols.stop])
 
         zero(nc.gpsimd, xs_planes)
-        for plane in (w1s[0], w3s[0], w1s[1], w3s[1], gs_moved[0], gs_moved[1], w2s):
+        for plane in (w1s[0], w3s[0], w1s[1], w3s[1], ident, gs_moved[0], gs_moved[1], w2s):
             zero(nc.vector, plane)
-        nc.vector.memset(ident[:], 0.0)
         make_identity(nc, ident[:], nomemset=True)
 
         def load_tokens(o):
@@ -276,23 +314,23 @@ def tile_moe_shr_glu_sigmoid_kernel(
         load_tokens(1)
         load_words(w3w, w3_words, 0)
         for o in range(PASSES):
-            gather_first_scales(o)
-            gather_words(0, o)
+            gather_single(0, o)
+            gather_words(0, o, P)
         load(xs_planes[16:32, 0:T], x_scales[1])
         load_scales(w3s, w3_scales, 0)
         load_words(w1w, w1_words, 1)
+        load_scales(w1s, w1_scales, 1)
         load_words(w3w, w3_words, 1)
-        for o in range(PASSES):
-            gather_words(1, o)
+        for e in (1, 2):
+            gather_words(e, 0)
         gather_packed(0)
         gather_packed(1)
-        load_scales(w1s, w1_scales, 1)
         move_second_planes(0)
         load_words(w1w, w1_words, 2)
         load_scales(w3s, w3_scales, 1)
         load_words(w3w, w3_words, 2)
-        move_second_planes(1)
         load_words(w1w, w1_words, 3)
+        move_second_planes(1)
         load_words(w3w, w3_words, 3)
 
         for e in range(E):
@@ -307,18 +345,25 @@ def tile_moe_shr_glu_sigmoid_kernel(
                         a_pass(2 * e + part, a_banks[part], o)
                 for part in range(2):
                     b_passes(2 * e + part)
+            if e < 2:
+                gather_single(5, 1 - e)
             if e == 1:
                 load_scales(w1s, w1_scales, 2)
                 load_scales(w3s, w3_scales, 2)
-                for e in (4, 5, 6):
-                    load_words(w1w, w1_words, e)
-                    load_words(w3w, w3_words, e)
-                    if e == 5:
-                        load(w2w[:], w2_words.rearrange("e s p b -> p (e s) b"))
-                        load_rows(w2s[:], w2_scales.rearrange("e s f n -> f (e s) n"))
+                load_words(w1w, w1_words, 4)
+                load_words(w3w, w3_words, 4)
+                load_words(w1w, w1_words, 5)
+                load_words(w3w, w3_words, 5)
+                load(w2w[:], w2_words.rearrange("e s p b -> p (e s) b"))
+                load_rows(w2s[:], w2_scales.rearrange("e s f n -> f (e s) n"))
+                load_words(w1w, w1_words, SHARED)
+                load_words(w3w, w3_words, SHARED)
                 for r, pos in enumerate((pos1, pos2)):
                     nc.sync.dma_start(pos_sb[r][:], pos)
                 nc.sync.dma_start(gate_sb[:], gate.rearrange("g n t -> n g t"))
+            if e == 3:
+                for o in range(PASSES):
+                    gather_words(5, o)
             if e in (3, 4):
                 pair = e - 3
                 for part in range(2):
@@ -350,8 +395,11 @@ def tile_moe_shr_glu_sigmoid_kernel(
         nc.gpsimd.tensor_tensor(weighted[1][:, 1, :], fetched[:, 2, :], gate_sb[:, 1, block_cols(1)], MULT)
         add_choices(1)
         first_layer(15, short[2])
-        first_layer(16, short[3])
-        first_layer(17, short[1])
+        for j, a_bank in ((16, short[3]), (17, short[1])):
+            for o in range(PASSES):
+                a_pass(j, a_bank, o)
+        b_passes(16)
+        last_b_in_halves(17, (long[1], long[2]))
         turn(12, 2, short[0], h_turned[1][:, 0:2])
         turn(14, 2, short[2], h_turned[1][:, 2:4], nc.vector.tensor_copy)
         turn(16, 1, short[3], h_turned[0][:, 0:1])
@@ -360,7 +408,7 @@ def tile_moe_shr_glu_sigmoid_kernel(
         quantise(14, 2, h_turned[1][:, 2:4])
         quantise(16, 1, h_turned[0][:, 0:1])
         quantise(17, 1, h_turned[2][:, 0:1])
-        finish(12, 2, long[2][:, 0:C])
-        finish(14, 2, long[3][:, 0:C])
+        finish(12, 2, long[3][:, 0:C])
+        finish(14, 2, long[2][:, 0:C])
         finish(16, 1, long[0][:, 0:P])
         finish(17, 1, long[1][:, 0:P])

from contextlib import ExitStack

import concourse.mybir as mybir
from concourse.masks import make_identity

K, T, E, C, H, N = 1024, 768, 6, 256, 512, 128
S = E * C
FLOPS = 2 * (S + T) * (2 * K * H + H * N)

F32 = mybir.dt.float32
BF16 = mybir.dt.bfloat16
I32 = mybir.dt.int32
U32 = mybir.dt.uint32
U16 = mybir.dt.uint16
U8 = mybir.dt.uint8
FP8X4 = mybir.dt.float8_e4m3fn_x4
FP4X4 = mybir.dt.float4_e2m1fn_x4
MULT = mybir.AluOpType.mult
ADD = mybir.AluOpType.add
SIGMOID = mybir.ActivationFunctionType.Sigmoid
COPY = mybir.ActivationFunctionType.Copy

P = 128
PASSES = K // 512
QUADRANTS = 4
LIST_ROWS = 16
SHARED = E
SCALE_GROUPS = ((0, 2), (2, 4), (4, 7))
PACKED_SETS = ((1, 3), (3, 5))
ROUTED_TILES = S // P
BLOCKS = T // C
POOL_TILES = (0, 2, 4, 6)


def tile_moe_shr_glu_sigmoid_kernel(
    tc, x_words, x_scales, w1_words, w1_scales, w3_words, w3_scales, w2_words, w2_scales, gate, offs, pos1, pos2, out
):
    nc = tc.nc
    with ExitStack() as ctx:
        keep = ctx.enter_context(tc.tile_pool(name="keep", bufs=1))
        psum = ctx.enter_context(tc.psum_pool(name="psum", bufs=1))

        def held(shape, dtype, name):
            return keep.tile(shape, dtype, name=name, align_bytes=256)

        def ring(count, shape, dtype, name):
            return [held(shape, dtype, f"{name}{r}") for r in range(count)]

        def zero(engine, tile):
            engine.memset(tile[:].bitcast(I32), 0)

        offs_sb = held([P, S // LIST_ROWS], U16, "offs_sb")
        pos_sb = [held([P, T // LIST_ROWS], U16, f"pos{r}_sb") for r in (1, 2)]
        xw = ring(PASSES, [P, T], I32, "xw")
        xs_planes = held([P, PASSES * T], U8, "xs_planes")
        w1s = 2 * [held([P, rows * PASSES, H], U8, f"w1s{rows}") for rows in (3, 2)]
        w3s = 2 * [held([P, rows * PASSES, H], U8, f"w3s{rows}") for rows in (3, 2)]
        w1w = ring(E + 1, [P, PASSES, 2 * H], U8, "w1w")
        w3w = ring(E + 1, [P, PASSES, 2 * H], U8, "w3w")
        w2s = held([P, E + 1, N], U8, "w2s")
        w2w = held([P, E + 1, 2 * N], U8, "w2w")
        ident = held([P, P], F32, "ident")
        gw = ring(4, [P, C], U32, "gw")
        gs_first = ring(PASSES, [P, C], U8, "gs_first")
        gs_packed = [held([P, (hi - lo) * C], U8, f"gs_packed{lo}") for lo, hi in PACKED_SETS]
        gs_moved = [held([P, (hi - lo) * C], U8, f"gs_moved{lo}") for lo, hi in PACKED_SETS]
        y_all = held([P, S], F32, "y_all")
        gate_sb = held([P, 2, T], F32, "gate_sb")
        sig_all = held([P, 8, H], F32, "sig_all")
        sig = [sig_all[:, r, :] for r in range(8)]
        b_sb = ring(2, [P, H], F32, "b_sb")
        h = ring(8, [P, H], BF16, "h")
        h_turned = ring(3, [P, 4, P, 4], BF16, "hT")
        h_codes = held([P, S + T], U32, "h_codes")
        h_scales = held([P, S + T], U8, "h_scales")
        fetched = held([P, 4, C], F32, "fetched")
        weighted = ring(BLOCKS, [P, 2, C], F32, "weighted")
        partial = held([P, T], F32, "partial")
        result = held([P, T], F32, "result")
        short = [psum.tile([P, H], F32, name=f"short{r}") for r in range(4)]
        long = [psum.tile([P, H], F32, name=f"long{r}") for r in range(4)]

        def load(tile, source):
            nc.sync.dma_start(tile.bitcast(I32), source.bitcast(I32))

        def load_rows(plane, rows):
            for r in range(4):
                load(plane[r:P:32], rows[r:16:4])

        def load_scales(planes, scales, g):
            lo, hi = SCALE_GROUPS[g]
            load_rows(planes[g][:, 0 : (hi - lo) * PASSES, :], scales[lo:hi].rearrange("e s f n -> f (e s) n"))

        def load_words(slots, words, e):
            load(slots[e][:], words[e].rearrange("s p b -> p s b"))

        def slot_offsets(lo, hi):
            return offs_sb[:, lo // LIST_ROWS : hi // LIST_ROWS]

        def gathered_words(e, o):
            if o == 1:
                return gw[2 * (1 - e % 2)]
            return gw[0] if e == 0 else gw[1 + 2 * (1 - e % 2)]

        def gather_words(e, o, step=C):
            for lo in range(0, C, step):
                nc.vector.tensor_copy(
                    gathered_words(e, o)[:, lo : lo + step],
                    xw[o][:].bitcast(U32).indirect(slot_offsets(e * C + lo, e * C + lo + step)),
                )

        def single_plane(e, o):
            return gs_packed[0][:, 0:C] if (e, o) == (5, 0) else gs_first[o][:]

        def gather_single(e, o):
            window = xs_planes[:, o * T : (o + 1) * T]
            nc.vector.tensor_copy(single_plane(e, o), window.indirect(slot_offsets(e * C, (e + 1) * C)))

        def gather_packed(g):
            lo, hi = PACKED_SETS[g]
            nc.vector.tensor_copy(gs_packed[g][:], xs_planes[:, 0:T].indirect(slot_offsets(lo * C, hi * C)))

        def move_second_planes(g):
            for r in range(4):
                load(gs_moved[g][r:P:32], gs_packed[g][16 + r : 32 : 4])

        def member(groups, e):
            g = [first <= e < end for first, end in groups].index(True)
            return g, e - groups[g][0]

        def token_operands(j, o):
            if j >= ROUTED_TILES:
                lo = (j - ROUTED_TILES) * P
                return xw[o][:, lo : lo + P], xs_planes[:, o * T + lo : o * T + lo + P]
            e, c = j // 2, j % 2 * P
            if e in (0, 5):
                return gathered_words(e, o)[:, c : c + P], single_plane(e, o)[:, c : c + P]
            g, place = member(PACKED_SETS, e)
            plane = (gs_packed, gs_moved)[o][g]
            return gathered_words(e, o)[:, c : c + P], plane[:, place * C + c : place * C + c + P]

        def one_pass(target, slots, planes, j, o, first, last):
            e = min(j // 2, SHARED)
            g, place = member(SCALE_GROUPS, e)
            codes, code_scales = token_operands(j, o)
            nc.tensor.matmul_mx(
                out=target[:],
                lhsT=codes.bitcast(FP8X4),
                lhsT_scale=code_scales,
                rhs=slots[e][:, o, :].bitcast(FP4X4),
                rhs_scale=planes[g][:, place * PASSES + o, :],
                start=first,
                stop=last,
            )

        def paired(ap):
            return ap.rearrange("t (u p f) -> t u p f", u=2, f=2)

        def permuted(ap):
            return ap.rearrange("t (p u f) -> t u p f", u=2, f=2)

        def sigmoid(j, source):
            nc.scalar.activation(paired(sig[j % len(sig)]), permuted(source[:]), SIGMOID)

        def b_bank(j):
            return long[j % 4]

        def product(j):
            if j == 0:
                gather_words(1, 1)
            if j in (1, 3, 5):
                for o in range(j == 1, PASSES):
                    gather_words(j // 2 + 2, o)
            if j in POOL_TILES:
                b_copy = b_sb[POOL_TILES.index(j) % len(b_sb)]
                nc.scalar.copy(paired(b_copy[:]), permuted(b_bank(j)[:]))
                nc.gpsimd.tensor_tensor(h[j % len(h)][:], b_copy[:], sig[j % len(sig)], MULT)
                return
            nc.vector.tensor_tensor(
                paired(h[j % len(h)][:]), permuted(b_bank(j)[:]), paired(sig[j % len(sig)]), MULT
            )

        def a_pass(j, a_bank, o):
            one_pass(a_bank, w1w, w1s, j, o, o == 0, o == 1)
            if o == 1:
                sigmoid(j, a_bank)

        def b_passes(j):
            for o in range(PASSES):
                one_pass(b_bank(j), w3w, w3s, j, o, o == 0, o == 1)
            product(j)

        def last_b_in_halves(j, targets):
            g, place = member(SCALE_GROUPS, SHARED)
            for half, target in enumerate(targets):
                cols = slice(half * C, (half + 1) * C)
                for o in range(PASSES):
                    codes, code_scales = token_operands(j, o)
                    nc.tensor.matmul_mx(
                        out=target[:, 0:C],
                        lhsT=codes.bitcast(FP8X4),
                        lhsT_scale=code_scales,
                        rhs=w3w[SHARED][:, o, half * H : (half + 1) * H].bitcast(FP4X4),
                        rhs_scale=w3s[g][:, place * PASSES + o, cols],
                        start=(o == 0),
                        stop=(o == 1),
                    )
                words = slice(half * P // 2, (half + 1) * P // 2)
                nc.vector.tensor_tensor(
                    paired(h[j % len(h)][:])[:, :, words, :],
                    permuted(target[:, 0:C]),
                    paired(sig[j % len(sig)])[:, :, words, :],
                    MULT,
                )

        def first_layer(j, a_bank):
            for o in range(PASSES):
                a_pass(j, a_bank, o)
            b_passes(j)

        def first_layer_first_passes(tiles, a_banks):
            for slots, planes, targets in ((w1w, w1s, a_banks), (w3w, w3s, [b_bank(j) for j in tiles])):
                for j, target in zip(tiles, targets):
                    one_pass(target, slots, planes, j, 0, True, False)
            for j, a_bank in zip(tiles, a_banks):
                one_pass(a_bank, w1w, w1s, j, 1, False, True)
                sigmoid(j, a_bank)
            for j in tiles:
                one_pass(b_bank(j), w3w, w3s, j, 1, False, True)
                product(j)

        def first_layer_by_pass(tiles, a_banks, passes):
            for o in passes:
                for j, a_bank in zip(tiles, a_banks):
                    one_pass(a_bank, w1w, w1s, j, o, o == passes[0], o == passes[1])
            for j, a_bank in zip(tiles, a_banks):
                sigmoid(j, a_bank)
            for j in tiles:
                one_pass(b_bank(j), w3w, w3s, j, passes[0], True, False)
            for j in tiles:
                one_pass(b_bank(j), w3w, w3s, j, passes[1], False, True)
                product(j)

        def turn(j, tiles, target, turned, copy=nc.scalar.copy):
            for part in range(tiles):
                pairs = h[(j + part) % len(h)][:].bitcast(F32)
                for u in range(2):
                    nc.tensor.transpose(
                        target[:, (2 * part + u) * P : (2 * part + u + 1) * P], pairs[:, u * P : (u + 1) * P], ident[:]
                    )
            copy(turned.bitcast(F32), target[:, 0 : 2 * tiles * P].rearrange("p (j u t) -> p j t u", u=2, t=P))

        def quantise(j, tiles, turned):
            cols = slice(j * P, (j + tiles) * P)
            nc.vector.quantize_mx(
                out=h_codes[:, cols].bitcast(FP8X4),
                scales=h_scales[:, cols],
                in_=turned.rearrange("p j t r -> p (j t r)"),
            )

        def second_layer(j, tiles, target):
            e = min(j // 2, SHARED)
            cols = slice(j * P, (j + tiles) * P)
            nc.tensor.matmul_mx(
                out=target,
                lhsT=w2w[:, e, :].bitcast(FP4X4),
                lhsT_scale=w2s[:, e, :],
                rhs=h_codes[:, cols].bitcast(FP8X4),
                rhs_scale=h_scales[:, cols],
                start=True,
                stop=True,
            )

        def routed_results(e, experts, target, copy):
            for part in range(experts):
                second_layer(2 * (e + part), 2, target[:, part * C : (part + 1) * C])
            copy(y_all[:, e * C : (e + experts) * C], target[:, 0 : experts * C])

        def block_cols(block):
            return slice(block * C, (block + 1) * C)

        def choice(r, block):
            return y_all[:].indirect(pos_sb[r][:, block * C // LIST_ROWS : (block + 1) * C // LIST_ROWS])

        def fetch(r, block, target):
            nc.scalar.activation(target, choice(r, block), COPY)

        def weigh(r, block, target):
            nc.vector.tensor_tensor(target, choice(r, block), gate_sb[:, r, block_cols(block)], MULT)

        def add_choices(block):
            nc.gpsimd.tensor_tensor(partial[:, block_cols(block)], weighted[block][:, 0, :], weighted[block][:, 1, :], ADD)

        def finish(j, tiles, source):
            cols = slice((j - ROUTED_TILES) * P, (j - ROUTED_TILES + tiles) * P)
            second_layer(j, tiles, source)
            nc.vector.tensor_tensor(result[:, cols], source, partial[:, cols], ADD)
            if cols.stop % C == 0:
                nc.sync.dma_start(out[:, cols.stop - C : cols.stop], result[:, cols.stop - C : cols.stop])

        zero(nc.gpsimd, xs_planes)
        for plane in (w1s[0], w3s[0], w1s[1], w3s[1], ident, gs_moved[0], gs_moved[1], w2s):
            zero(nc.vector, plane)
        make_identity(nc, ident[:], nomemset=True)

        def load_tokens(o):
            load(xw[o][:], x_words[o].rearrange("p t r -> p (t r)"))

        nc.sync.dma_start(offs_sb[:], offs)
        load_words(w1w, w1_words, 0)
        load_rows(xs_planes[:].rearrange("p (s t) -> p s t", s=PASSES), x_scales.rearrange("s f t -> f s t"))
        load_tokens(0)
        load_scales(w1s, w1_scales, 0)
        load_tokens(1)
        load_words(w3w, w3_words, 0)
        for o in range(PASSES):
            gather_single(0, o)
            gather_words(0, o, P)
        load(xs_planes[16:32, 0:T], x_scales[1])
        load_scales(w3s, w3_scales, 0)
        load_words(w1w, w1_words, 1)
        load_scales(w1s, w1_scales, 1)
        load_words(w3w, w3_words, 1)
        for e in (1, 2):
            gather_words(e, 0)
        gather_packed(0)
        gather_packed(1)
        move_second_planes(0)
        load_words(w1w, w1_words, 2)
        load_scales(w3s, w3_scales, 1)
        load_words(w3w, w3_words, 2)
        load_words(w1w, w1_words, 3)
        move_second_planes(1)
        load_words(w3w, w3_words, 3)

        for e in range(E):
            a_banks = short[2 * (e % 2) : 2 * (e % 2) + 2]
            if e == 0:
                first_layer_by_pass((0, 1), a_banks, (0, 1))
            elif e == 1:
                first_layer_first_passes((2, 3), a_banks)
            else:
                for part in range(2):
                    for o in range(PASSES):
                        a_pass(2 * e + part, a_banks[part], o)
                for part in range(2):
                    b_passes(2 * e + part)
            if e < 2:
                gather_single(5, 1 - e)
            if e == 1:
                load_scales(w1s, w1_scales, 2)
                load_scales(w3s, w3_scales, 2)
                load_words(w1w, w1_words, 4)
                load_words(w3w, w3_words, 4)
                load_words(w1w, w1_words, 5)
                load_words(w3w, w3_words, 5)
                load(w2w[:], w2_words.rearrange("e s p b -> p (e s) b"))
                load_rows(w2s[:], w2_scales.rearrange("e s f n -> f (e s) n"))
                load_words(w1w, w1_words, SHARED)
                load_words(w3w, w3_words, SHARED)
                for r, pos in enumerate((pos1, pos2)):
                    nc.sync.dma_start(pos_sb[r][:], pos)
                nc.sync.dma_start(gate_sb[:], gate.rearrange("g n t -> n g t"))
            if e == 3:
                for o in range(PASSES):
                    gather_words(5, o)
            if e in (3, 4):
                pair = e - 3
                for part in range(2):
                    turn(4 * pair + 2 * part, 2, a_banks[part], h_turned[pair][:, 2 * part : 2 * part + 2])
                quantise(4 * pair, 4, h_turned[pair][:])
        routed_results(0, 2, short[0], nc.scalar.copy)
        routed_results(2, 2, short[1], nc.vector.tensor_copy)
        turn(8, 2, short[2], h_turned[2][:, 0:2])
        turn(10, 1, short[3], h_turned[0][:, 0:1])
        turn(11, 1, long[1], h_turned[0][:, 1:2], nc.vector.tensor_copy)
        quantise(8, 2, h_turned[2][:, 0:2])
        quantise(10, 2, h_turned[0][:, 0:2])
        first_layer(12, short[0])
        a_pass(13, short[1], 0)
        routed_results(4, 1, short[2], nc.scalar.copy)
        routed_results(5, 1, short[3], nc.scalar.copy)
        a_pass(13, short[1], 1)
        fetch(0, 0, fetched[:, 0, :])
        fetch(1, 0, fetched[:, 1, :])
        weigh(0, 1, weighted[1][:, 0, :])
        for r in range(2):
            weigh(r, 2, weighted[2][:, r, :])
        b_passes(13)
        first_layer(14, short[0])
        fetch(1, 1, fetched[:, 2, :])
        add_choices(2)
        nc.gpsimd.tensor_tensor(weighted[0][:], fetched[:, 0:2, :], gate_sb[:, :, block_cols(0)], MULT)
        add_choices(0)
        nc.gpsimd.tensor_tensor(weighted[1][:, 1, :], fetched[:, 2, :], gate_sb[:, 1, block_cols(1)], MULT)
        add_choices(1)
        first_layer(15, short[2])
        for j, a_bank in ((16, short[3]), (17, short[1])):
            for o in range(PASSES):
                a_pass(j, a_bank, o)
        b_passes(16)
        last_b_in_halves(17, (long[1], long[2]))
        turn(12, 2, short[0], h_turned[1][:, 0:2])
        turn(14, 2, short[2], h_turned[1][:, 2:4], nc.vector.tensor_copy)
        turn(16, 1, short[3], h_turned[0][:, 0:1])
        turn(17, 1, short[1], h_turned[2][:, 0:1])
        quantise(12, 2, h_turned[1][:, 0:2])
        quantise(14, 2, h_turned[1][:, 2:4])
        quantise(16, 1, h_turned[0][:, 0:1])
        quantise(17, 1, h_turned[2][:, 0:1])
        finish(12, 2, long[3][:, 0:C])
        finish(14, 2, long[2][:, 0:C])
        finish(16, 1, long[0][:, 0:P])
        finish(17, 1, long[1][:, 0:P])
